import numpy as np, ml_dtypes
CORES = [113,118,241,246]
N = 4
BF = ml_dtypes.bfloat16
def gentries(a):
    return np.ascontiguousarray(a.reshape(8, 16, -1).transpose(0, 2, 1)).reshape(8, -1)
def gtable(e):
    e = np.asarray(e); return np.ascontiguousarray(e.reshape(8, -1, 16).transpose(0, 2, 1)).reshape(128, -1).astype(np.int32)
W, LW, RO, E, LN = 2048, 11, 4, 1, 2
T = 3 * W // 4
def curves(rng):
    p = rng.choice(np.array([0.7, 1.0, 1.4], np.float32), (N, 8, 16, 1))
    return np.minimum((16 * rng.random((N, 8, 16, W), dtype=np.float32) ** p).astype(np.int64), 15)
def load(rng):
    return ((0.5 + 1.5 * rng.random((N, 128, W), dtype=np.float32)) * np.exp2(2 * rng.random((N, 1, W)) - 1).astype(np.float32)).astype(np.float32)
def roots(rng):
    return (0.875 + 0.25 * rng.random((N, 128, 5))).astype(np.float32)
def warp(rng, *lead):
    u = np.sort(rng.random(lead + (W,)), axis=-1); k = rng.integers(1, 4, lead + (1,)); a = rng.uniform(-0.9, 0.9, lead + (1,))
    w = np.clip(np.floor(W * (u + a * np.array([0.15915, 0.07957, 0.05305])[k - 1] * np.sin(6.283185307179586 * k * u))).astype(np.int64), 0, W - 1)
    back = rng.integers(1, 40, lead + (W // 16,)) * (rng.random(lead + (W // 16,)) < 0.15)
    turn = 7 * (rng.random(lead + (W // 8,)) < 0.1)
    i = np.maximum(np.arange(W) - np.repeat(back, 16, axis=-1), 0) ^ np.repeat(turn, 8, axis=-1)
    return np.take_along_axis(w, i, -1)
def cliffs(rng, *lead):
    j = np.arange(W); w = np.sort(rng.integers(0, W - 1, lead + (W,)), axis=-1)[..., np.minimum(4 * j // 3, W - 1)]; r = rng.random(lead + (W,))
    e = np.where(j < T, np.where(r < 0.45, w, 0), np.where(r < 0.6, W - 1, 0))
    e[..., 0] = 0; e[..., W - 1] = W - 1
    return e
def pack(x, v, rt, e, ga):
    return {"xs": np.ascontiguousarray(x.reshape(N, 128, W)).astype(np.float32).astype(BF), "pay": v.astype(BF), "rho": rt.astype(np.float32),
            "ew": np.stack([gtable(a.reshape(8, -1)) for a in e]), "gam": np.stack([gtable(a) for a in ga])}
def setup_inputs(rng):
    return pack(curves(rng), load(rng), roots(rng), warp(rng, N, 8, RO, E), warp(rng, N, 8))
def setup_inputs_spread(rng):
    p = np.exp2(rng.uniform(-2, 2, (N, 8, 1, W))).astype(np.float32)
    x = np.minimum((16 * rng.random((N, 8, 16, W), dtype=np.float32) ** p).astype(np.int64), 15)
    e = warp(rng, N, 8, RO, E); e[:, 1::2] = rng.integers(0, W, (N, 4, RO, E, W))
    return pack(x, load(rng), roots(rng), e, warp(rng, N, 8))
def setup_inputs_ends(rng):
    x = 15 * (rng.random((N, 8, 16, W)) < rng.choice(np.array([0.15, 0.5, 0.85]), (N, 8, 1, 1))).astype(np.int64)
    x[0, 0] = 15; x[0, 4] = 15; x[0, 7] = 15; x[N - 1, 7] = 0; x[2, 3] = 0
    x[1, 7] = 0; x[1, 7, 15, W - 1] = 15
    e = cliffs(rng, N, 8, RO, E); ga = cliffs(rng, N, 8)
    e[:, 2::3] = (W - 1) * rng.integers(0, 2, e[:, 2::3].shape)
    e[1, 7, 0, 1:, T:W - 1] = 0; e[1, 7, 0, 0, T:] = ga[2, 0, T:]
    h = T + int(np.argmax(e[1, 7, 0, 0, T:] == W - 1)); e[1, 7, 0, 0, h] = 0
    for q, g in ((N - 1, 6), (1, 3)):
        a = (q + 1) % N
        x[q, g] = 0; x[q, g, 15, W - 1] = 1
        ga[a, g + 1, W - 32:W - 1] = 0
        e[q, g, 0, 1:, T:W - 1] = 0; e[q, g, 0, 0, T:] = ga[a, g + 1, T:]; e[q, g, 0, 0, W - 1] = 0
    v = np.where(rng.random((N, 128, W)) < 0.7, 4.0, 0.25)
    rt = 0.875 + 0.25 * rng.integers(0, 2, (N, 128, 5))
    return pack(x, v.astype(np.float32), rt, e, ga)
def setup_inputs_corners(rng):
    j = np.arange(W)
    kinds = np.stack([j, W - 1 - j, 0 * j, 0 * j + W - 1, np.minimum(3 * j, W - 1), np.minimum(4 * j, W - 1), j >> 1, (5 * j) & (W - 1)])
    o = rng.permutation(8); k = o[(np.arange(N)[:, None] + np.arange(8)) % 8]
    ga = kinds[k]; e = kinds[rng.integers(0, 8, (N, 8, RO, E))]
    e = np.where(rng.random((N, 8, RO, E, 1)) < 0.3, rng.integers(0, W, e.shape), e)
    x = curves(rng); off = int(rng.integers(0, 8))
    for q in range(N):
        for g in range(8):
            m = (3 * q + g + off) % 8
            if m == 0: x[q, g] = 0
            elif m == 1: x[q, g] = 15
            elif m == 2: x[q, g] = rng.integers(0, 16, (16, 1))
            elif m == 3: x[q, g] = (16 * j) >> LW
            elif m == 4: x[q, g] = 0; x[q, g, :, W - 1] = 15
    return pack(x, load(rng), roots(rng), e, ga)
def setup_inputs_ties(rng):
    x = curves(rng); e = warp(rng, N, 8, RO, E); ga = warp(rng, N, 8); j = np.arange(W); a = int(rng.integers(0, N)); b = (a + 1) % N
    x[:, ::2] = np.where((j & 2) > 0, 15, np.minimum(x[:, ::2], 14))
    x[a, 1::2] = 15; x[b, 1::4] = rng.integers(0, 16, (2, 16, 1))
    base = (j & ~3) | 2
    e[:, ::2, 0, 0] = base + rng.integers(0, 2, (N, 4, W)); ga[:, 1::2] = base + rng.integers(0, 2, (N, 4, W))
    e[1::2, ::2, 0, 0, W - 1] = W - 4
    x[1::2, ::2, :, W - 4] = 15; x[1::2, ::2, int(rng.integers(0, 16)), W - 4] = 14
    x[0, 6] = np.where((j & 2) == 0, 15, np.minimum(x[0, 6], 14)); ga[1, 7] = (j & ~3) + 1; e[0, 6, 0] = warp(rng, E)
    return pack(x, load(rng), roots(rng), e, ga)
def check_ranges(d):
    bad = []
    for k, lo, hi in (("xs", 0, 15), ("pay", 0.25, 4), ("rho", 0.875, 1.125), ("ew", 0, W - 1), ("gam", 0, W - 1)):
        v = np.asarray(d[k]).astype(np.float64)
        if not (np.min(v) >= lo and np.max(v) <= hi): bad.append("range of " + k)
    v = np.asarray(d["xs"]).astype(np.float64)
    if not np.all(v == np.floor(v)): bad.append("xs is not whole")
    return bad
def pick(a, c):
    return np.take_along_axis(a, c[:, :, None, :], 3)
def inverse(w):
    w = w.reshape(-1, W); top = np.maximum.accumulate(w, axis=1)
    before = np.concatenate([np.full((len(w), 1), -1, np.int64), top[:, :-1]], axis=1)
    i, j = np.nonzero(w > before); t = np.zeros(w.shape, np.int64); t[i, w[i, j]] = j
    return np.maximum.accumulate(t, axis=1).reshape(N, 8, W)
def root(rt, c):
    s = np.concatenate([np.minimum(np.abs(c[..., 1:] - c[..., :-1]), 4), np.ones((N, 8, 1), np.int64)], axis=-1)
    return pick(rt, s)
def reference(xs, pay, rho, ew, gam):
    x = xs.astype(np.int64).reshape(N, 8, 16, W); p0 = pay.astype(np.float64).reshape(N, 8, 16, W); rt = rho.astype(np.float64).reshape(N, 8, 16, 5)
    e = np.stack([gentries(a) for a in ew]).astype(np.int64).reshape(N, 8, RO, E, W); ga = np.stack([gentries(a) for a in gam]).astype(np.int64)
    v = p0; m = np.maximum.reduce(x, axis=0)
    stay = np.broadcast_to(np.arange(W), (N, 8, W))
    for t in range(RO):
        gn = np.roll(np.roll(ga, -1, axis=0), -1, axis=1)
        tr = np.stack([stay] + [e[:, :, t, i] for i in range(E)] + [gn, inverse(gn)])
        mn = np.roll(m, -1, axis=0)[None]
        sc = np.stack([np.sum(np.abs(pick(x, c) - mn), axis=(2, 3)) for c in tr])
        b = np.argmin(sc, axis=0)
        c = np.take_along_axis(tr, b[None, :, :, None], 0)[0]
        x = pick(x, c); v = pick(v, c) * root(rt, c); ga = np.take_along_axis(ga, c, 2)
        mu = np.add.reduce(inverse(ga), axis=0) >> LN
        mu = np.broadcast_to(mu, (N, 8, W))
        x = pick(x, mu); v = pick(v, mu) * root(rt, mu); ga = np.take_along_axis(ga, mu, 2)
        m = np.maximum.reduce(x, axis=0)
        v = v + m * 0.03125
    u = v + x * 0.0625 + pick(p0, ga)
    y = (np.add.reduce(u, axis=0) * 0.25).reshape(128, W)
    n = W // N
    return {"y": np.stack([y[:, r * n:(r + 1) * n] for r in range(N)]).astype(np.float32)}

def check_inputs(d):
    bad = list(check_ranges(d))
    if not bad:
        for name, y in reference(**d).items():
            for q in range(N):
                v = np.abs(np.asarray(y[q], np.float64)); s = np.sqrt(np.mean(v * v))
                if v.max() > 3 * s or s < 2.0 ** 0: bad.append('%s of rank %d is uneven or too small' % (name, q))
    return bad

@@ -1,0 +1,656 @@
+from concourse.bass import DstId, RemoteDMATransfer
+from concourse.mybir import dt, AluOpType, AxisListType, ActivationFunctionType
+
+W = 2048
+RO = 4
+KA0, KA1, KA2 = 62, 46, 64
+TW = 4112
+F, B, H, I32, U = "float32", "bfloat16", "float16", "int32", "uint16"
+
+
+def _sb(cols, d):
+    return ("sbuf", [128, cols], d)
+
+
+SCRATCH = {
+    "X": _sb(W, B), "Xp": _sb(W, B), "Ms": _sb(W, B), "Mu": _sb(W, B), "Mp": _sb(6 * W, B), "Sg": _sb(512, F), "G0": _sb(128, H),
+    "lq": _sb(5 * 3 * 512, B), "Wm": _sb(W + 16, B), "Wc": _sb(W, B), "W0": _sb(W, B), "IW": _sb(W, B),
+    "D0": _sb(W, B), "D1": _sb(W, B), "D2": _sb(W, B), "D3": _sb(W, B),
+    "tA": _sb(TW, F), "tB": _sb(TW, F), "zer": _sb(2064, F), "val": _sb(W, F), "inv": _sb(W, H),
+    "V0": _sb(W, F), "V1": _sb(W, F), "R": _sb(W, F), "Tg": _sb(W, F),
+    "pb": _sb(W, B), "p4": _sb(W, B), "e32": _sb(512, I32), "eu": _sb(512, U), "eh": _sb(512, H),
+    "g32": _sb(128, I32), "gu": _sb(128, U), "gn": _sb(128, U), "rh": _sb(8, F), "tab": _sb(128, F),
+    "pi": _sb(8, I32), "pj": _sb(8, I32), "pf": _sb(16, F), "iom": _sb(144, F), "iog": _sb(128, F), "ib": _sb(16, F),
+    "E": _sb(144, F), "EA": _sb(144, B), "EB": _sb(144, B), "EC": _sb(144, B), "EN": _sb(144, B), "EI": _sb(144, H),
+    "Ih": _sb(128, H), "Iq": _sb(128, H), "Pq": _sb(128, H), "Ib": _sb(128, B), "Nb": _sb(128, B), "ob": _sb(128, B),
+    "GM": _sb(128, F), "LT": _sb(128, H), "U1": _sb(128, F), "U2": _sb(128, F), "mB": _sb(16, F),
+    "cap": _sb(128, B), "N5": _sb(128, B), "tie": _sb(4, F), "l0": _sb(128, H), "dum": _sb(128, F), "wr": _sb(8, F),
+    "loc": _sb(132, F), "Rm": _sb(16, H), "s1": _sb(128, F), "s3": _sb(128, F), "s4": _sb(128, F),
+    "car": _sb(4, F), "mid": _sb(4, F), "lst": _sb(128, U), "l2u": _sb(128, U), "l2h": _sb(128, H), "l3u": _sb(128, U),
+    "l3h": _sb(128, H), "cu": _sb(128, U), "dg": _sb(512, H), "acc": _sb(16, F), "mn": _sb(4, F),
+    "ivh": _sb(RO * 128, H), "li": _sb(RO * 3 * 128, H), "muu": _sb(128, U), "msu": _sb(128, U), "muf": _sb(132, F),
+    "du": _sb(128, U), "ixu": _sb(128, U), "gpu": _sb(128, U), "a1": _sb(128, F), "a2": _sb(128, B), "a3": _sb(128, B),
+    "lf": _sb(3 * 512, F), "Mg": _sb(512, F), "yo": _sb(512, F),
+    "st": ("dram", [3, 128, 256], B), "ld": ("dram", [3, 128, 256], B),
+    "hd": ("dram", [5 * 256, 512], B),
+    "PA": ("psum", [128, 512], F), "PB": ("psum", [128, 512], F), "PC": ("psum", [128, 512], F),
+    "PD": ("psum", [128, 512], F), "PG": ("psum", [128, 512], F), "PF": ("psum", [128, 512], F),
+    "PS": ("psum", [128, 1024], F),
+}
+ARR = (["ag"] + ["aq%d" % t for t in range(5)] + ["ah%d" % t for t in range(5)] + ["am%d" % t for t in range(5)]
+       + ["ai%d" % t for t in range(RO)] + ["an%d" % t for t in range(3)] + ["af%d" % t for t in range(3)])
+SEMAPHORES = ["cD", "cA", "cP", "cG"] + ARR + ["s%d" % k for k in range(110)]
+ESZ = {F: 4, B: 2, H: 2, I32: 4, U: 2}
+AL = AluOpType
+AF = ActivationFunctionType
+
+
+def bits(es):
+    m = 0
+    for e in es:
+        m |= 1 << e
+    return m
+
+
+def helper_of(T, topo, c):
+    return [h for h in topo.cores_of(c) if T.rank_of(h) is None and topo.die(h) == topo.die(c)][0]
+
+
+def split_engines(T, topo, core):
+    mates = topo.cores_of(core)
+    far = topo.engines(core, [c for c in T.cores if c not in mates][0])
+    near = topo.engines(core, [c for c in mates if c != core][0])
+    return [e for e in near if e not in far], far
+
+
+def dest(topo, d, core):
+    rid, pid = topo.addr(d, core)
+    return DstId(rid=rid, pnc=pid)
+
+
+def helper_program(g, core, T, topo, q):
+    e_near, e_far = split_engines(T, topo, core)
+    near = [c for c in T.cores if c in topo.cores_of(core)]
+    far = [c for c in T.cores if c not in near]
+    n = len(e_far) // 2
+    plan = [(c, e_far[k * n:(k + 1) * n]) for k, c in enumerate(far)] + [(c, e_near[k * n:(k + 1) * n]) for k, c in enumerate(near)]
+    for t in range(6):
+        r0 = 256 * t + 16 if t < 4 else 1024 + 128 * (t - 4)
+        if t < 5:
+            g.wait_ge(T.sem["ah%d" % t], len(e_near) + len(e_far))
+        g.remote_dma_fused([RemoteDMATransfer(dst_ids=[dest(topo, c, core)], dma_engine_mask=bits(es),
+                                              remote_sem=T.sem["am%d" % min(t, 4)], src=T.hd[r0:r0 + 128, :],
+                                              dst=T.Mp[:, W * t + 512 * q:W * t + 512 * q + 512])
+                            for c, es in plan], local_sem=T.sem["s0"])
+    g.wait_ge(T.sem["s0"], 6 * 4 * n)
+
+
+def emit(g, T, ops):
+    Q = {"D": g.vector, "A": g.scalar, "P": g.tensor, "G": g, "S": g.sync}
+    hist = {}
+    know = {q: {} for q in Q}
+    for n, o in enumerate(ops):
+        deps = set(o.get("after", []))
+        for wr, regs in ((False, o["r"]), (True, o["w"])):
+            for (b, pm, c0, c1) in regs:
+                ps = SCRATCH[b][0] == "psum"
+                for (m, w2, pm2, d0, d1) in hist.get(b, []):
+                    if o["grp"] and o["grp"] == ops[m]["grp"]:
+                        continue
+                    if ps and ops[m]["q"] != o["q"]:
+                        deps.add(m)
+                    elif (wr or w2) and (pm & pm2) and c0 < d1 and d0 < c1 and not (ps and o["q"] == "P"):
+                        deps.add(m)
+        for wr, regs in ((False, o["r"]), (True, o["w"])):
+            for (b, pm, c0, c1) in regs:
+                hist.setdefault(b, []).append((n, wr, pm, c0, c1))
+        o["waits"] = []
+        if o["k"] == "arr":
+            o["snap"] = {("t", n): n}
+            continue
+        kn = know[o["q"]]
+        for m in sorted(deps, reverse=True):
+            p = ops[m]
+            key = p["q"] if p["k"] == "c" else ("t", m)
+            if kn.get(key, -1) >= m:
+                continue
+            o["waits"].append(m)
+            p["need"] = True
+            for k2, v2 in p["snap"].items():
+                if kn.get(k2, -1) < v2:
+                    kn[k2] = v2
+        o["snap"] = dict(kn)
+        o["snap"][o["q"] if o["k"] == "c" else ("t", n)] = n
+    cnt = {q: 0 for q in Q}
+    pool = [0]
+    for o in ops:
+        if o["k"] == "arr":
+            continue
+        e = Q[o["q"]]
+        for m in o["waits"]:
+            e.wait_ge(T.sem[ops[m]["tok"][0]], ops[m]["tok"][1])
+        if o["k"] == "c":
+            ins = o["f"](e)
+            if o.get("need"):
+                cnt[o["q"]] += 1
+                o["tok"] = ("c" + o["q"], cnt[o["q"]])
+                ins.then_inc(T.sem[o["tok"][0]], 1)
+        else:
+            s = "s%d" % pool[0]
+            pool[0] += 1
+            if o["k"] == "dma":
+                o["tok"] = (s, 16)
+                o["f"](e).then_inc(T.sem[s], 16)
+            else:
+                o["tok"] = (s, o["n"])
+                o["f"](e, T.sem[s])
+    for o in ops:
+        if o["k"] != "c" and not o.get("need"):
+            g.wait_ge(T.sem[o["tok"][0]], o["tok"][1])
+
+
+def rank_program(g, core, T, topo):
+    rank = T.rank_of(core)
+    if rank is None:
+        for q, c in enumerate(T.cores):
+            if core == helper_of(T, topo, c):
+                helper_program(g, core, T, topo, q)
+        return
+    cores = list(T.cores)
+    ops = []
+    grp = [0]
+    ALLP = (1 << 128) - 1
+
+    def v(name, c0=None, c1=None, st=1, rows=None):
+        shp, d = SCRATCH[name][1], SCRATCH[name][2]
+        c0 = 0 if c0 is None else c0
+        c1 = shp[1] if c1 is None else c1
+        pm = ALLP
+        if rows is None:
+            rs = slice(0, 128)
+        else:
+            rs = slice(rows[0], rows[1], rows[2])
+            pm = bits(range(rows[0], rows[1], rows[2]))
+        ap = T[name][rs, c0:c1:st] if st != 1 else T[name][rs, c0:c1]
+        z = ESZ[d]
+        return {"ap": ap, "reg": [(name, pm, c0 * z // 16, (c1 * z + 15) // 16)]}
+
+    def dr(name, ap, k):
+        return {"ap": ap, "reg": [(name, ALLP, k, k + 1)]}
+
+    def ext(ap):
+        return {"ap": ap, "reg": []}
+
+    def ind(win, off):
+        return {"ap": win["ap"].indirect(off["ap"]), "reg": win["reg"] + off["reg"], "off": off["reg"], "win": win["reg"]}
+
+    def add(q, k, f, r, w, **kw):
+        rr, ww = [], []
+        for x in r:
+            if isinstance(x, dict):
+                rr += x["reg"]
+        for x in w:
+            ww += x.get("win", x["reg"])
+            rr += x.get("off", [])
+        o = {"q": q, "k": k, "f": f, "r": rr, "w": ww, "grp": grp[0]}
+        o.update(kw)
+        ops.append(o)
+
+    def a_(x):
+        return x["ap"] if isinstance(x, dict) else x
+
+    def cp(o, i):
+        add("D", "c", lambda e: e.tensor_copy(o["ap"], i["ap"]), [i], [o])
+
+    def tt(o, a, b, op):
+        add("D", "c", lambda e: e.tensor_tensor(o["ap"], a["ap"], b["ap"], op), [a, b], [o])
+
+    def ts(o, a, s1, op0, s2=None, op1=None):
+        if op1 is None:
+            add("D", "c", lambda e: e.tensor_scalar(o["ap"], a["ap"], a_(s1), None, op0), [a, s1], [o])
+        else:
+            add("D", "c", lambda e: e.tensor_scalar(o["ap"], a["ap"], a_(s1), a_(s2), op0, op1), [a, s1, s2], [o])
+
+    def ms(o, c):
+        add("D", "c", lambda e: e.memset(o["ap"], c), [], [o])
+
+    def red(o, i, op):
+        add("D", "c", lambda e: e.tensor_reduce(o["ap"], i["ap"], AxisListType.X, op), [i], [o])
+
+    def scan(o, a, b, init):
+        add("D", "c", lambda e: e.tensor_tensor_scan(o["ap"], a["ap"], b["ap"], a_(init), AL.max, AL.max), [a, b, init], [o])
+
+    def act(o, i, fn, bias=None, scale=None, acc=None):
+        kw = {}
+        if bias is not None:
+            kw["bias"] = a_(bias)
+        if scale is not None:
+            kw["scale"] = a_(scale)
+        if acc is not None:
+            kw["accum_out"] = acc["ap"]
+        add("A", "c", lambda e: e.activation(o["ap"], i["ap"], fn, **kw), [i, bias, scale], [o] + ([acc] if acc else []))
+
+    def mm(o, l, r, start, stop):
+        add("P", "c", lambda e: e.matmul(o["ap"], l["ap"], r["ap"], start, stop), [l, r], [o])
+
+    def dma(q, o, i, acc=False):
+        if acc:
+            add(q, "dma", lambda e: e.dma_start(o["ap"], i["ap"], accum_op=AL.add), [i], [o])
+        else:
+            add(q, "dma", lambda e: e.dma_start(o["ap"], i["ap"]), [i], [o])
+
+    def iota(o, pat, base, cm):
+        small = SCRATCH[o["reg"][0][0]][2] != I32
+        add("G", "c", lambda e: e.iota(o["ap"], pat, base, cm, allow_small_or_imprecise_dtypes=small) if small
+            else e.iota(o["ap"], pat, base, cm), [], [o])
+
+    def send(trs):
+        def f(e, s):
+            e.remote_dma_fused([RemoteDMATransfer(dst_ids=[dest(topo, c, core) for c in cs], dma_engine_mask=bits(es),
+                                                  remote_sem=T.sem[sem], srcs=[x["ap"] for x in srcs],
+                                                  dsts=[x["ap"] for x in dsts], alu_op=alu)
+                                for (cs, es, sem, srcs, dsts, alu) in trs], local_sem=s)
+        add("G", "rem", f, [x for tr in trs for x in tr[3]], [], n=sum(len(tr[1]) for tr in trs))
+
+    def arrive(o, sem, n):
+        add("-", "arr", None, [], [o], tok=(sem, n))
+
+    def gat(q, o, win, off, scale=None):
+        if q == "D" and scale is not None:
+            ts(o, ind(win, off), scale, AL.mult)
+        elif q == "D":
+            cp(o, ind(win, off))
+        else:
+            act(o, ind(win, off), AF.Identity, scale=scale)
+
+    def gat4(oname, win, lname, qd=(0, 1), qa=(2, 3)):
+        for a, b in zip(qd, qa):
+            gat("D", v(oname, 512 * a, 512 * a + 512), win, v(lname, 32 * a, 32 * a + 32))
+            gat("A", v(oname, 512 * b, 512 * b + 512), win, v(lname, 32 * b, 32 * b + 32))
+
+    def conv(o, em, src, k0=0, k1=128):
+        for i in range(16):
+            mm(v(o, k0, k1), v(em, 15 - i, 143 - i), v(src, 16 * k0 + i, 16 * (k1 - 1) + i + 1, 16), i == 0, i == 15)
+
+    chipmates = topo.cores_of(core)
+    near = [q for q in range(4) if q != rank and cores[q] in chipmates]
+    far = [q for q in range(4) if cores[q] not in chipmates]
+    e_near, e_far = split_engines(T, topo, core)
+    hf = len(e_far) // 2
+    eng3 = {near[0]: e_near, far[0]: e_far[:hf], far[1]: e_far[hf:]}
+    n3 = len(e_near) + len(e_far)
+    prev = (rank - 1) % 4
+    e_prev = e_near if prev in near else e_far
+    n_next = len(e_near) if (rank + 1) % 4 in near else len(e_far)
+    hlp = helper_of(T, topo, core)
+
+    def slot(frm, to):
+        return (frm - to) % 4 - 1
+
+    def quarters(src, t):
+        for qs in ([far + near] if t == 0 else [far, near]):
+            send([([cores[q]], eng3[q], "aq%d" % t, [v(src, 512 * q, 512 * q + 512)],
+                   [v("lq", 1536 * t + 512 * slot(rank, q), 1536 * t + 512 * slot(rank, q) + 512)], 0) for q in qs])
+        arrive(v("lq", 1536 * t, 1536 * t + 1536), "aq%d" % t, n3)
+
+    def fold(src, t):
+        srcs = [v(src, 512 * rank, 512 * rank + 512)] + [v("lq", 1536 * t + 512 * k, 1536 * t + 512 * k + 512) for k in range(3)]
+        ds = [ext(T.hd[256 * t + 128 * k:256 * t + 128 * k + 128, :]) for k in range(2)]
+        if t < 4:
+            send([([hlp], e_near, "ah%d" % t, srcs, ds[:1], 2), ([hlp], e_far, "ah%d" % t, srcs, ds[1:], 2)])
+            arrive(v("Mp", W * t, W * t + W), "am%d" % t, 4 * hf)
+        else:
+            send([([hlp], e_near, "ah4", srcs, ds[:1], 2), ([hlp], e_far, "ah4", srcs, ds[1:], 1)])
+            arrive(v("Mp", W * t, W * t + 2 * W), "am4", 8 * hf)
+
+    def blocks(em, src):
+        mm(v("PA", 0, 128), v("Ib"), v("ob"), True, False)
+        order = [0, 1, 2, 3, 8, 9, 10, 11, 4, 5, 6, 7, 12, 13, 14, 15]
+        for i in order:
+            mm(v("PA", 0, 128), v(em, 15 - i, 143 - i), v(src, 128 * i, 128 * i + 128), False, i == 15)
+
+    def records():
+        p1, p2 = v("PA", 128, 256), v("PA", 256, 384)
+        scan(v("loc", 1, 129), v("PA", 0, 128), v("zer", 0, 128), 0.0)
+        ts(v("Rm"), v("mB"), v("loc", 128, 129), AL.add, 0.0, AL.max)
+        mm(v("PB", 0, 16), v("LT"), v("Rm"), True, True)
+        tt(p1, v("PA", 0, 128), v("loc", 0, 128), AL.is_gt)
+        tt(v("s3"), p1, v("loc", 1, 129), AL.mult)
+        red(v("car", 0, 1), v("PB", 0, 16), AL.max)
+        ts(p1, v("s3"), v("car", 0, 1), AL.is_le)
+        tt(p2, p1, v("dum"), AL.mult)
+        tt(v("s4"), p2, v("s3"), AL.max)
+        cp(v("lst"), v("s4"))
+
+    def scat_d(ka):
+        cp(ind(v("tA"), v("lst", 0, ka)), v("val", 0, 16 * ka))
+
+    def scat_a(ka):
+        act(ind(v("tB"), v("lst", ka, 128)), v("val", 16 * ka, W), AF.Silu)
+
+    def running(between=False):
+        scan(v("inv", 0, 1024), v("tA", 1, 1025), v("tB", 1, 1025), 0.0)
+        if between:
+            slopes(part=1)
+        conv("PC", "EI", "inv", 0, 64)
+        mm(v("PB", 128, 129), v("G0"), v("inv", 1023, 1024), True, True)
+        scan(v("inv", 1024, W), v("tA", 1025, W + 1), v("tB", 1025, W + 1), 0.0)
+        conv("PB", "EI", "inv", 64, 128)
+
+    def inv_half(o, c0, h):
+        if h == 0:
+            cp(v(o, c0, c0 + 64), v("PC", 0, 64))
+        else:
+            ts(v(o, c0 + 64, c0 + 128), v("PB", 64, 128), v("PB", 128, 129), AL.max)
+
+    def wipe(behind=None):
+        r16 = (0, 128, 16)
+        for n in ("tA", "tB"):
+            dma("S", v(n, 0, 2052, rows=r16), v("zer", 0, 2052, rows=r16))
+            if behind is not None:
+                ops[-1]["after"] = [behind]
+
+    def score(k, lname, l0, Ms, cuts):
+        for c in range(len(cuts) - 1):
+            a, b = cuts[c], cuts[c + 1]
+            tt(v("D%d" % k, 16 * a, 16 * b), ind(v("X"), v(lname, l0 + a, l0 + b)), v(Ms[0], Ms[1] + 16 * a, Ms[1] + 16 * b), AL.subtract)
+
+    def absum(k, cuts, which, q="A"):
+        for c in which:
+            d = v("D%d" % k, 16 * cuts[c], 16 * cuts[c + 1])
+            o = v("acc", 4 * c + k, 4 * c + k + 1)
+            if q == "A":
+                act(d, d, AF.Abs, acc=o)
+            else:
+                add("D", "c", lambda e, o=o, d=d: e.tensor_reduce(o["ap"], d["ap"], AxisListType.X, AL.add,
+                                                                  apply_absolute_value=True), [d], [o])
+
+    def stay(h, Ms, src="X", k=0):
+        for c in range(2):
+            o = 1024 * h + 512 * c
+            mm(v("PS", 512 * c, 512 * c + 512), v("Ib"), v(src, o, o + 512), True, False)
+            mm(v("PS", 512 * c, 512 * c + 512), v("Nb"), v(Ms[0], Ms[1] + o, Ms[1] + o + 512), False, True)
+        act(v("D0", 1024 * h, 1024 * h + 1024), v("PS"), AF.Abs, acc=v("acc", 4 * h + k, 4 * h + k + 1))
+
+    def slopes_pe(k0=0, k1=128):
+        conv("PG", "EC", "Wc", k0, k1)
+        conv("PF", "EB", "Wc", k0, k1)
+
+    def mu_slope():
+        cp(v("muf", 0, 128), v("muu"))
+        mm(v("PD", 0, 128), v("U1"), v("muf", 0, 128), True, False)
+        mm(v("PD", 0, 128), v("U2"), v("muf", 1, 129), False, True)
+
+    def slopes(k0=0, k1=128, part=None):
+        if part != 1:
+            act(v("a1", k0, k1), v("PG", k0, k1), AF.Abs)
+            act(v("a3", k0, k1), v("a1", k0, k1), AF.Relu, bias=4.0, scale=-1.0)
+            mm(v("PS", k0, k1), v("Ib"), v("cap", k0, k1), True, False)
+            mm(v("PS", k0, k1), v("Nb"), v("a2", k0, k1), False, False)
+            mm(v("PS", k0, k1), v("N5"), v("a3", k0, k1), False, True)
+        if part != 0:
+            cp(v("ixu", k0, k1), v("PS", k0, k1))
+            if part is None:
+                cp(v("du", k0, k1), v("PF", k0, k1))
+
+    def mu_cap():
+        act(v("a2"), v("PD", 0, 128), AF.Relu, bias=4.0, scale=-1.0)
+
+    dma("S", v("g32"), ext(T.gam[:]))
+    dma("A", v("X"), ext(T.xs[:]))
+    iota(v("pi", 0, 2), [[112, 2]], 0, 1)
+    iota(v("iom"), [[1, 144]], 0, 0)
+    iota(v("iog"), [[16, 8], [0, 16]], 0, 0)
+    dma("S", v("e32"), ext(T.ew[:]))
+    dma("S", v("rh", 0, 5), ext(T.rho[:]))
+    ms(v("zer", 0, 128), 0.0)
+    ms(v("ob"), 1.0)
+    ms(v("loc"), 0.0)
+    ms(v("acc"), 0.0)
+    ts(v("pj", 0, 1), v("pi", 0, 1), 15, AL.bitwise_and)
+    ts(v("pj", 1, 3), v("pi", 0, 2), 112, AL.bitwise_and)
+    ts(v("pj", 3, 5), v("pi", 0, 2), 127, AL.bitwise_and)
+    cp(v("pf", 0, 5), v("pj", 0, 5))
+    pm, gb, gbp, pp, ppm = [v("pf", k, k + 1) for k in range(5)]
+    lo, hi = v("pf", 8, 9), v("pf", 12, 13)
+    ts(lo, pm, 8.0, AL.is_ge)
+    ts(hi, pm, 8.0, AL.is_lt)
+    ts(v("ib"), v("iom", 0, 16), lo, AL.mult)
+    grp[0] = 1
+    act(v("val", 15, W, 16), v("iom", 0, 128), AF.Silu, bias=1920.0)
+    for i in range(16):
+        act(v("IW", i, W - 15 + i, 16), v("iom", 0, 128), AF.Identity, bias=v("ib", i, i + 1), scale=hi)
+    for i in range(15):
+        act(v("val", i, W - 15 + i, 16), v("iom", 0, 128), AF.Identity, bias=float(128 * i))
+    grp[0] = 0
+    cp(v("gu"), v("g32"))
+    quarters("X", 0)
+    send([([cores[prev]], e_prev, "ag", [v("gu")], [v("gn")], 0)])
+    arrive(v("gn"), "ag", n_next)
+    fold("X", 0)
+    ms(v("tA", 0, 2052), 0.0)
+    act(v("tB", 0, 2052), v("tA", 0, 2052), AF.Identity)
+    dma("S", v("zer", 128, 2052, rows=(0, 128, 16)), v("tA", 128, 2052, rows=(0, 128, 16)))
+    ts(v("wr", 0, 4), v("iom", 0, 4), pm, AL.is_equal, 16.0, AL.mult)
+    ts(v("wr", 4, 8), v("iom", 8, 12), pm, AL.is_equal)
+    ts(v("E"), v("iom"), -15.0, AL.add, gbp, AL.is_equal)
+    ts(v("Ib"), v("iom", 0, 128), pp, AL.is_equal)
+    tt(v("wr", 0, 4), v("wr", 0, 4), v("wr", 4, 8), AL.add)
+    tt(v("wr", 4, 5), v("wr", 2, 3), v("wr", 1, 2), AL.subtract)
+    ts(v("EN"), v("E"), v("wr", 3, 4), AL.mult)
+    ts(v("mB"), v("iom", 0, 16), pm, AL.not_equal, -4096.0, AL.mult)
+    ts(v("GM"), v("iog"), gb, AL.is_equal)
+    ts(v("s1"), v("iom", 0, 128), pp, AL.is_gt)
+    ts(v("l0"), v("iom", 0, 128), 16.0, AL.mult, pm, AL.add)
+    ts(v("wr", 5, 6), pm, 0.0, AL.is_equal)
+    ts(v("E"), v("iom"), -15.0, AL.add, gb, AL.is_equal)
+    tt(v("LT"), v("s1"), v("GM"), AL.mult)
+    ts(v("dum"), v("l0"), 2049.0, AL.add)
+    ts(v("wr", 6, 7), pm, 0.0, AL.not_equal)
+    ts(v("EI"), v("E"), v("wr", 5, 6), AL.mult)
+    ts(v("Ih"), v("iom", 0, 128), pp, AL.is_equal)
+    ts(v("Nb"), v("Ib"), -1.0, AL.mult)
+    cp(v("eu"), v("e32"))
+    ts(v("G0"), v("GM"), v("wr", 5, 6), AL.mult)
+    ts(v("EA"), v("E"), v("wr", 0, 1), AL.mult)
+    ts(v("tie"), v("iom", 0, 4), 4.0, AL.add, 1.0 / 64, AL.mult)
+    gat4("W0", v("IW"), "gn")
+    cp(v("eh"), v("e32"))
+    gat("A", v("D1"), v("X"), v("eu", 0, 128))
+
+    def late_constants():
+        ts(v("EB"), v("E"), v("wr", 1, 2), AL.mult)
+        ts(v("EC"), v("E"), v("wr", 4, 5), AL.mult)
+        ts(v("U2"), v("E", 0, 128), v("wr", 5, 6), AL.mult)
+        ts(v("Iq"), v("Ih"), 0.25, AL.mult)
+        ts(v("Pq"), v("iom", 0, 128), ppm, AL.is_equal, 0.25, AL.mult)
+        ts(v("a1"), v("iom", 1, 129), pp, AL.is_equal, v("wr", 6, 7), AL.mult)
+        act(v("p4"), v("pb"), AF.Identity, scale=0.25)
+        ms(v("cap"), 24.0)
+        ts(v("N5"), v("Ib"), -5.0, AL.mult)
+        ms(v("tab"), 0.0)
+        ms(v("muf", 128, 132), 4096.0)
+        tt(v("U1"), v("a1"), v("Ih"), AL.subtract)
+        ts(v("cap", 127, 128), pm, 15.0, AL.not_equal, 3.0, AL.mult)
+        ts(v("cap", 127, 128), v("cap", 127, 128), 21.0, AL.add)
+        for s in range(5):
+            ts(v("tab", 32 + 5 * s, 37 + 5 * s), v("rh", 0, 5), v("rh", s, s + 1), AL.mult)
+        ts(v("tab", 0, 25), v("tab", 32, 57), 32.0, AL.mult)
+        ts(v("tab", 64, 89), v("tab", 32, 57), 1.0 / 128, AL.mult)
+
+    H2, C3 = [0, 64, 128], [0, 56, 104, 128]
+    for t in range(RO):
+        last = t == RO - 1
+        Ms = ("Ms", 0) if t else ("Mp", 0)
+        src = "W0" if t == 0 else "Wc"
+        ka = KA1 if t else KA0
+        if t > 0:
+            gat4("Wc", v("Wm", 0, W), "muu")
+            ts(v("msu"), v("PG", 0, 128), -0.375, AL.add)
+            gat("A", v("X"), v("Xp"), v("muu"))
+        blocks("EN", src)
+        if t > 0:
+            mu_slope()
+        records()
+        conv("PF", "EN", src)
+        if t > 0:
+            gat("A", v(Ms[0]), v("Mp", W * t, W * t + W), v("msu"))
+            conv("PG", "EC", "Wc")
+        scat_d(ka)
+        scat_a(ka)
+        cp(v("l2u"), v("PF", 0, 128))
+        cp(v("l2h"), v("PF", 0, 128))
+        if t == 0:
+            gat("A", v("Wc"), v("IW"), v("gu"))
+            running()
+            dma("S", v("pb"), ext(T.pay[:]))
+        else:
+            conv("PF", "EB", "Wc")
+            dma("S", v("Mu", rows=(16, 128, 1)), v(Ms[0], rows=(0, 112, 1)))
+            dma("S", v("Mu", rows=(0, 16, 1)), v(Ms[0], rows=(112, 128, 1)))
+        dma("S", v("Wc", rows=(1, 128, 8)), v("IW", rows=(1, 128, 8)))
+        if t > 0:
+            score(1, "eu", 128 * t, Ms, H2)
+            score(2, "l2u", 0, Ms, H2)
+            stay(0, Ms)
+            absum(1, H2, [0])
+            stay(1, Ms)
+            absum(1, H2, [1])
+            absum(2, H2, [0, 1])
+        else:
+            score(2, "l2u", 0, Ms, H2)
+            stay(0, Ms)
+            absum(2, H2, [0])
+            stay(1, Ms)
+            absum(2, H2, [1])
+            stay(0, Ms, "D1", 1)
+            stay(1, Ms, "D1", 1)
+        if t > 0:
+            running()
+        wipe()
+        inv_half("l3u", 0, 0)
+        inv_half("l3h", 0, 0)
+        score(3, "l3u", 0, Ms, C3[:2])
+        inv_half("l3u", 0, 1)
+        inv_half("l3h", 0, 1)
+        mm(v("PB", 0, 4), v("GM"), v("tie"), True, False)
+        score(3, "l3u", 0, Ms, C3[1:])
+        absum(3, C3, [0, 1] if t else [0])
+        absum(3, C3, [2] if t else [2, 1], "D")
+        for c in (0, 2, 1):
+            mm(v("PB", 0, 4), v("GM"), v("acc", 4 * c, 4 * c + 4), False, c == 1)
+        red(v("mn", 0, 1), v("PB", 0, 4), AL.min)
+        for k in range(4):
+            ts(v("dg", 128 * k, 128 * k + 128), v("Ih"), v("PB", k, k + 1), AL.mult, v("mn", 0, 1), AL.is_equal)
+        for k, l in enumerate([v("l0"), v("eh", 128 * t, 128 * t + 128), v("l2h"), v("l3h")]):
+            mm(v("PA", 0, 128), v("dg", 128 * k, 128 * k + 128), l, k == 0, k == 3)
+        cp(v("cu"), v("PA", 0, 128))
+        gat4("Wm", v("Wc"), "cu")
+        if not last:
+            dma("S", dr("st", T.st[t], t), v("Wm", 0, W, rows=(0, 128, 8)))
+        blocks("EA", "Wm")
+        if t > 0:
+            cp(v("du"), v("PF", 0, 128))
+        k0 = 32 * far[0]
+        gat("A", v("Xp", 16 * k0, 16 * k0 + 1024), v("X"), v("cu", k0, k0 + 64))
+        act(v("Wm", W, W + 1), v("Wm", W - 1, W), AF.Identity, bias=lo)
+        gat("A", v("Xp", 512 * near[0], 512 * near[0] + 512), v("X"), v("cu", 32 * near[0], 32 * near[0] + 32))
+        quarters("Xp", t + 1)
+        records()
+        if t > 0:
+            mu_cap()
+            slopes(part=0)
+        dma("S", v("Wm", 0, W, rows=(2, 128, 8)), v("Wm", 1, W + 1, rows=(1, 128, 8)))
+        if not last:
+            send([([cores[prev]], e_prev, "an%d" % t, [dr("st", T.st[t], t)], [dr("ld", T.ld[t], t)], 0)])
+            arrive(dr("ld", T.ld[t], t), "an%d" % t, n_next)
+            dma("S", v("Wm", 0, W, rows=(3, 128, 8)), dr("ld", T.ld[t], t))
+        scat_d(KA2)
+        scat_a(KA2)
+        if not last:
+            gat("A", v("Xp", 512 * rank, 512 * rank + 512), v("X"), v("cu", 32 * rank, 32 * rank + 32))
+            fold("Xp", t + 1)
+        if t > 0:
+            slopes(part=1)
+            for h in range(2):
+                gat("A", v("R", 1024 * h, 1024 * h + 1024), v("tab", 0 if t == 1 else 32, 32 if t == 1 else 64),
+                    v("ixu", 64 * h, 64 * h + 64))
+        if last:
+            gat("A", v("Xp", 512 * rank, 512 * rank + 512), v("X"), v("cu", 32 * rank, 32 * rank + 32))
+        running()
+        iv = v("ivh", 128 * t, 128 * t + 128)
+        inv_half("ivh", 128 * t, 0)
+        inv_half("ivh", 128 * t, 1)
+        send([([cores[q]], eng3[q], "ai%d" % t, [iv],
+               [v("li", 384 * t + 128 * slot(rank, q), 384 * t + 128 * slot(rank, q) + 128)], 0) for q in eng3])
+        if not last:
+            wipe(len(ops) - 1)
+        arrive(v("li", 384 * t, 384 * t + 384), "ai%d" % t, n3)
+        if last:
+            fold("Xp", t + 1)
+        if t == 0:
+            late_constants()
+        if t > 0:
+            vo = "V%d" % (t % 2)
+            vi = v("pb") if t == 1 else v("V%d" % ((t + 1) % 2))
+            for a, b in [(0, 1024), (1024, W)]:
+                tt(v(vo, a, b), ind(vi, v("du", a // 16, b // 16)), v("R", a, b), AL.mult)
+                if not last:
+                    if a == 0:
+                        continue
+                    a = 0
+                dma("G", v(vo, a, b), v("Mu", a, b), acc=True)
+        parts = [iv] + [v("li", 384 * t + 128 * k, 384 * t + 128 * k + 128) for k in range(3)]
+        for k in range(4):
+            mm(v("PD", 0, 128), v("Iq"), parts[k], k == 0, k == 3)
+        ts(v("muu"), v("PD", 0, 128), -0.375, AL.add)
+        if not last:
+            for k in range(4):
+                mm(v("PG", 0, 128), v("Pq"), parts[k], k == 0, k == 3)
+
+    far.sort(key=lambda q: topo.die(cores[q]) != topo.die(core))
+    order = far + near + [rank]
+    mu_slope()
+    gat4("Wc", v("Wm", 0, W), "muu", (order[0], order[2]), (order[1], order[3]))
+
+    def lists(hh):
+        k0 = 32 * min(order[2 * hh:2 * hh + 2])
+        pe, pd = ("PC", "PA") if hh else ("PB", "PF")
+        conv("PG", "EC", "Wc", k0, k0 + 64)
+        conv(pd, "EB", "Wc", k0, k0 + 64)
+        slopes(k0, k0 + 64, 0)
+        conv(pe, "EA", "Wc", k0, k0 + 64)
+        cp(v("du", k0, k0 + 64), v(pd, k0, k0 + 64))
+        slopes(k0, k0 + 64, 1)
+        cp(v("gpu", k0, k0 + 64), v(pe, k0, k0 + 64))
+
+    mu_cap()
+    lists(0)
+    for k, q in enumerate(order):
+        cs = (512 * q, 512 * q + 512)
+        gat("A", v("R", *cs), v("tab", 64, 96), v("ixu", 32 * q, 32 * q + 32))
+        tt(v("V0", *cs), ind(v("V1"), v("du", 32 * q, 32 * q + 32)), v("R", *cs), AL.mult)
+        s = slot(rank, q)
+        if k < 2:
+            tt(v("Tg", *cs), ind(v("p4"), v("gpu", 32 * q, 32 * q + 32)), v("V0", *cs), AL.add)
+            send([([cores[q]], e_far, "af%d" % s, [v("Tg", *cs)], [v("lf", 512 * s, 512 * s + 512)], 0)])
+        else:
+            gat("A", v("Tg", *cs), v("p4"), v("gpu", 32 * q, 32 * q + 32))
+        if k == 0:
+            lists(1)
+        if k == 2:
+            send([([cores[q]], e_near, "af%d" % s, [v("V0", *cs), v("Tg", *cs)], [v("lf", 512 * s, 512 * s + 512)], 1)])
+    cs = (512 * rank, 512 * rank + 512)
+    gat("A", v("Mg"), v("Mp", 4 * W, 5 * W), v("muu", 32 * rank, 32 * rank + 32), scale=1.0 / 32)
+    gat("A", v("Sg"), v("Mp", 5 * W, 6 * W), v("muu", 32 * rank, 32 * rank + 32), scale=1.0 / 64)
+    for s in range(3):
+        arrive(v("lf", 512 * s, 512 * s + 512), "af%d" % s, len(e_near) if (rank + s + 1) % 4 in near else len(e_far))
+    tt(v("PA"), v("V0", *cs), v("Tg", *cs), AL.add)
+    so = [slot(q, rank) for q in order[:3]]
+    tt(v("PA"), v("PA"), v("lf", 512 * so[0], 512 * so[0] + 512), AL.add)
+    tt(v("PA"), v("PA"), v("Mg"), AL.add)
+    tt(v("PA"), v("PA"), v("Sg"), AL.add)
+    tt(v("PA"), v("PA"), v("lf", 512 * so[1], 512 * so[1] + 512), AL.add)
+    tt(v("yo"), v("PA"), v("lf", 512 * so[2], 512 * so[2] + 512), AL.add)
+    dma("S", ext(T.y[:]), v("yo"))
+    emit(g, T, ops)

@@ -3,8 +3,10 @@ from concourse.mybir import dt, AluOpType, AxisListType, ActivationFunctionType
 
 W = 2048
 RO = 4
-KA0, KA1, KA2 = 62, 46, 64
-TW = 4112
+TW = 2576
+XD = 16
+AD = False
+KK = 8192.0
 F, B, H, I32, U = "float32", "bfloat16", "float16", "int32", "uint16"
 
 
@@ -13,33 +15,37 @@ def _sb(cols, d):
 
 
 SCRATCH = {
-    "X": _sb(W, B), "Xp": _sb(W, B), "Ms": _sb(W, B), "Mu": _sb(W, B), "Mp": _sb(6 * W, B), "Sg": _sb(512, F), "G0": _sb(128, H),
-    "lq": _sb(5 * 3 * 512, B), "Wm": _sb(W + 16, B), "Wc": _sb(W, B), "W0": _sb(W, B), "IW": _sb(W, B),
+    "X": _sb(W, B), "Xp": _sb(W, B), "Ms": _sb(W, B), "Mu0": _sb(W, B), "Mu1": _sb(W, B), "Mp": _sb(5 * W, B),
+    "lq": _sb(5 * 3 * 512, B), "Wm": _sb(W + 16, B), "Wc": _sb(W, B), "IW": _sb(W, B),
     "D0": _sb(W, B), "D1": _sb(W, B), "D2": _sb(W, B), "D3": _sb(W, B),
-    "tA": _sb(TW, F), "tB": _sb(TW, F), "zer": _sb(2064, F), "val": _sb(W, F), "inv": _sb(W, H),
-    "V0": _sb(W, F), "V1": _sb(W, F), "R": _sb(W, F), "Tg": _sb(W, F),
-    "pb": _sb(W, B), "p4": _sb(W, B), "e32": _sb(512, I32), "eu": _sb(512, U), "eh": _sb(512, H),
-    "g32": _sb(128, I32), "gu": _sb(128, U), "gn": _sb(128, U), "rh": _sb(8, F), "tab": _sb(128, F),
+    "tA": _sb(TW, F), "tB": _sb(TW, F), "zer": _sb(1040, F), "val": _sb(256, F), "inv": _sb(W + 16, H), "dec": _sb(1040, B),
+    "rst": _sb(128, H), "cz": _sb(128, H), "Bg": _sb(128, H), "KI": _sb(128, H), "KN": _sb(128, H), "Cs": _sb(136, H),
+    "Sel": _sb(128, H), "Q": _sb(128, H), "Kr": _sb(128, H), "Kf": _sb(128, H), "Z0": _sb(128, H), "cb": _sb(256, H),
+    "Eo": _sb(144, H), "mQ": _sb(256, H), "mF": _sb(256, H), "TA": _sb(144, H), "TB": _sb(144, H),
+    "Rot": _sb(128, H), "io8": _sb(128, F), "iod": _sb(16, F), "Ts": _sb(384, H), "S3": _sb(32, B), "gn32": _sb(128, I32), "gnh": _sb(128, H), "oh": _sb(128, H),
+    "pg": _sb(16, F), "ab": _sb(8, F),
+    "V0": _sb(W, F), "V1": _sb(W, F), "R": _sb(W, F),
+    "pb": _sb(W, B), "p4": _sb(W, B), "Tg": _sb(1024, F), "EA": _sb(144, B), "e32": _sb(512, I32), "eu": _sb(512, U), "eh": _sb(512, H),
+    "g32": _sb(128, I32), "gu": _sb(128, U), "rh": _sb(8, F), "tab": _sb(128, F),
     "pi": _sb(8, I32), "pj": _sb(8, I32), "pf": _sb(16, F), "iom": _sb(144, F), "iog": _sb(128, F), "ib": _sb(16, F),
-    "E": _sb(144, F), "EA": _sb(144, B), "EB": _sb(144, B), "EC": _sb(144, B), "EN": _sb(144, B), "EI": _sb(144, H),
-    "Ih": _sb(128, H), "Iq": _sb(128, H), "Pq": _sb(128, H), "Ib": _sb(128, B), "Nb": _sb(128, B), "ob": _sb(128, B),
-    "GM": _sb(128, F), "LT": _sb(128, H), "U1": _sb(128, F), "U2": _sb(128, F), "mB": _sb(16, F),
-    "cap": _sb(128, B), "N5": _sb(128, B), "tie": _sb(4, F), "l0": _sb(128, H), "dum": _sb(128, F), "wr": _sb(8, F),
-    "loc": _sb(132, F), "Rm": _sb(16, H), "s1": _sb(128, F), "s3": _sb(128, F), "s4": _sb(128, F),
-    "car": _sb(4, F), "mid": _sb(4, F), "lst": _sb(128, U), "l2u": _sb(128, U), "l2h": _sb(128, H), "l3u": _sb(128, U),
-    "l3h": _sb(128, H), "cu": _sb(128, U), "dg": _sb(512, H), "acc": _sb(16, F), "mn": _sb(4, F),
-    "ivh": _sb(RO * 128, H), "li": _sb(RO * 3 * 128, H), "muu": _sb(128, U), "msu": _sb(128, U), "muf": _sb(132, F),
+    "E": _sb(144, F), "EB": _sb(144, B), "EC": _sb(144, B), "EI": _sb(144, H),
+    "Ih": _sb(128, H), "Iq": _sb(128, H), "Ib": _sb(128, B), "Nb": _sb(128, B), "ob": _sb(384, B),
+    "GM": _sb(128, F), "U1": _sb(128, H), "U2": _sb(128, H),
+    "cap": _sb(128, B), "N5": _sb(128, B), "tie": _sb(4, F), "l0": _sb(128, H), "wr": _sb(8, F),
+    "loc": _sb(136, H), "s1": _sb(128, F), "s3": _sb(128, F), "s4": _sb(128, F),
+    "mid": _sb(4, F), "ltA": _sb(16, U), "ltB": _sb(16, U), "l2u": _sb(128, U), "l2h": _sb(128, H), "l3u": _sb(128, U),
+    "l3h": _sb(128, H), "cu": _sb(128, U), "dg": _sb(512, H), "acc": _sb(16 * RO, F), "mn": _sb(4, F),
+    "ivh": _sb(RO * 128, H), "li": _sb(RO * 3 * 128, H), "muu": _sb(128, U), "msu": _sb(128, U), "Rb": _sb(128, B), "rl": _sb(1536, B), "muf": _sb(132, H),
     "du": _sb(128, U), "ixu": _sb(128, U), "gpu": _sb(128, U), "a1": _sb(128, F), "a2": _sb(128, B), "a3": _sb(128, B),
-    "lf": _sb(3 * 512, F), "Mg": _sb(512, F), "yo": _sb(512, F),
+    "lf": _sb(3 * 512, F), "Mg": _sb(512, B), "yo": _sb(512, F),
     "st": ("dram", [3, 128, 256], B), "ld": ("dram", [3, 128, 256], B),
-    "hd": ("dram", [5 * 256, 512], B),
     "PA": ("psum", [128, 512], F), "PB": ("psum", [128, 512], F), "PC": ("psum", [128, 512], F),
     "PD": ("psum", [128, 512], F), "PG": ("psum", [128, 512], F), "PF": ("psum", [128, 512], F),
-    "PS": ("psum", [128, 1024], F),
+    "PS": ("psum", [128, 512], F), "PT": ("psum", [128, 512], F),
 }
-ARR = (["ag"] + ["aq%d" % t for t in range(5)] + ["ah%d" % t for t in range(5)] + ["am%d" % t for t in range(5)]
-       + ["ai%d" % t for t in range(RO)] + ["an%d" % t for t in range(3)] + ["af%d" % t for t in range(3)])
-SEMAPHORES = ["cD", "cA", "cP", "cG"] + ARR + ["s%d" % k for k in range(110)]
+ARR = (["ag", "ap"] + ["aq%d" % t for t in range(5)] + ["ah%d" % t for t in range(5)] + ["ak%d" % t for t in range(5)] + ["am%d" % t for t in range(5)]
+       + ["ai%d" % t for t in range(2 * RO)] + ["an%d" % t for t in range(3)] + ["af%d" % t for t in range(3)])
+SEMAPHORES = ["cD", "cA", "cP", "cG"] + ARR + ["s%d" % k for k in range(80)]
 ESZ = {F: 4, B: 2, H: 2, I32: 4, U: 2}
 AL = AluOpType
 AF = ActivationFunctionType
@@ -50,10 +56,6 @@ def bits(es):
     for e in es:
         m |= 1 << e
     return m
-
-
-def helper_of(T, topo, c):
-    return [h for h in topo.cores_of(c) if T.rank_of(h) is None and topo.die(h) == topo.die(c)][0]
 
 
 def split_engines(T, topo, core):
@@ -68,23 +70,6 @@ def dest(topo, d, core):
     return DstId(rid=rid, pnc=pid)
 
 
-def helper_program(g, core, T, topo, q):
-    e_near, e_far = split_engines(T, topo, core)
-    near = [c for c in T.cores if c in topo.cores_of(core)]
-    far = [c for c in T.cores if c not in near]
-    n = len(e_far) // 2
-    plan = [(c, e_far[k * n:(k + 1) * n]) for k, c in enumerate(far)] + [(c, e_near[k * n:(k + 1) * n]) for k, c in enumerate(near)]
-    for t in range(6):
-        r0 = 256 * t + 16 if t < 4 else 1024 + 128 * (t - 4)
-        if t < 5:
-            g.wait_ge(T.sem["ah%d" % t], len(e_near) + len(e_far))
-        g.remote_dma_fused([RemoteDMATransfer(dst_ids=[dest(topo, c, core)], dma_engine_mask=bits(es),
-                                              remote_sem=T.sem["am%d" % min(t, 4)], src=T.hd[r0:r0 + 128, :],
-                                              dst=T.Mp[:, W * t + 512 * q:W * t + 512 * q + 512])
-                            for c, es in plan], local_sem=T.sem["s0"])
-    g.wait_ge(T.sem["s0"], 6 * 4 * n)
-
-
 def emit(g, T, ops):
     Q = {"D": g.vector, "A": g.scalar, "P": g.tensor, "G": g, "S": g.sync}
     hist = {}
@@ -97,9 +82,11 @@ def emit(g, T, ops):
                 for (m, w2, pm2, d0, d1) in hist.get(b, []):
                     if o["grp"] and o["grp"] == ops[m]["grp"]:
                         continue
+                    u = 1 if o["k"] == "c" and ops[m]["k"] == "c" else 16
                     if ps and ops[m]["q"] != o["q"]:
                         deps.add(m)
-                    elif (wr or w2) and (pm & pm2) and c0 < d1 and d0 < c1 and not (ps and o["q"] == "P"):
+                    elif ((wr or w2) and (pm & pm2) and c0 // u <= (d1 - 1) // u and d0 // u <= (c1 - 1) // u
+                          and not (ps and o["q"] == "P")):
                         deps.add(m)
         for wr, regs in ((False, o["r"]), (True, o["w"])):
             for (b, pm, c0, c1) in regs:
@@ -152,16 +139,15 @@ def emit(g, T, ops):
 def rank_program(g, core, T, topo):
     rank = T.rank_of(core)
     if rank is None:
-        for q, c in enumerate(T.cores):
-            if core == helper_of(T, topo, c):
-                helper_program(g, core, T, topo, q)
         return
     cores = list(T.cores)
     ops = []
     grp = [0]
+    rnd = [0]
+    turn = [0]
     ALLP = (1 << 128) - 1
 
-    def v(name, c0=None, c1=None, st=1, rows=None):
+    def v(name, c0=None, c1=None, st=1, rows=None, rev=False):
         shp, d = SCRATCH[name][1], SCRATCH[name][2]
         c0 = 0 if c0 is None else c0
         c1 = shp[1] if c1 is None else c1
@@ -172,11 +158,13 @@ def rank_program(g, core, T, topo):
             rs = slice(rows[0], rows[1], rows[2])
             pm = bits(range(rows[0], rows[1], rows[2]))
         ap = T[name][rs, c0:c1:st] if st != 1 else T[name][rs, c0:c1]
+        if rev:
+            ap = T[name][rs, ::-1]
         z = ESZ[d]
-        return {"ap": ap, "reg": [(name, pm, c0 * z // 16, (c1 * z + 15) // 16)]}
+        return {"ap": ap, "reg": [(name, pm, c0 * z, c1 * z)]}
 
     def dr(name, ap, k):
-        return {"ap": ap, "reg": [(name, ALLP, k, k + 1)]}
+        return {"ap": ap, "reg": [(name, ALLP, 16 * k, 16 * k + 16)]}
 
     def ext(ap):
         return {"ap": ap, "reg": []}
@@ -217,8 +205,8 @@ def rank_program(g, core, T, topo):
     def red(o, i, op):
         add("D", "c", lambda e: e.tensor_reduce(o["ap"], i["ap"], AxisListType.X, op), [i], [o])
 
-    def scan(o, a, b, init):
-        add("D", "c", lambda e: e.tensor_tensor_scan(o["ap"], a["ap"], b["ap"], a_(init), AL.max, AL.max), [a, b, init], [o])
+    def scan(o, a, b, init, op0=AL.max, op1=AL.max):
+        add("D", "c", lambda e: e.tensor_tensor_scan(o["ap"], a["ap"], b["ap"], a_(init), op0, op1), [a, b, init], [o])
 
     def act(o, i, fn, bias=None, scale=None, acc=None):
         kw = {}
@@ -282,116 +270,156 @@ def rank_program(g, core, T, topo):
     prev = (rank - 1) % 4
     e_prev = e_near if prev in near else e_far
     n_next = len(e_near) if (rank + 1) % 4 in near else len(e_far)
-    hlp = helper_of(T, topo, core)
 
     def slot(frm, to):
         return (frm - to) % 4 - 1
 
+    def lq(t, frm, to):
+        c = 1536 * t + 512 * slot(frm, to)
+        return v("lq", c, c + 512)
+
     def quarters(src, t):
         for qs in ([far + near] if t == 0 else [far, near]):
-            send([([cores[q]], eng3[q], "aq%d" % t, [v(src, 512 * q, 512 * q + 512)],
-                   [v("lq", 1536 * t + 512 * slot(rank, q), 1536 * t + 512 * slot(rank, q) + 512)], 0) for q in qs])
-        arrive(v("lq", 1536 * t, 1536 * t + 1536), "aq%d" % t, n3)
+            send([([cores[q]], eng3[q], ("ah%d" if q in near else "aq%d") % t, [v(src, 512 * q, 512 * q + 512)],
+                   [lq(t, rank, q)], 0) for q in qs])
+        arrive(lq(t, near[0], rank), "ah%d" % t, len(e_near))
+        add("-", "arr", None, [], [lq(t, q, rank) for q in far], tok=("aq%d" % t, len(e_far)))
 
-    def fold(src, t):
-        srcs = [v(src, 512 * rank, 512 * rank + 512)] + [v("lq", 1536 * t + 512 * k, 1536 * t + 512 * k + 512) for k in range(3)]
-        ds = [ext(T.hd[256 * t + 128 * k:256 * t + 128 * k + 128, :]) for k in range(2)]
-        if t < 4:
-            send([([hlp], e_near, "ah%d" % t, srcs, ds[:1], 2), ([hlp], e_far, "ah%d" % t, srcs, ds[1:], 2)])
-            arrive(v("Mp", W * t, W * t + W), "am%d" % t, 4 * hf)
-        else:
-            send([([hlp], e_near, "ah4", srcs, ds[:1], 2), ([hlp], e_far, "ah4", srcs, ds[1:], 1)])
-            arrive(v("Mp", W * t, W * t + 2 * W), "am4", 8 * hf)
+    def mq(u, q):
+        return v("Mp", W * u + 512 * q, W * u + 512 * q + 512)
 
-    def blocks(em, src):
-        mm(v("PA", 0, 128), v("Ib"), v("ob"), True, False)
-        order = [0, 1, 2, 3, 8, 9, 10, 11, 4, 5, 6, 7, 12, 13, 14, 15]
-        for i in order:
-            mm(v("PA", 0, 128), v(em, 15 - i, 143 - i), v(src, 128 * i, 128 * i + 128), False, i == 15)
+    def nothing():
+        pass
 
-    def records():
-        p1, p2 = v("PA", 128, 256), v("PA", 256, 384)
-        scan(v("loc", 1, 129), v("PA", 0, 128), v("zer", 0, 128), 0.0)
-        ts(v("Rm"), v("mB"), v("loc", 128, 129), AL.add, 0.0, AL.max)
-        mm(v("PB", 0, 16), v("LT"), v("Rm"), True, True)
-        tt(p1, v("PA", 0, 128), v("loc", 0, 128), AL.is_gt)
-        tt(v("s3"), p1, v("loc", 1, 129), AL.mult)
-        red(v("car", 0, 1), v("PB", 0, 16), AL.max)
-        ts(p1, v("s3"), v("car", 0, 1), AL.is_le)
-        tt(p2, p1, v("dum"), AL.mult)
-        tt(v("s4"), p2, v("s3"), AL.max)
-        cp(v("lst"), v("s4"))
+    def fold(src, t, part, f1=nothing, f2=nothing):
+        a, b, c, d = [v(src, 512 * rank, 512 * rank + 512)] + [lq(t, q, rank) for q in near + far]
+        r1, r2, r3 = [v("rl", 512 * k, 512 * k + 512) for k in range(3)]
+        if part < 2:
+            bank, x, y, r = (("PS", a, b, r1), ("PT", c, d, r2))[part]
+            mm(v(bank), v("Ib"), x, True, False)
+            mm(v(bank), v("Nb"), y, False, True)
+            act(r, v(bank), AF.Relu)
+            return
+        for k, (m, x) in enumerate((("Ib", b), ("Nb", d), ("Ib", r1), ("Nb", r2))):
+            mm(v("PG"), v(m), x, k == 0, k == 3)
+        f1()
+        act(r3, v("PG"), AF.Relu)
+        terms = [("Rb", d), ("Rb", r2), ("Rb", r3)]
+        if t == RO:
+            terms = [("Ib", x) for x in (a, b, c, d)] + [("Rb", x) for x in (d, r2, r3)]
+        for k, (m, x) in enumerate(terms):
+            mm(v("PF"), v(m), x, k == 0, k == len(terms) - 1)
+        f2()
+        act(mq(t, rank), v("PF"), AF.Identity)
+        send([([cores[q]], eng3[q], ("ak%d" if q in near else "am%d") % t, [mq(t, rank)], [mq(t, rank)], 0) for q in eng3])
+        arrive(mq(t, near[0]), "ak%d" % t, len(e_near))
+        add("-", "arr", None, [], [mq(t, q) for q in far], tok=("am%d" % t, len(e_far)))
 
-    def scat_d(ka):
-        cp(ind(v("tA"), v("lst", 0, ka)), v("val", 0, 16 * ka))
+    def blocks(src, sel, n):
+        mm(v("PA", 0, 128 * n), v("Ib"), v("ob", 0, 128 * n), True, False)
+        for o in range(16):
+            mm(v("PA", o, 128 * n - 15 + o, 16), v(src, o, W - 15 + o, 16), sel, False, o == 15)
 
-    def scat_a(ka):
-        act(ind(v("tB"), v("lst", ka, 128)), v("val", 16 * ka, W), AF.Silu)
+    def turned(n):
+        for k in range(n):
+            mm(v("PF", 128 * k, 128 * k + 128), v("Ts", 128 * k, 128 * k + 128), v("Ih"), True, True)
 
-    def running(between=False):
-        scan(v("inv", 0, 1024), v("tA", 1, 1025), v("tB", 1, 1025), 0.0)
-        if between:
-            slopes(part=1)
-        conv("PC", "EI", "inv", 0, 64)
-        mm(v("PB", 128, 129), v("G0"), v("inv", 1023, 1024), True, True)
-        scan(v("inv", 1024, W), v("tA", 1025, W + 1), v("tB", 1025, W + 1), 0.0)
-        conv("PB", "EI", "inv", 64, 128)
+    def records(win, f1=nothing, f2=nothing, f3=nothing, f4=nothing):
+        r8 = (0, 8, 1)
+        loc = v("loc", 8, 136)
+        mm(v("PC", 0, 128), v("KI"), v("cz"), True, False)
+        mm(v("PG", 0, 128), v("KI"), v("oh"), True, False)
+        scan(loc, v("rst"), v("PA", 0, 128), 0.0, AL.add, AL.max)
+        mm(v("PB", 0, 128, rows=r8), v("loc", 23, 136, 16), v("Ih"), True, True)
+        mm(v("PC", 0, 128), v("KI"), v("loc", 7, 135), False, False)
+        mm(v("PC", 0, 128), v("KN"), loc, False, True)
+        mm(v("PG", 0, 128), v("KN"), loc, False, False)
+        f1()
+        scan(v("Cs", 1, 129, rows=r8), v("PB", 0, 128, rows=r8), v("zer", 0, 128, rows=r8), 0.0)
+        mm(v("PG", 0, 128), v("Cs", 0, 128, rows=r8), v("Sel", rows=r8), False, True)
+        tt(v("s3"), v("PC", 0, 128), loc, AL.max)
+        f2()
+        tt(v("s4"), v("PG", 0, 128), v("s3"), AL.max)
+        scan(v("Q", rev=True), v("Bg", rev=True), v("s4", rev=True), 0.0, AL.max, AL.min)
+        mm(v("PB", 0, 128), v("Q"), v("Ih"), True, True)
+        mm(v("PA", 0, 256), v("Z0"), v("cb"), True, False)
+        f3()
+        cp(v("Kr"), v("PB", 0, 128))
+        ts(v("Kf"), v("PB", 0, 128), 2049.0, AL.is_ge)
+        for k in range(8):
+            mm(v("PC", 0, 16), v("Eo", 14 - 2 * k, 142 - 2 * k), v("Kr", k, 121 + k, 8), k == 0, k == 7)
+        for (mx, kk) in (("mQ", "Kr"), ("mF", "Kf")):
+            for h in range(2):
+                mm(v("PA", h, 255 + h, 2), v(mx, 128 * h, 128 * h + 128), v(kk), False, kk == "Kf" and h == 1)
+        f4()
+        cp(v("l" + win), v("PC", 0, 16))
+        ts(v("val"), v("PA", 0, 256), 0.0, AL.max)
+        cp(ind(v(win), v("l" + win)), v("val"))
+
+    def running(win, f1=nothing):
+        for h in range(2):
+            a, b = (0, 1025) if h == 0 else (1025, W + 1)
+            scan(v("inv", a, b), v("dec", 0, b - a), v(win, a + 1, b + 1), v("mid", 0, 1) if h else 0.0, AL.add, AL.max)
+            if h == 0:
+                cp(v("mid", 0, 1), v("inv", b - 1, b))
+            for o in range(17):
+                em = v("TA", 15, 143) if o == 0 else v("TB", 0, 128) if o == 16 else v("EI", 15 - o, 143 - o)
+                mm(v("PB" if h else "PC", 64 * h, 64 * h + 64), em, v("inv", 1024 * h + o, 1024 * h + o + 1009, 16), o == 0, o == 16)
+            if h == 0:
+                f1()
 
     def inv_half(o, c0, h):
-        if h == 0:
-            cp(v(o, c0, c0 + 64), v("PC", 0, 64))
-        else:
-            ts(v(o, c0 + 64, c0 + 128), v("PB", 64, 128), v("PB", 128, 129), AL.max)
+        cp(v(o, c0 + 64 * h, c0 + 64 * h + 64), v("PB" if h else "PC", 64 * h, 64 * h + 64))
 
-    def wipe(behind=None):
-        r16 = (0, 128, 16)
-        for n in ("tA", "tB"):
-            dma("S", v(n, 0, 2052, rows=r16), v("zer", 0, 2052, rows=r16))
-            if behind is not None:
-                ops[-1]["after"] = [behind]
+    def wipe(win):
+        act(ind(v(win), v("l" + win)), v("zer", 0, 256), AF.Tanh)
 
     def score(k, lname, l0, Ms, cuts):
         for c in range(len(cuts) - 1):
             a, b = cuts[c], cuts[c + 1]
             tt(v("D%d" % k, 16 * a, 16 * b), ind(v("X"), v(lname, l0 + a, l0 + b)), v(Ms[0], Ms[1] + 16 * a, Ms[1] + 16 * b), AL.subtract)
 
+    def acc(c, k, n=1):
+        return v("acc", 16 * rnd[0] + 4 * c + k, 16 * rnd[0] + 4 * c + k + n)
+
     def absum(k, cuts, which, q="A"):
         for c in which:
             d = v("D%d" % k, 16 * cuts[c], 16 * cuts[c + 1])
-            o = v("acc", 4 * c + k, 4 * c + k + 1)
+            o = acc(c, k)
             if q == "A":
                 act(d, d, AF.Abs, acc=o)
             else:
-                add("D", "c", lambda e, o=o, d=d: e.tensor_reduce(o["ap"], d["ap"], AxisListType.X, AL.add,
-                                                                  apply_absolute_value=True), [d], [o])
+                absred(o, d)
 
-    def stay(h, Ms, src="X", k=0):
-        for c in range(2):
-            o = 1024 * h + 512 * c
-            mm(v("PS", 512 * c, 512 * c + 512), v("Ib"), v(src, o, o + 512), True, False)
-            mm(v("PS", 512 * c, 512 * c + 512), v("Nb"), v(Ms[0], Ms[1] + o, Ms[1] + o + 512), False, True)
-        act(v("D0", 1024 * h, 1024 * h + 1024), v("PS"), AF.Abs, acc=v("acc", 4 * h + k, 4 * h + k + 1))
+    def absred(o, d):
+        add("D", "c", lambda e: e.tensor_reduce(o["ap"], d["ap"], AxisListType.X, AL.add, apply_absolute_value=True), [d], [o])
 
-    def slopes_pe(k0=0, k1=128):
-        conv("PG", "EC", "Wc", k0, k1)
-        conv("PF", "EB", "Wc", k0, k1)
+    def stay(c, Ms, src="X", k=0, q="A"):
+        o = 512 * c
+        turn[0] = (turn[0] + 1) % 4
+        bank, a = v(("PS", "PT", "PA", "PG")[turn[0]]), acc(c, k)
+        mm(bank, v("Ib"), v(src, o, o + 512), True, False)
+        mm(bank, v("Nb"), v(Ms[0], Ms[1] + o, Ms[1] + o + 512), False, True)
+        if q == "A":
+            act(v("D0", 512 * turn[0], 512 * turn[0] + 512), bank, AF.Abs, acc=a)
+        else:
+            absred(a, bank)
 
-    def mu_slope():
-        cp(v("muf", 0, 128), v("muu"))
+    def mu_slope(rot=True):
         mm(v("PD", 0, 128), v("U1"), v("muf", 0, 128), True, False)
         mm(v("PD", 0, 128), v("U2"), v("muf", 1, 129), False, True)
+        if rot:
+            mm(v("PD", 128, 256), v("Rot"), v("muf", 0, 128), True, True)
 
-    def slopes(k0=0, k1=128, part=None):
+    def slopes(k0=0, k1=128, part=None, src=("PG", 0)):
         if part != 1:
-            act(v("a1", k0, k1), v("PG", k0, k1), AF.Abs)
+            act(v("a1", k0, k1), v(src[0], src[1] + k0, src[1] + k1), AF.Abs)
             act(v("a3", k0, k1), v("a1", k0, k1), AF.Relu, bias=4.0, scale=-1.0)
             mm(v("PS", k0, k1), v("Ib"), v("cap", k0, k1), True, False)
             mm(v("PS", k0, k1), v("Nb"), v("a2", k0, k1), False, False)
             mm(v("PS", k0, k1), v("N5"), v("a3", k0, k1), False, True)
         if part != 0:
             cp(v("ixu", k0, k1), v("PS", k0, k1))
-            if part is None:
-                cp(v("du", k0, k1), v("PF", k0, k1))
 
     def mu_cap():
         act(v("a2"), v("PD", 0, 128), AF.Relu, bias=4.0, scale=-1.0)
@@ -401,71 +429,113 @@ def rank_program(g, core, T, topo):
     iota(v("pi", 0, 2), [[112, 2]], 0, 1)
     iota(v("iom"), [[1, 144]], 0, 0)
     iota(v("iog"), [[16, 8], [0, 16]], 0, 0)
+    iota(v("io8"), [[16, 8], [0, 2], [1, 8]], 0, 0)
+    iota(v("iod"), [[1, 8], [1, 2]], 0, 0)
     dma("S", v("e32"), ext(T.ew[:]))
     dma("S", v("rh", 0, 5), ext(T.rho[:]))
-    ms(v("zer", 0, 128), 0.0)
-    ms(v("ob"), 1.0)
-    ms(v("loc"), 0.0)
-    ms(v("acc"), 0.0)
-    ts(v("pj", 0, 1), v("pi", 0, 1), 15, AL.bitwise_and)
-    ts(v("pj", 1, 3), v("pi", 0, 2), 112, AL.bitwise_and)
-    ts(v("pj", 3, 5), v("pi", 0, 2), 127, AL.bitwise_and)
-    cp(v("pf", 0, 5), v("pj", 0, 5))
-    pm, gb, gbp, pp, ppm = [v("pf", k, k + 1) for k in range(5)]
+    send([([cores[prev]], e_prev, "ag", [v("g32")], [v("gn32")], 0)])
+    arrive(v("gn32"), "ag", n_next)
+    quarters("X", 0)
+    ms(v("oh"), 1.0)
+    for (c, b, m) in [(0, 1, 15), (1, 2, 112), (3, 2, 127), (5, 1, 7)]:
+        ts(v("pj", c, c + b), v("pi", 0, b), m, AL.bitwise_and)
+    ms(v("rst"), 0.0)
+    cp(v("pf", 0, 6), v("pj", 0, 6))
+    ms(v("Bg"), 0.0)
+    pm, gb, gbp, pp, ppm, p8 = [v("pf", k, k + 1) for k in range(6)]
     lo, hi = v("pf", 8, 9), v("pf", 12, 13)
+    gii, i0, c1, c2, eo, p4, p16 = [v("pg", k, k + 1) for k in range(7)]
+    z0, wa, wb, wd = v("wr", 5, 6), v("ab", 0, 1), v("ab", 1, 2), v("ab", 2, 3)
     ts(lo, pm, 8.0, AL.is_ge)
     ts(hi, pm, 8.0, AL.is_lt)
+    ms(v("rst", 0, 113, 16), -4096.0)
     ts(v("ib"), v("iom", 0, 16), lo, AL.mult)
+    ts(z0, pm, 0.0, AL.is_equal)
     grp[0] = 1
-    act(v("val", 15, W, 16), v("iom", 0, 128), AF.Silu, bias=1920.0)
     for i in range(16):
         act(v("IW", i, W - 15 + i, 16), v("iom", 0, 128), AF.Identity, bias=v("ib", i, i + 1), scale=hi)
-    for i in range(15):
-        act(v("val", i, W - 15 + i, 16), v("iom", 0, 128), AF.Identity, bias=float(128 * i))
     grp[0] = 0
-    cp(v("gu"), v("g32"))
-    quarters("X", 0)
-    send([([cores[prev]], e_prev, "ag", [v("gu")], [v("gn")], 0)])
-    arrive(v("gn"), "ag", n_next)
-    fold("X", 0)
     ms(v("tA", 0, 2052), 0.0)
-    act(v("tB", 0, 2052), v("tA", 0, 2052), AF.Identity)
-    dma("S", v("zer", 128, 2052, rows=(0, 128, 16)), v("tA", 128, 2052, rows=(0, 128, 16)))
-    ts(v("wr", 0, 4), v("iom", 0, 4), pm, AL.is_equal, 16.0, AL.mult)
-    ts(v("wr", 4, 8), v("iom", 8, 12), pm, AL.is_equal)
-    ts(v("E"), v("iom"), -15.0, AL.add, gbp, AL.is_equal)
-    ts(v("Ib"), v("iom", 0, 128), pp, AL.is_equal)
-    tt(v("wr", 0, 4), v("wr", 0, 4), v("wr", 4, 8), AL.add)
-    tt(v("wr", 4, 5), v("wr", 2, 3), v("wr", 1, 2), AL.subtract)
-    ts(v("EN"), v("E"), v("wr", 3, 4), AL.mult)
-    ts(v("mB"), v("iom", 0, 16), pm, AL.not_equal, -4096.0, AL.mult)
-    ts(v("GM"), v("iog"), gb, AL.is_equal)
-    ts(v("s1"), v("iom", 0, 128), pp, AL.is_gt)
-    ts(v("l0"), v("iom", 0, 128), 16.0, AL.mult, pm, AL.add)
-    ts(v("wr", 5, 6), pm, 0.0, AL.is_equal)
-    ts(v("E"), v("iom"), -15.0, AL.add, gb, AL.is_equal)
-    tt(v("LT"), v("s1"), v("GM"), AL.mult)
-    ts(v("dum"), v("l0"), 2049.0, AL.add)
-    ts(v("wr", 6, 7), pm, 0.0, AL.not_equal)
-    ts(v("EI"), v("E"), v("wr", 5, 6), AL.mult)
-    ts(v("Ih"), v("iom", 0, 128), pp, AL.is_equal)
-    ts(v("Nb"), v("Ib"), -1.0, AL.mult)
+    ts(wd, lo, -KK, AL.mult, z0, AL.add)
+    ts(p16, pp, 16.0, AL.mult)
+    ts(wd, wd, hi, AL.subtract)
+    act(v("zer", 0, 1040), v("tA", 0, 1040), AF.Identity)
+    act(v("dec"), v("zer", 0, 1040), AF.Identity, bias=wd)
+    cp(v("gu"), v("g32"))
     cp(v("eu"), v("e32"))
-    ts(v("G0"), v("GM"), v("wr", 5, 6), AL.mult)
-    ts(v("EA"), v("E"), v("wr", 0, 1), AL.mult)
-    ts(v("tie"), v("iom", 0, 4), 4.0, AL.add, 1.0 / 64, AL.mult)
-    gat4("W0", v("IW"), "gn")
-    cp(v("eh"), v("e32"))
+    gat("A", v("Wc"), v("IW"), v("gu"))
     gat("A", v("D1"), v("X"), v("eu", 0, 128))
+    ts(v("Ih"), v("iom", 0, 128), pp, AL.is_equal)
+    ts(v("KI"), v("iom", 0, 128), pp, AL.is_equal, KK, AL.mult)
+    ts(v("Rot"), v("iom", 0, 128), ppm, AL.is_equal)
+    ts(v("KN"), v("iom", 0, 128), pp, AL.is_equal, -KK, AL.mult)
+    ts(v("cz"), v("rst"), 0.5, AL.add)
+    ms(v("loc", 0, 8), 0.0)
+    ms(v("Cs", 0, 8), 0.0)
+    ts(p4, pp, 4.0, AL.mult, 2066.0, AL.add)
+    ts(i0, p8, 0.0, AL.is_equal)
+    ts(gii, gb, p8, AL.add)
+    ts(v("Sel"), v("iog"), p16, AL.is_equal, KK, AL.mult)
+    ts(v("Bg", 7, 128, 8), v("iod"), -2.0, AL.mult, p4, AL.add)
+    ts(c2, i0, -1.0, AL.add)
+    ts(eo, gb, lo, AL.add)
+    ts(v("s3"), v("io8"), gii, AL.is_equal)
+    ts(v("s4"), v("iog"), gb, AL.is_equal, i0, AL.mult)
+    ts(c1, c2, KK, AL.mult)
+    ts(v("E"), v("iom"), -14.0, AL.add, eo, AL.is_equal)
+    tt(v("s4"), v("s3"), v("s4"), AL.subtract)
+    ts(v("s1"), v("iom", 0, 128), gb, AL.is_equal, c2, AL.mult)
+    ts(v("s3"), v("s3"), c1, AL.mult)
+    ts(v("Eo"), v("E"), i0, AL.mult)
+    ts(v("Z0"), v("iom", 0, 128), pp, AL.is_equal, z0, AL.mult)
+    tt(v("s3"), v("s3"), v("s1"), AL.add)
+    for (mx, base) in (("mQ", "s4"), ("mF", "s3")):
+        for h in range(2):
+            ts(v(mx, 128 * h, 128 * h + 128), v(base), lo if h else hi, AL.mult)
+    for h in range(2):
+        ts(v("cb", 128 * h, 128 * h + 128), v("iom", 0, 128), 8.0, AL.mult, 7.0 + 1024 * h, AL.add)
+    ts(wa, z0, 2.0, AL.mult, hi, AL.subtract)
+    ts(wb, pm, 9.0, AL.is_ge, z0, AL.add)
+    ts(v("E"), v("iom"), -15.0, AL.add, gb, AL.is_equal)
+    ts(wb, wb, -1.0, AL.mult, hi, AL.add)
+    ts(v("TA"), v("E"), wa, AL.mult)
+    ts(v("TB"), v("E"), wb, AL.mult)
+    cp(v("gnh"), v("gn32"))
+
+    def mid_constants():
+        tt(v("EI", 0, 143), v("TA", 0, 143), v("TB", 1, 144), AL.add)
+        ts(v("Ib"), v("iom", 0, 128), pp, AL.is_equal)
+        ts(v("Nb"), v("iom", 0, 128), pp, AL.is_equal, -1.0, AL.mult)
+        cp(v("Rb"), v("Rot"))
+
+    def sum_constants():
+        ms(v("acc"), 0.0)
+        ts(v("GM"), v("iog"), gb, AL.is_equal)
+        ts(v("tie"), v("iom", 0, 4), 4.0, AL.add, 1.0 / 64, AL.mult)
+
+    def mid_constants2():
+        ts(v("l0"), v("iom", 0, 128), 16.0, AL.mult, pm, AL.add)
+        cp(v("eh"), v("e32"))
+        ms(v("ob", 0, 128), 1.0)
+        ms(v("ob", 128, 384), 0.0)
+        ts(v("wr", 0, 4), v("iom", 0, 4), pm, AL.is_equal, 16.0, AL.mult)
+        ts(v("ab", 4, 8), v("iom", 8, 12), pm, AL.is_equal)
+        ts(v("wr", 6, 7), pm, 0.0, AL.not_equal)
+        tt(v("wr", 0, 4), v("wr", 0, 4), v("ab", 4, 8), AL.add)
+        tt(v("wr", 4, 5), v("wr", 2, 3), v("wr", 1, 2), AL.subtract)
+        ts(v("S3", 24, 32), v("E", 15, 128, 16), v("wr", 0, 1), AL.mult)
 
     def late_constants():
+        ts(v("s3", 0, 8), v("iog", 0, 113, 16), gbp, AL.is_equal)
+        ts(v("EA"), v("E"), v("wr", 0, 1), AL.mult)
         ts(v("EB"), v("E"), v("wr", 1, 2), AL.mult)
         ts(v("EC"), v("E"), v("wr", 4, 5), AL.mult)
+        ts(v("S3", 0, 8), v("s3", 0, 8), v("wr", 3, 4), AL.mult)
+        cp(v("S3", 8, 16), v("EB", 15, 128, 16))
+        cp(v("S3", 16, 24), v("EC", 15, 128, 16))
         ts(v("U2"), v("E", 0, 128), v("wr", 5, 6), AL.mult)
         ts(v("Iq"), v("Ih"), 0.25, AL.mult)
-        ts(v("Pq"), v("iom", 0, 128), ppm, AL.is_equal, 0.25, AL.mult)
         ts(v("a1"), v("iom", 1, 129), pp, AL.is_equal, v("wr", 6, 7), AL.mult)
-        act(v("p4"), v("pb"), AF.Identity, scale=0.25)
         ms(v("cap"), 24.0)
         ts(v("N5"), v("Ib"), -5.0, AL.mult)
         ms(v("tab"), 0.0)
@@ -478,67 +548,83 @@ def rank_program(g, core, T, topo):
         ts(v("tab", 0, 25), v("tab", 32, 57), 32.0, AL.mult)
         ts(v("tab", 64, 89), v("tab", 32, 57), 1.0 / 128, AL.mult)
 
-    H2, C3 = [0, 64, 128], [0, 56, 104, 128]
+    H2, C3, Q4 = [0, 64, 128], [0, 56, 104, 128], [0, 32, 64, 96, 128]
     for t in range(RO):
         last = t == RO - 1
+        rnd[0] = t
         Ms = ("Ms", 0) if t else ("Mp", 0)
-        src = "W0" if t == 0 else "Wc"
-        ka = KA1 if t else KA0
+        Mu = "Mu%d" % (t % 2)
+        def xq(q, k0, k1):
+            gat(q, v("X", 16 * k0, 16 * k1), v("Xp"), v("muu", k0, k1))
+
+        def lists2():
+            ts(v("l2u"), v("PF", 0, 128), -1.0, AL.add)
+            ts(v("l2h"), v("PF", 0, 128), -1.0, AL.add)
+
         if t > 0:
-            gat4("Wc", v("Wm", 0, W), "muu")
-            ts(v("msu"), v("PG", 0, 128), -0.375, AL.add)
-            gat("A", v("X"), v("Xp"), v("muu"))
-        blocks("EN", src)
-        if t > 0:
-            mu_slope()
-        records()
-        conv("PF", "EN", src)
-        if t > 0:
-            gat("A", v(Ms[0]), v("Mp", W * t, W * t + W), v("msu"))
-            conv("PG", "EC", "Wc")
-        scat_d(ka)
-        scat_a(ka)
-        cp(v("l2u"), v("PF", 0, 128))
-        cp(v("l2h"), v("PF", 0, 128))
-        if t == 0:
-            gat("A", v("Wc"), v("IW"), v("gu"))
-            running()
+            blocks("Wc", v("S3", 0, 24), 3)
+            cp(v("muf", 0, 128), v("muu"))
+            xq("D", 128 - XD, 128)
+            xq("A", 0, 128 - XD)
+            records("tA", f1=lambda: cp(v("Ts"), v("PA", 0, 384)), f2=lambda: (turned(3), mu_slope()), f3=lists2,
+                    f4=lambda: (cp(v("msu"), v("PD", 128, 256)), cp(v("du"), v("PF", 128, 256))))
+            gat("A", v("D1"), v("X"), v("eu", 128 * t, 128 * t + 128))
+            for h in range(2):
+                gat("A", v("Ms", 1024 * h, 1024 * h + 1024), v("Mp", W * t, W * t + W), v("msu", 64 * h, 64 * h + 64))
+            dma("S", v(Mu, rows=(16, 128, 1)), v("Ms", rows=(0, 112, 1)))
+            dma("S", v(Mu, rows=(0, 16, 1)), v("Ms", rows=(112, 128, 1)))
+            running("tA", lambda: (stay(0, Ms), stay(1, Ms)))
+            for c in range(2, 4):
+                stay(c, Ms)
+        else:
+            mm(v("PA", 0, 128), v("Ih"), v("oh"), True, False)
+            mm(v("PA", 0, 128), v("gnh"), v("Rot"), False, True)
+            mm(v("PF", 0, 128), v("Ih"), v("oh"), True, False)
+            mm(v("PF", 0, 128), v("Rot"), v("gnh"), False, True)
+            records("tA", f1=mid_constants, f2=lambda: fold("X", 0, 0), f3=lambda: (lists2(), fold("X", 0, 1)),
+                    f4=sum_constants)
+            fold("X", 0, 2)
+            gat("A", v("D2"), v("X"), v("l2u"))
+            running("tA")
             dma("S", v("pb"), ext(T.pay[:]))
-        else:
-            conv("PF", "EB", "Wc")
-            dma("S", v("Mu", rows=(16, 128, 1)), v(Ms[0], rows=(0, 112, 1)))
-            dma("S", v("Mu", rows=(0, 16, 1)), v(Ms[0], rows=(112, 128, 1)))
+            ops[-1]["after"] = [len(ops) - 2]
         dma("S", v("Wc", rows=(1, 128, 8)), v("IW", rows=(1, 128, 8)))
-        if t > 0:
-            score(1, "eu", 128 * t, Ms, H2)
-            score(2, "l2u", 0, Ms, H2)
-            stay(0, Ms)
-            absum(1, H2, [0])
-            stay(1, Ms)
-            absum(1, H2, [1])
-            absum(2, H2, [0, 1])
-        else:
-            score(2, "l2u", 0, Ms, H2)
-            stay(0, Ms)
-            absum(2, H2, [0])
-            stay(1, Ms)
-            absum(2, H2, [1])
-            stay(0, Ms, "D1", 1)
-            stay(1, Ms, "D1", 1)
-        if t > 0:
-            running()
-        wipe()
         inv_half("l3u", 0, 0)
-        inv_half("l3h", 0, 0)
-        score(3, "l3u", 0, Ms, C3[:2])
+        if t > 0:
+            inv_half("l3h", 0, 0)
+            score(3, "l3u", 0, Ms, H2[:2])
         inv_half("l3u", 0, 1)
-        inv_half("l3h", 0, 1)
-        mm(v("PB", 0, 4), v("GM"), v("tie"), True, False)
-        score(3, "l3u", 0, Ms, C3[1:])
-        absum(3, C3, [0, 1] if t else [0])
-        absum(3, C3, [2] if t else [2, 1], "D")
-        for c in (0, 2, 1):
-            mm(v("PB", 0, 4), v("GM"), v("acc", 4 * c, 4 * c + 4), False, c == 1)
+        if t > 0:
+            inv_half("l3h", 0, 1)
+            score(3, "l3u", 0, Ms, H2[1:])
+            for c in range(4):
+                stay(c, Ms, "D1", 1)
+            mm(v("PB", 0, 4), v("GM"), v("tie"), True, False)
+            score(2, "l2u", 0, Ms, C3)
+            absum(3, H2, [0, 1])
+            absum(2, C3, [2, 1], "D")
+            absum(2, C3, [0], "D" if AD else "A")
+        else:
+            inv_half("l3h", 0, 0)
+            inv_half("l3h", 0, 1)
+            mm(v("PB", 0, 4), v("GM"), v("tie"), True, False)
+            for c in [rank] + near + far:
+                score(3, "l3u", 0, Ms, Q4[c:c + 2])
+                if c == far[0]:
+                    dma("S", v("tB", 0, 1026), v("zer", 0, 1026))
+                    ops[-1]["after"] = [len(ops) - 2]
+                    dma("S", v("tB", 1026, 2052), v("zer", 0, 1026))
+                for (src, k) in (("X", 0), ("D1", 1), ("D2", 2)):
+                    stay(c, Ms, src, k, "D" if k == 2 and c in far else "A")
+                absum(3, Q4, [c], "D")
+                if c == near[0]:
+                    mid_constants2()
+        sums = (3, 2, 1, 0) if t else [rank] + near + far
+        for c in sums:
+            mm(v("PB", 0, 4), v("GM"), acc(c, 0, 4), False, c == sums[3])
+        if t > 0:
+            mu_cap()
+            slopes(part=0, src=("PF", 256))
         red(v("mn", 0, 1), v("PB", 0, 4), AL.min)
         for k in range(4):
             ts(v("dg", 128 * k, 128 * k + 128), v("Ih"), v("PB", k, k + 1), AL.mult, v("mn", 0, 1), AL.is_equal)
@@ -548,109 +634,119 @@ def rank_program(g, core, T, topo):
         gat4("Wm", v("Wc"), "cu")
         if not last:
             dma("S", dr("st", T.st[t], t), v("Wm", 0, W, rows=(0, 128, 8)))
-        blocks("EA", "Wm")
+        blocks("Wm", v("S3", 24, 32), 1)
         if t > 0:
-            cp(v("du"), v("PF", 0, 128))
+            slopes(part=1)
         k0 = 32 * far[0]
         gat("A", v("Xp", 16 * k0, 16 * k0 + 1024), v("X"), v("cu", k0, k0 + 64))
         act(v("Wm", W, W + 1), v("Wm", W - 1, W), AF.Identity, bias=lo)
-        gat("A", v("Xp", 512 * near[0], 512 * near[0] + 512), v("X"), v("cu", 32 * near[0], 32 * near[0] + 32))
+        for q in (near[0], rank):
+            gat("A", v("Xp", 512 * q, 512 * q + 512), v("X"), v("cu", 32 * q, 32 * q + 32))
         quarters("Xp", t + 1)
-        records()
-        if t > 0:
-            mu_cap()
-            slopes(part=0)
+        records("tB")
         dma("S", v("Wm", 0, W, rows=(2, 128, 8)), v("Wm", 1, W + 1, rows=(1, 128, 8)))
         if not last:
             send([([cores[prev]], e_prev, "an%d" % t, [dr("st", T.st[t], t)], [dr("ld", T.ld[t], t)], 0)])
             arrive(dr("ld", T.ld[t], t), "an%d" % t, n_next)
             dma("S", v("Wm", 0, W, rows=(3, 128, 8)), dr("ld", T.ld[t], t))
-        scat_d(KA2)
-        scat_a(KA2)
-        if not last:
-            gat("A", v("Xp", 512 * rank, 512 * rank + 512), v("X"), v("cu", 32 * rank, 32 * rank + 32))
-            fold("Xp", t + 1)
         if t > 0:
-            slopes(part=1)
             for h in range(2):
                 gat("A", v("R", 1024 * h, 1024 * h + 1024), v("tab", 0 if t == 1 else 32, 32 if t == 1 else 64),
                     v("ixu", 64 * h, 64 * h + 64))
         if last:
-            gat("A", v("Xp", 512 * rank, 512 * rank + 512), v("X"), v("cu", 32 * rank, 32 * rank + 32))
-        running()
-        iv = v("ivh", 128 * t, 128 * t + 128)
-        inv_half("ivh", 128 * t, 0)
-        inv_half("ivh", 128 * t, 1)
-        send([([cores[q]], eng3[q], "ai%d" % t, [iv],
-               [v("li", 384 * t + 128 * slot(rank, q), 384 * t + 128 * slot(rank, q) + 128)], 0) for q in eng3])
+            ts(v("Rb"), v("Ib"), 2.0, AL.mult)
+        if t == 0:
+            act(v("p4"), v("pb"), AF.Identity, scale=0.25)
+        fold("Xp", t + 1, 0)
         if not last:
-            wipe(len(ops) - 1)
-        arrive(v("li", 384 * t, 384 * t + 384), "ai%d" % t, n3)
-        if last:
-            fold("Xp", t + 1)
+            wipe("tA")
+        running("tB", lambda: fold("Xp", t + 1, 1))
+        def li(h, s):
+            c = 384 * t + 192 * h + 64 * s
+            return v("li", c, c + 64)
+
+        vo = "V%d" % (t % 2)
+        vi = v("pb") if t == 1 else v("V%d" % ((t + 1) % 2))
+        iv = [v("ivh", 128 * t + 64 * h, 128 * t + 64 * h + 64) for h in range(2)]
+        for h in range(2):
+            inv_half("ivh", 128 * t, h)
+            send([([cores[q]], eng3[q], "ai%d" % (2 * t + h), [iv[h]], [li(h, slot(rank, q))], 0) for q in eng3])
+            add("-", "arr", None, [], [li(h, s) for s in range(3)], tok=("ai%d" % (2 * t + h), n3))
+            if t > 0:
+                for a, b in [(0, 512)] if h == 0 else [(512, 1024), (1024, W)]:
+                    tt(v(vo, a, b), ind(vi, v("du", a // 16, b // 16)), v("R", a, b), AL.mult)
+                    if last and a:
+                        dma("G", v(vo, b - 1024, b), v(Mu, b - 1024, b), acc=True)
         if t == 0:
             late_constants()
-        if t > 0:
-            vo = "V%d" % (t % 2)
-            vi = v("pb") if t == 1 else v("V%d" % ((t + 1) % 2))
-            for a, b in [(0, 1024), (1024, W)]:
-                tt(v(vo, a, b), ind(vi, v("du", a // 16, b // 16)), v("R", a, b), AL.mult)
-                if not last:
-                    if a == 0:
-                        continue
-                    a = 0
-                dma("G", v(vo, a, b), v("Mu", a, b), acc=True)
-        parts = [iv] + [v("li", 384 * t + 128 * k, 384 * t + 128 * k + 128) for k in range(3)]
-        for k in range(4):
-            mm(v("PD", 0, 128), v("Iq"), parts[k], k == 0, k == 3)
-        ts(v("muu"), v("PD", 0, 128), -0.375, AL.add)
         if not last:
-            for k in range(4):
-                mm(v("PG", 0, 128), v("Pq"), parts[k], k == 0, k == 3)
+            wipe("tB")
+        fold("Xp", t + 1, 2)
+        if t > 0 and not last:
+            dma("G", v(vo), v(Mu), acc=True)
+        for h in range(2):
+            bank = v("PC" if h else "PD", 0, 64)
+            for k, x in enumerate([iv[h]] + [li(h, s) for s in range(3)]):
+                mm(bank, v("Iq"), x, k == 0, k == 3)
+            ts(v("muu", 64 * h, 64 * h + 64), bank, -0.375, AL.add)
+            for k, e in enumerate("DA"):
+                q = 2 * h + k
+                gat(e, v("Wc", 512 * q, 512 * q + 512), v("Wm", 0, W), v("muu", 32 * q, 32 * q + 32))
 
     far.sort(key=lambda q: topo.die(cores[q]) != topo.die(core))
     order = far + near + [rank]
-    mu_slope()
-    gat4("Wc", v("Wm", 0, W), "muu", (order[0], order[2]), (order[1], order[3]))
+    cp(v("muf", 0, 128), v("muu"))
+    mu_slope(False)
 
     def lists(hh):
         k0 = 32 * min(order[2 * hh:2 * hh + 2])
-        pe, pd = ("PC", "PA") if hh else ("PB", "PF")
         conv("PG", "EC", "Wc", k0, k0 + 64)
-        conv(pd, "EB", "Wc", k0, k0 + 64)
+        conv("PA" if hh else "PF", "EB", "Wc", k0, k0 + 64)
         slopes(k0, k0 + 64, 0)
-        conv(pe, "EA", "Wc", k0, k0 + 64)
-        cp(v("du", k0, k0 + 64), v(pd, k0, k0 + 64))
+        conv("PC" if hh else "PT", "EA", "Wc", k0, k0 + 64)
+
+    def lists_out(hh):
+        k0 = 32 * min(order[2 * hh:2 * hh + 2])
+        cp(v("du", k0, k0 + 64), v("PA" if hh else "PF", k0, k0 + 64))
         slopes(k0, k0 + 64, 1)
-        cp(v("gpu", k0, k0 + 64), v(pe, k0, k0 + 64))
+        cp(v("gpu", k0, k0 + 64), v("PC" if hh else "PT", k0, k0 + 64))
+
+    def part(name, q):
+        return v(name, 512 * q, 512 * q + 512)
 
     mu_cap()
     lists(0)
+    lists_out(0)
     for k, q in enumerate(order):
-        cs = (512 * q, 512 * q + 512)
-        gat("A", v("R", *cs), v("tab", 64, 96), v("ixu", 32 * q, 32 * q + 32))
-        tt(v("V0", *cs), ind(v("V1"), v("du", 32 * q, 32 * q + 32)), v("R", *cs), AL.mult)
-        s = slot(rank, q)
-        if k < 2:
-            tt(v("Tg", *cs), ind(v("p4"), v("gpu", 32 * q, 32 * q + 32)), v("V0", *cs), AL.add)
-            send([([cores[q]], e_far, "af%d" % s, [v("Tg", *cs)], [v("lf", 512 * s, 512 * s + 512)], 0)])
-        else:
-            gat("A", v("Tg", *cs), v("p4"), v("gpu", 32 * q, 32 * q + 32))
+        gat("A", part("R", q), v("tab", 64, 96), v("ixu", 32 * q, 32 * q + 32))
         if k == 0:
             lists(1)
+        tt(part("V0", q), ind(v("V1"), v("du", 32 * q, 32 * q + 32)), part("R", q), AL.mult)
+        s = slot(rank, q)
+        if k < 2:
+            tt(part("Tg", k), ind(v("p4"), v("gpu", 32 * q, 32 * q + 32)), part("V0", q), AL.add)
+            send([([cores[q]], e_far, "af%d" % s, [part("Tg", k)], [part("lf", s)], 0)])
+        if k == 0:
+            lists_out(1)
+        if k == 1:
+            for x in order[2:]:
+                gat("A", part("D1", x), v("p4"), v("gpu", 32 * x, 32 * x + 32))
+            send([([cores[near[0]]], e_near, "ap", [part("D1", near[0])], [part("D2", 0)], 0)])
         if k == 2:
-            send([([cores[q]], e_near, "af%d" % s, [v("V0", *cs), v("Tg", *cs)], [v("lf", 512 * s, 512 * s + 512)], 1)])
-    cs = (512 * rank, 512 * rank + 512)
-    gat("A", v("Mg"), v("Mp", 4 * W, 5 * W), v("muu", 32 * rank, 32 * rank + 32), scale=1.0 / 32)
-    gat("A", v("Sg"), v("Mp", 5 * W, 6 * W), v("muu", 32 * rank, 32 * rank + 32), scale=1.0 / 64)
+            send([([cores[q]], e_near, "af%d" % s, [part("V0", q)], [part("lf", s)], 0)])
+    gat("A", v("Mg"), v("Mp", 4 * W, 5 * W), v("muu", 32 * rank, 32 * rank + 32), scale=1.0 / 64)
+    arrive(part("D2", 0), "ap", len(e_near))
     for s in range(3):
-        arrive(v("lf", 512 * s, 512 * s + 512), "af%d" % s, len(e_near) if (rank + s + 1) % 4 in near else len(e_far))
-    tt(v("PA"), v("V0", *cs), v("Tg", *cs), AL.add)
-    so = [slot(q, rank) for q in order[:3]]
-    tt(v("PA"), v("PA"), v("lf", 512 * so[0], 512 * so[0] + 512), AL.add)
-    tt(v("PA"), v("PA"), v("Mg"), AL.add)
-    tt(v("PA"), v("PA"), v("Sg"), AL.add)
-    tt(v("PA"), v("PA"), v("lf", 512 * so[1], 512 * so[1] + 512), AL.add)
-    tt(v("yo"), v("PA"), v("lf", 512 * so[2], 512 * so[2] + 512), AL.add)
-    dma("S", ext(T.y[:]), v("yo"))
+        arrive(part("lf", s), "af%d" % s, len(e_near) if (rank + s + 1) % 4 in near else len(e_far))
+    terms = [part("D1", rank), part("D2", 0), v("Mg")]
+    for k, x in enumerate(terms):
+        mm(v("PB"), v("Ib"), x, k == 0, k == len(terms) - 1)
+    tt(v("PB"), v("PB"), part("V0", rank), AL.add)
+    for q in (order[0], order[2]):
+        tt(v("PB"), v("PB"), part("lf", slot(q, rank)), AL.add)
+    s = slot(order[1], rank)
+    for h in range(2):
+        a, b = 256 * h, 256 * h + 256
+        tt(v("yo", a, b), v("PB", a, b), v("lf", 512 * s + a, 512 * s + b), AL.add)
+        dma("A" if h else "S", ext(T.y[:, a:b]), v("yo", a, b))
     emit(g, T, ops)

@@ -4,8 +4,16 @@ from concourse.mybir import dt, AluOpType, AxisListType, ActivationFunctionType
 W = 2048
 RO = 4
 TW = 2576
-XD = 16
-AD = False
+XD = 40
+SE = 3
+FS = False
+ZD = 1
+FM = True
+DD = 64
+DE = 32
+MD = 0
+AE = True
+C3 = [0, 56, 96, 128]
 KK = 8192.0
 F, B, H, I32, U = "float32", "bfloat16", "float16", "int32", "uint16"
 
@@ -18,17 +26,17 @@ SCRATCH = {
     "X": _sb(W, B), "Xp": _sb(W, B), "Ms": _sb(W, B), "Mu0": _sb(W, B), "Mu1": _sb(W, B), "Mp": _sb(5 * W, B),
     "lq": _sb(5 * 3 * 512, B), "Wm": _sb(W + 16, B), "Wc": _sb(W, B), "IW": _sb(W, B),
     "D0": _sb(W, B), "D1": _sb(W, B), "D2": _sb(W, B), "D3": _sb(W, B),
-    "tA": _sb(TW, F), "tB": _sb(TW, F), "zer": _sb(1040, F), "val": _sb(256, F), "inv": _sb(W + 16, H), "dec": _sb(1040, B),
+    "tA": _sb(TW, F), "tB": _sb(TW, F), "zer": _sb(1040, F), "val": _sb(256, F), "inv": _sb(W + 16, H), "dec": _sb(2064, B),
     "rst": _sb(128, H), "cz": _sb(128, H), "Bg": _sb(128, H), "KI": _sb(128, H), "KN": _sb(128, H), "Cs": _sb(136, H),
     "Sel": _sb(128, H), "Q": _sb(128, H), "Kr": _sb(128, H), "Kf": _sb(128, H), "Z0": _sb(128, H), "cb": _sb(256, H),
     "Eo": _sb(144, H), "mQ": _sb(256, H), "mF": _sb(256, H), "TA": _sb(144, H), "TB": _sb(144, H),
-    "Rot": _sb(128, H), "io8": _sb(128, F), "iod": _sb(16, F), "Ts": _sb(384, H), "S3": _sb(32, B), "gn32": _sb(128, I32), "gnh": _sb(128, H), "oh": _sb(128, H),
+    "Rot": _sb(128, H), "io8": _sb(128, F), "iod": _sb(16, F), "Ts": _sb(256, H), "Pq": _sb(128, H), "S3": _sb(56, B), "I3": _sb(128, B), "gn32": _sb(128, I32), "gnh": _sb(128, H), "oh": _sb(128, H),
     "pg": _sb(16, F), "ab": _sb(8, F),
     "V0": _sb(W, F), "V1": _sb(W, F), "R": _sb(W, F),
-    "pb": _sb(W, B), "p4": _sb(W, B), "Tg": _sb(1024, F), "EA": _sb(144, B), "e32": _sb(512, I32), "eu": _sb(512, U), "eh": _sb(512, H),
+    "pb": _sb(W, B), "p4": _sb(W, B), "Tg": _sb(1024, F), "e32": _sb(512, I32), "eu": _sb(512, U), "eh": _sb(512, H),
     "g32": _sb(128, I32), "gu": _sb(128, U), "rh": _sb(8, F), "tab": _sb(128, F),
     "pi": _sb(8, I32), "pj": _sb(8, I32), "pf": _sb(16, F), "iom": _sb(144, F), "iog": _sb(128, F), "ib": _sb(16, F),
-    "E": _sb(144, F), "EB": _sb(144, B), "EC": _sb(144, B), "EI": _sb(144, H),
+    "E": _sb(144, F), "EI": _sb(144, H),
     "Ih": _sb(128, H), "Iq": _sb(128, H), "Ib": _sb(128, B), "Nb": _sb(128, B), "ob": _sb(384, B),
     "GM": _sb(128, F), "U1": _sb(128, H), "U2": _sb(128, H),
     "cap": _sb(128, B), "N5": _sb(128, B), "tie": _sb(4, F), "l0": _sb(128, H), "wr": _sb(8, F),
@@ -43,9 +51,9 @@ SCRATCH = {
     "PD": ("psum", [128, 512], F), "PG": ("psum", [128, 512], F), "PF": ("psum", [128, 512], F),
     "PS": ("psum", [128, 512], F), "PT": ("psum", [128, 512], F),
 }
-ARR = (["ag", "ap"] + ["aq%d" % t for t in range(5)] + ["ah%d" % t for t in range(5)] + ["ak%d" % t for t in range(5)] + ["am%d" % t for t in range(5)]
-       + ["ai%d" % t for t in range(2 * RO)] + ["an%d" % t for t in range(3)] + ["af%d" % t for t in range(3)])
-SEMAPHORES = ["cD", "cA", "cP", "cG"] + ARR + ["s%d" % k for k in range(80)]
+ARR = (["ag", "ap"] + ["aq%d" % t for t in range(5)] + ["ah%d" % t for t in range(5)] + ["ak0", "ak1"] + ["ar%d" % t for t in range(5)] + ["am%d" % t for t in range(5)]
+       + ["ai%d" % t for t in range(2 * RO)] + ["an%d" % t for t in range(3)] + ["af%d" % t for t in range(5)])
+SEMAPHORES = ["cD", "cA", "cP", "cG"] + ARR + ["s%d" % k for k in range(96)]
 ESZ = {F: 4, B: 2, H: 2, I32: 4, U: 2}
 AL = AluOpType
 AF = ActivationFunctionType
@@ -263,6 +271,7 @@ def rank_program(g, core, T, topo):
     chipmates = topo.cores_of(core)
     near = [q for q in range(4) if q != rank and cores[q] in chipmates]
     far = [q for q in range(4) if cores[q] not in chipmates]
+    far.sort(key=lambda q: topo.die(cores[q]) != topo.die(core))
     e_near, e_far = split_engines(T, topo, core)
     hf = len(e_far) // 2
     eng3 = {near[0]: e_near, far[0]: e_far[:hf], far[1]: e_far[hf:]}
@@ -278,12 +287,9 @@ def rank_program(g, core, T, topo):
         c = 1536 * t + 512 * slot(frm, to)
         return v("lq", c, c + 512)
 
-    def quarters(src, t):
-        for qs in ([far + near] if t == 0 else [far, near]):
-            send([([cores[q]], eng3[q], ("ah%d" if q in near else "aq%d") % t, [v(src, 512 * q, 512 * q + 512)],
-                   [lq(t, rank, q)], 0) for q in qs])
-        arrive(lq(t, near[0], rank), "ah%d" % t, len(e_near))
-        add("-", "arr", None, [], [lq(t, q, rank) for q in far], tok=("aq%d" % t, len(e_far)))
+    def quarter(t, q, es, sem):
+        send([([cores[q]], es, sem, [v("Xp", 512 * q, 512 * q + 512)], [lq(t, rank, q)], 0)])
+        arrive(lq(t, q, rank), sem, len(es))
 
     def mq(u, q):
         return v("Mp", W * u + 512 * q, W * u + 512 * q + 512)
@@ -291,45 +297,57 @@ def rank_program(g, core, T, topo):
     def nothing():
         pass
 
+    def spread(src, dst, lands, sems):
+        for qs in (near + far[:1], far[1:]):
+            send([([cores[q]], e_near if q in near else e_far, sems[(near + far).index(q)], [src(q)], [dst(q)], 0) for q in qs])
+        for k, q in enumerate(near + far):
+            arrive(lands(q), sems[k], len(e_near) if q in near else len(e_far))
+
     def fold(src, t, part, f1=nothing, f2=nothing):
         a, b, c, d = [v(src, 512 * rank, 512 * rank + 512)] + [lq(t, q, rank) for q in near + far]
         r1, r2, r3 = [v("rl", 512 * k, 512 * k + 512) for k in range(3)]
-        if part < 2:
-            bank, x, y, r = (("PS", a, b, r1), ("PT", c, d, r2))[part]
-            mm(v(bank), v("Ib"), x, True, False)
-            mm(v(bank), v("Nb"), y, False, True)
-            act(r, v(bank), AF.Relu)
-            return
-        for k, (m, x) in enumerate((("Ib", b), ("Nb", d), ("Ib", r1), ("Nb", r2))):
-            mm(v("PG"), v(m), x, k == 0, k == 3)
-        f1()
-        act(r3, v("PG"), AF.Relu)
-        terms = [("Rb", d), ("Rb", r2), ("Rb", r3)]
-        if t == RO:
-            terms = [("Ib", x) for x in (a, b, c, d)] + [("Rb", x) for x in (d, r2, r3)]
-        for k, (m, x) in enumerate(terms):
-            mm(v("PF"), v(m), x, k == 0, k == len(terms) - 1)
-        f2()
-        act(mq(t, rank), v("PF"), AF.Identity)
-        send([([cores[q]], eng3[q], ("ak%d" if q in near else "am%d") % t, [mq(t, rank)], [mq(t, rank)], 0) for q in eng3])
-        arrive(mq(t, near[0]), "ak%d" % t, len(e_near))
-        add("-", "arr", None, [], [mq(t, q) for q in far], tok=("am%d" % t, len(e_far)))
 
-    def blocks(src, sel, n):
-        mm(v("PA", 0, 128 * n), v("Ib"), v("ob", 0, 128 * n), True, False)
+        def summed(bank, terms, start, stop):
+            for k, (m, x) in enumerate(terms):
+                mm(v(bank), v(m), x, start and k == 0, stop and k == len(terms) - 1)
+
+        if part == 0:
+            summed("PS", [("Ib", a), ("Nb", b)], True, True)
+            act(r1, v("PS"), AF.Relu)
+        elif part == 1:
+            summed("PT", [("Ib", c), ("Nb", d)], True, True)
+            act(r2, v("PT"), AF.Relu)
+        elif part == 2:
+            if t == RO:
+                summed("PF", [("Ib", a), ("Ib", b)], True, False)
+        else:
+            summed("PG", [("Ib", b), ("Nb", d), ("Ib", r1), ("Nb", r2)], True, True)
+            f1()
+            act(r3, v("PG"), AF.Relu)
+            summed("PF", [("Rb", d), ("Rb", r2), ("Rb", r3)] if t < RO else
+                   [("Ib", c), ("I3", d), ("Rb", r2), ("Rb", r3)], t < RO, True)
+            f2()
+            act(mq(t, rank), v("PF"), AF.Identity)
+            if t:
+                send([([cores[q]], eng3[q], "am%d" % t, [mq(t, rank)], [mq(t, rank)], 0) for q in eng3])
+                add("-", "arr", None, [], [mq(t, q) for q in eng3], tok=("am%d" % t, n3))
+            else:
+                spread(lambda q: mq(t, rank), lambda q: mq(t, rank), lambda q: mq(t, q), ("ak0", "am0", "ak1"))
+
+    def blocks(src, sel, n, bank="PA"):
+        mm(v(bank, 0, 128 * n), v("Ib"), v("ob", 0, 128 * n), True, False)
         for o in range(16):
-            mm(v("PA", o, 128 * n - 15 + o, 16), v(src, o, W - 15 + o, 16), sel, False, o == 15)
+            mm(v(bank, o, 128 * n - 15 + o, 16), v(src, o, W - 15 + o, 16), sel, False, o == 15)
 
-    def turned(n):
-        for k in range(n):
-            mm(v("PF", 128 * k, 128 * k + 128), v("Ts", 128 * k, 128 * k + 128), v("Ih"), True, True)
+    def turned(k, c):
+        mm(v("PD", c, c + 128), v("Ts", 128 * k, 128 * k + 128), v("Ih"), True, True)
 
-    def records(win, f1=nothing, f2=nothing, f3=nothing, f4=nothing):
+    def records(win, bank, f1=nothing, f2=nothing, f3=nothing, f4=nothing, f5=nothing, f6=nothing):
         r8 = (0, 8, 1)
         loc = v("loc", 8, 136)
         mm(v("PC", 0, 128), v("KI"), v("cz"), True, False)
         mm(v("PG", 0, 128), v("KI"), v("oh"), True, False)
-        scan(loc, v("rst"), v("PA", 0, 128), 0.0, AL.add, AL.max)
+        scan(loc, v("rst"), v(bank, 0, 128), 0.0, AL.add, AL.max)
         mm(v("PB", 0, 128, rows=r8), v("loc", 23, 136, 16), v("Ih"), True, True)
         mm(v("PC", 0, 128), v("KI"), v("loc", 7, 135), False, False)
         mm(v("PC", 0, 128), v("KN"), loc, False, True)
@@ -346,15 +364,17 @@ def rank_program(g, core, T, topo):
         f3()
         cp(v("Kr"), v("PB", 0, 128))
         ts(v("Kf"), v("PB", 0, 128), 2049.0, AL.is_ge)
-        for k in range(8):
-            mm(v("PC", 0, 16), v("Eo", 14 - 2 * k, 142 - 2 * k), v("Kr", k, 121 + k, 8), k == 0, k == 7)
         for (mx, kk) in (("mQ", "Kr"), ("mF", "Kf")):
             for h in range(2):
                 mm(v("PA", h, 255 + h, 2), v(mx, 128 * h, 128 * h + 128), v(kk), False, kk == "Kf" and h == 1)
+        for k in range(8):
+            mm(v("PC", 0, 16), v("Eo", 14 - 2 * k, 142 - 2 * k), v("Kr", k, 121 + k, 8), k == 0, k == 7)
         f4()
-        cp(v("l" + win), v("PC", 0, 16))
         ts(v("val"), v("PA", 0, 256), 0.0, AL.max)
+        cp(v("l" + win), v("PC", 0, 16))
+        f5()
         cp(ind(v(win), v("l" + win)), v("val"))
+        f6()
 
     def running(win, f1=nothing):
         for h in range(2):
@@ -362,17 +382,27 @@ def rank_program(g, core, T, topo):
             scan(v("inv", a, b), v("dec", 0, b - a), v(win, a + 1, b + 1), v("mid", 0, 1) if h else 0.0, AL.add, AL.max)
             if h == 0:
                 cp(v("mid", 0, 1), v("inv", b - 1, b))
-            for o in range(17):
-                em = v("TA", 15, 143) if o == 0 else v("TB", 0, 128) if o == 16 else v("EI", 15 - o, 143 - o)
-                mm(v("PB" if h else "PC", 64 * h, 64 * h + 64), em, v("inv", 1024 * h + o, 1024 * h + o + 1009, 16), o == 0, o == 16)
+            counted("PB" if h else "PC", 64 * h, 64 * h + 64)
             if h == 0:
                 f1()
+
+    def counted(bank, k0, k1):
+        for o in range(17):
+            em = v("TA", 15, 143) if o == 0 else v("TB", 0, 128) if o == 16 else v("EI", 15 - o, 143 - o)
+            mm(v(bank, k0, k1), em, v("inv", 16 * k0 + o, 16 * k1 + o - 15, 16), o == 0, o == 16)
+
+    def running_whole(win, f1=nothing):
+        scan(v("inv", 0, W + 1), v("dec", 0, W + 1), v(win, 1, W + 2), 0.0, AL.add, AL.max)
+        f1()
+        counted("PC", 0, 128)
 
     def inv_half(o, c0, h):
         cp(v(o, c0 + 64 * h, c0 + 64 * h + 64), v("PB" if h else "PC", 64 * h, 64 * h + 64))
 
-    def wipe(win):
-        act(ind(v(win), v("l" + win)), v("zer", 0, 256), AF.Tanh)
+    def wipe(win, behind):
+        for h in range(2):
+            dma("S", v(win, 1032 * h, 1032 * h + 1032), v("zer", 0, 1032))
+            ops[-1]["after"] = [behind]
 
     def score(k, lname, l0, Ms, cuts):
         for c in range(len(cuts) - 1):
@@ -405,24 +435,21 @@ def rank_program(g, core, T, topo):
         else:
             absred(a, bank)
 
-    def mu_slope(rot=True):
+    def mu_slope():
         mm(v("PD", 0, 128), v("U1"), v("muf", 0, 128), True, False)
         mm(v("PD", 0, 128), v("U2"), v("muf", 1, 129), False, True)
-        if rot:
-            mm(v("PD", 128, 256), v("Rot"), v("muf", 0, 128), True, True)
 
-    def slopes(k0=0, k1=128, part=None, src=("PG", 0)):
+    def slopes(bank, f1=nothing, part=None):
         if part != 1:
-            act(v("a1", k0, k1), v(src[0], src[1] + k0, src[1] + k1), AF.Abs)
-            act(v("a3", k0, k1), v("a1", k0, k1), AF.Relu, bias=4.0, scale=-1.0)
-            mm(v("PS", k0, k1), v("Ib"), v("cap", k0, k1), True, False)
-            mm(v("PS", k0, k1), v("Nb"), v("a2", k0, k1), False, False)
-            mm(v("PS", k0, k1), v("N5"), v("a3", k0, k1), False, True)
-        if part != 0:
-            cp(v("ixu", k0, k1), v("PS", k0, k1))
-
-    def mu_cap():
-        act(v("a2"), v("PD", 0, 128), AF.Relu, bias=4.0, scale=-1.0)
+            act(v("a1"), v(bank, 256, 384), AF.Abs)
+            f1()
+            act(v("a3"), v("a1"), AF.Relu, bias=4.0, scale=-1.0)
+            act(v("a2"), v("PD", 0, 128), AF.Relu, bias=4.0, scale=-1.0)
+        if part == 0:
+            return
+        mm(v("PS", 0, 128), v("Ib"), v("cap"), True, False)
+        mm(v("PS", 0, 128), v("a3"), v("N5"), False, False)
+        mm(v("PS", 0, 128), v("Nb"), v("a2"), False, True)
 
     dma("S", v("g32"), ext(T.gam[:]))
     dma("A", v("X"), ext(T.xs[:]))
@@ -435,7 +462,13 @@ def rank_program(g, core, T, topo):
     dma("S", v("rh", 0, 5), ext(T.rho[:]))
     send([([cores[prev]], e_prev, "ag", [v("g32")], [v("gn32")], 0)])
     arrive(v("gn32"), "ag", n_next)
-    quarters("X", 0)
+    if FS:
+        spread(lambda q: v("X", 512 * q, 512 * q + 512), lambda q: lq(0, rank, q), lambda q: lq(0, q, rank), ("ah0", "aq0", "ar0"))
+    else:
+        send([([cores[q]], eng3[q], s, [v("X", 512 * q, 512 * q + 512)], [lq(0, rank, q)], 0)
+              for q, s in zip(near + far, ("ah0", "aq0", "ar0"))])
+        for q, s in zip(near + far, ("ah0", "aq0", "ar0")):
+            arrive(lq(0, q, rank), s, len(eng3[q]))
     ms(v("oh"), 1.0)
     for (c, b, m) in [(0, 1, 15), (1, 2, 112), (3, 2, 127), (5, 1, 7)]:
         ts(v("pj", c, c + b), v("pi", 0, b), m, AL.bitwise_and)
@@ -455,16 +488,13 @@ def rank_program(g, core, T, topo):
     for i in range(16):
         act(v("IW", i, W - 15 + i, 16), v("iom", 0, 128), AF.Identity, bias=v("ib", i, i + 1), scale=hi)
     grp[0] = 0
-    ms(v("tA", 0, 2052), 0.0)
+    ms(v("zer"), 0.0)
+    wipe("tA", len(ops) - 1)
     ts(wd, lo, -KK, AL.mult, z0, AL.add)
     ts(p16, pp, 16.0, AL.mult)
     ts(wd, wd, hi, AL.subtract)
-    act(v("zer", 0, 1040), v("tA", 0, 1040), AF.Identity)
-    act(v("dec"), v("zer", 0, 1040), AF.Identity, bias=wd)
-    cp(v("gu"), v("g32"))
-    cp(v("eu"), v("e32"))
-    gat("A", v("Wc"), v("IW"), v("gu"))
-    gat("A", v("D1"), v("X"), v("eu", 0, 128))
+    act(v("dec", 0, 1032), v("zer", 0, 1032), AF.Identity, bias=wd)
+    dma("S", v("dec", 1032, 2064), v("dec", 0, 1032))
     ts(v("Ih"), v("iom", 0, 128), pp, AL.is_equal)
     ts(v("KI"), v("iom", 0, 128), pp, AL.is_equal, KK, AL.mult)
     ts(v("Rot"), v("iom", 0, 128), ppm, AL.is_equal)
@@ -477,6 +507,10 @@ def rank_program(g, core, T, topo):
     ts(gii, gb, p8, AL.add)
     ts(v("Sel"), v("iog"), p16, AL.is_equal, KK, AL.mult)
     ts(v("Bg", 7, 128, 8), v("iod"), -2.0, AL.mult, p4, AL.add)
+    cp(v("gu"), v("g32"))
+    cp(v("eu"), v("e32"))
+    gat("A", v("Wc"), v("IW"), v("gu"))
+    gat("A", v("D1"), v("X"), v("eu", 0, 128))
     ts(c2, i0, -1.0, AL.add)
     ts(eo, gb, lo, AL.add)
     ts(v("s3"), v("io8"), gii, AL.is_equal)
@@ -525,18 +559,22 @@ def rank_program(g, core, T, topo):
         tt(v("wr", 4, 5), v("wr", 2, 3), v("wr", 1, 2), AL.subtract)
         ts(v("S3", 24, 32), v("E", 15, 128, 16), v("wr", 0, 1), AL.mult)
 
-    def late_constants():
-        ts(v("s3", 0, 8), v("iog", 0, 113, 16), gbp, AL.is_equal)
-        ts(v("EA"), v("E"), v("wr", 0, 1), AL.mult)
-        ts(v("EB"), v("E"), v("wr", 1, 2), AL.mult)
-        ts(v("EC"), v("E"), v("wr", 4, 5), AL.mult)
-        ts(v("S3", 0, 8), v("s3", 0, 8), v("wr", 3, 4), AL.mult)
-        cp(v("S3", 8, 16), v("EB", 15, 128, 16))
-        cp(v("S3", 16, 24), v("EC", 15, 128, 16))
-        ts(v("U2"), v("E", 0, 128), v("wr", 5, 6), AL.mult)
+    def row_constants(cols):
+        for (c, k) in cols:
+            ts(v("S3", c, c + 8), v("E", 15, 128, 16), v("wr", k, k + 1), AL.mult)
+
+    def mean_constants():
         ts(v("Iq"), v("Ih"), 0.25, AL.mult)
+        ts(v("Pq"), v("Rot"), 0.25, AL.mult)
+        ts(v("S3", 0, 8), v("iog", 0, 113, 16), gbp, AL.is_equal, v("wr", 3, 4), AL.mult)
+
+    def slope_constants():
+        ts(v("U2"), v("E", 0, 128), v("wr", 5, 6), AL.mult)
         ts(v("a1"), v("iom", 1, 129), pp, AL.is_equal, v("wr", 6, 7), AL.mult)
         ms(v("cap"), 24.0)
+
+    def late_constants():
+        ts(v("I3"), v("Ib"), 3.0, AL.mult)
         ts(v("N5"), v("Ib"), -5.0, AL.mult)
         ms(v("tab"), 0.0)
         ms(v("muf", 128, 132), 4096.0)
@@ -548,7 +586,8 @@ def rank_program(g, core, T, topo):
         ts(v("tab", 0, 25), v("tab", 32, 57), 32.0, AL.mult)
         ts(v("tab", 64, 89), v("tab", 32, 57), 1.0 / 128, AL.mult)
 
-    H2, C3, Q4 = [0, 64, 128], [0, 56, 104, 128], [0, 32, 64, 96, 128]
+    H2, Q4 = [0, 64, 128], [0, 32, 64, 96, 128]
+    ready = (("X", 0), ("D1", 1), ("D2", 2))
     for t in range(RO):
         last = t == RO - 1
         rnd[0] = t
@@ -557,196 +596,231 @@ def rank_program(g, core, T, topo):
         def xq(q, k0, k1):
             gat(q, v("X", 16 * k0, 16 * k1), v("Xp"), v("muu", k0, k1))
 
-        def lists2():
-            ts(v("l2u"), v("PF", 0, 128), -1.0, AL.add)
-            ts(v("l2h"), v("PF", 0, 128), -1.0, AL.add)
+        def lists2(*names):
+            for n in names:
+                ts(v(n), v("PD", 256, 384), -1.0, AL.add)
 
         if t > 0:
-            blocks("Wc", v("S3", 0, 24), 3)
-            cp(v("muf", 0, 128), v("muu"))
+            blocks("Wc", v("S3", 0, 24), 3, "PF")
+            ts(v("msu"), v("PD", 128, 256), -0.375, AL.add)
             xq("D", 128 - XD, 128)
             xq("A", 0, 128 - XD)
-            records("tA", f1=lambda: cp(v("Ts"), v("PA", 0, 384)), f2=lambda: (turned(3), mu_slope()), f3=lists2,
-                    f4=lambda: (cp(v("msu"), v("PD", 128, 256)), cp(v("du"), v("PF", 128, 256))))
-            gat("A", v("D1"), v("X"), v("eu", 128 * t, 128 * t + 128))
-            for h in range(2):
-                gat("A", v("Ms", 1024 * h, 1024 * h + 1024), v("Mp", W * t, W * t + W), v("msu", 64 * h, 64 * h + 64))
+
+            def drawn(q, k0, k1):
+                if k1 > k0:
+                    gat(q, v("D1", 16 * k0, 16 * k1), v("X"), v("eu", 128 * t + k0, 128 * t + k1))
+
+            records("tA", "PF", f1=lambda: cp(v("Ts", 0, 128), v("PF", 0, 128)), f2=lambda: turned(0, 256),
+                    f3=lambda: drawn("D", 128 - DE, 128 - DE // 2), f4=lambda: drawn("D", 128 - DE // 2, 128),
+                    f5=lambda: lists2("l2u"), f6=lambda: lists2("l2h"))
+            drawn("A", 0, DD)
+            for a, b in ((0, 64), (64, 128 - MD)):
+                gat("A", v("Ms", 16 * a, 16 * b), v("Mp", W * t, W * t + W), v("msu", a, b))
+            drawn("A", DD, 128 - DE)
+            if MD:
+                gat("D", v("Ms", W - 16 * MD, W), v("Mp", W * t, W * t + W), v("msu", 128 - MD, 128))
             dma("S", v(Mu, rows=(16, 128, 1)), v("Ms", rows=(0, 112, 1)))
             dma("S", v(Mu, rows=(0, 16, 1)), v("Ms", rows=(112, 128, 1)))
-            running("tA", lambda: (stay(0, Ms), stay(1, Ms)))
-            for c in range(2, 4):
-                stay(c, Ms)
+            running_whole("tA", lambda: [stay(c, Ms) for c in range(SE)])
         else:
             mm(v("PA", 0, 128), v("Ih"), v("oh"), True, False)
             mm(v("PA", 0, 128), v("gnh"), v("Rot"), False, True)
-            mm(v("PF", 0, 128), v("Ih"), v("oh"), True, False)
-            mm(v("PF", 0, 128), v("Rot"), v("gnh"), False, True)
-            records("tA", f1=mid_constants, f2=lambda: fold("X", 0, 0), f3=lambda: (lists2(), fold("X", 0, 1)),
+            mm(v("PD", 256, 384), v("Ih"), v("oh"), True, False)
+            mm(v("PD", 256, 384), v("Rot"), v("gnh"), False, True)
+            records("tA", "PA", f1=mid_constants, f2=lambda: fold("X", 0, 0), f3=lambda: (lists2("l2u", "l2h"), fold("X", 0, 1)),
                     f4=sum_constants)
-            fold("X", 0, 2)
-            gat("A", v("D2"), v("X"), v("l2u"))
-            running("tA")
+            d2 = [lambda k=k: gat("A", v("D2", 512 * k, 512 * k + 512), v("X"), v("l2u", 32 * k, 32 * k + 32))
+                  for k in [rank] + near + far]
+            fold("X", 0, 3, d2[0], d2[1])
+            running_whole("tA", lambda: stay(rank, Ms))
+            for k in range(2, 4):
+                d2[k]()
+            mid_constants2()
             dma("S", v("pb"), ext(T.pay[:]))
             ops[-1]["after"] = [len(ops) - 2]
         dma("S", v("Wc", rows=(1, 128, 8)), v("IW", rows=(1, 128, 8)))
-        inv_half("l3u", 0, 0)
         if t > 0:
-            inv_half("l3h", 0, 0)
-            score(3, "l3u", 0, Ms, H2[:2])
-        inv_half("l3u", 0, 1)
-        if t > 0:
-            inv_half("l3h", 0, 1)
-            score(3, "l3u", 0, Ms, H2[1:])
+            score(2, "l2u", 0, Ms, H2[:2])
+            n = len(ops) - 1
+            wipe("tB", n)
+            if not last:
+                wipe("tA", n)
+            if AE:
+                absum(2, H2, [0])
+            for c in range(SE, 4):
+                stay(c, Ms)
+            score(2, "l2u", 0, Ms, H2[1:])
+            cp(v("l3u"), v("PC", 0, 128))
+            cp(v("l3h"), v("PC", 0, 128))
             for c in range(4):
                 stay(c, Ms, "D1", 1)
             mm(v("PB", 0, 4), v("GM"), v("tie"), True, False)
-            score(2, "l2u", 0, Ms, C3)
-            absum(3, H2, [0, 1])
-            absum(2, C3, [2, 1], "D")
-            absum(2, C3, [0], "D" if AD else "A")
+            score(3, "l3u", 0, Ms, C3)
+            cp(v("muf", 0, 128), v("muu"))
+            if not AE:
+                absum(2, H2, [0])
+            absum(3, C3, [0])
+            absum(3, C3, [2, 1], "D")
+            absum(2, H2, [1])
         else:
-            inv_half("l3h", 0, 0)
-            inv_half("l3h", 0, 1)
+            cp(v("l3u"), v("PC", 0, 128))
+            cp(v("l3h"), v("PC", 0, 128))
             mm(v("PB", 0, 4), v("GM"), v("tie"), True, False)
             for c in [rank] + near + far:
                 score(3, "l3u", 0, Ms, Q4[c:c + 2])
                 if c == far[0]:
-                    dma("S", v("tB", 0, 1026), v("zer", 0, 1026))
-                    ops[-1]["after"] = [len(ops) - 2]
-                    dma("S", v("tB", 1026, 2052), v("zer", 0, 1026))
-                for (src, k) in (("X", 0), ("D1", 1), ("D2", 2)):
-                    stay(c, Ms, src, k, "D" if k == 2 and c in far else "A")
+                    n = len(ops) - 1
+                    wipe("tB", n)
+                    wipe("tA", n)
+                for (src, k) in ready if c != rank else ready[1:]:
+                    stay(c, Ms, src, k, "D" if k == 2 and c in (near + far)[:ZD] else "A")
                 absum(3, Q4, [c], "D")
-                if c == near[0]:
-                    mid_constants2()
-        sums = (3, 2, 1, 0) if t else [rank] + near + far
+        sums = (3, 0, 2, 1) if t else [rank] + near + far
+        if t > 0:
+            cp(v("Ts", 128, 256), v("PF", 128, 256))
         for c in sums:
             mm(v("PB", 0, 4), v("GM"), acc(c, 0, 4), False, c == sums[3])
         if t > 0:
-            mu_cap()
-            slopes(part=0, src=("PF", 256))
+            mu_slope()
+            turned(1, 384)
+            slopes("PF", part=0)
         red(v("mn", 0, 1), v("PB", 0, 4), AL.min)
         for k in range(4):
             ts(v("dg", 128 * k, 128 * k + 128), v("Ih"), v("PB", k, k + 1), AL.mult, v("mn", 0, 1), AL.is_equal)
         for k, l in enumerate([v("l0"), v("eh", 128 * t, 128 * t + 128), v("l2h"), v("l3h")]):
             mm(v("PA", 0, 128), v("dg", 128 * k, 128 * k + 128), l, k == 0, k == 3)
+        if t > 0:
+            slopes("PF", part=1)
         cp(v("cu"), v("PA", 0, 128))
-        gat4("Wm", v("Wc"), "cu")
+        for h, e in enumerate("DA"):
+            gat(e, v("Wm", 1024 * h, 1024 * h + 1024), v("Wc"), v("cu", 64 * h, 64 * h + 64))
         if not last:
             dma("S", dr("st", T.st[t], t), v("Wm", 0, W, rows=(0, 128, 8)))
         blocks("Wm", v("S3", 24, 32), 1)
         if t > 0:
-            slopes(part=1)
-        k0 = 32 * far[0]
-        gat("A", v("Xp", 16 * k0, 16 * k0 + 1024), v("X"), v("cu", k0, k0 + 64))
-        act(v("Wm", W, W + 1), v("Wm", W - 1, W), AF.Identity, bias=lo)
-        for q in (near[0], rank):
+            cp(v("ixu"), v("PS", 0, 128))
+            cp(v("du"), v("PD", 384, 512))
+        for q, sem in zip(far, ("aq%d", "ar%d")):
             gat("A", v("Xp", 512 * q, 512 * q + 512), v("X"), v("cu", 32 * q, 32 * q + 32))
-        quarters("Xp", t + 1)
-        records("tB")
+            quarter(t + 1, q, e_far, sem % (t + 1))
+        act(v("Wm", W, W + 1), v("Wm", W - 1, W), AF.Identity, bias=lo)
+        vo = "V%d" % (t % 2)
+        vi = v("pb") if t == 1 else v("V%d" % ((t + 1) % 2))
+
+        def factors(k0, k1):
+            if t > 0 and k1 > k0:
+                gat("A", v("R", 16 * k0, 16 * k1), v("tab", 0 if t == 1 else 32, 32 if t == 1 else 64), v("ixu", k0, k1))
+
+        def carry(k0, k1):
+            if k1 > k0:
+                tt(v(vo, 16 * k0, 16 * k1), ind(vi, v("du", k0, k1)), v("R", 16 * k0, 16 * k1), AL.mult)
+
         dma("S", v("Wm", 0, W, rows=(2, 128, 8)), v("Wm", 1, W + 1, rows=(1, 128, 8)))
         if not last:
             send([([cores[prev]], e_prev, "an%d" % t, [dr("st", T.st[t], t)], [dr("ld", T.ld[t], t)], 0)])
             arrive(dr("ld", T.ld[t], t), "an%d" % t, n_next)
             dma("S", v("Wm", 0, W, rows=(3, 128, 8)), dr("ld", T.ld[t], t))
-        if t > 0:
-            for h in range(2):
-                gat("A", v("R", 1024 * h, 1024 * h + 1024), v("tab", 0 if t == 1 else 32, 32 if t == 1 else 64),
-                    v("ixu", 64 * h, 64 * h + 64))
+        for q in (near[0], rank):
+            gat("A", v("Xp", 512 * q, 512 * q + 512), v("X"), v("cu", 32 * q, 32 * q + 32))
+        quarter(t + 1, near[0], e_near, "ah%d" % (t + 1))
+        if t == 0:
+            records("tB", "PA", f1=mean_constants, f2=lambda: row_constants([(8, 1)]),
+                    f3=lambda: row_constants([(16, 4), (32, 1), (40, 0)]),
+                    f4=lambda: (row_constants([(48, 4)]), slope_constants()))
+        else:
+            records("tB", "PA")
+        factors(0, 64)
+        factors(64, 128)
         if last:
             ts(v("Rb"), v("Ib"), 2.0, AL.mult)
-        if t == 0:
-            act(v("p4"), v("pb"), AF.Identity, scale=0.25)
         fold("Xp", t + 1, 0)
-        if not last:
-            wipe("tA")
-        running("tB", lambda: fold("Xp", t + 1, 1))
+        fold("Xp", t + 1, 2)
+        if FM:
+            running("tB", lambda: fold("Xp", t + 1, 1))
+        else:
+            running("tB")
+            fold("Xp", t + 1, 1)
+
         def li(h, s):
             c = 384 * t + 192 * h + 64 * s
             return v("li", c, c + 64)
 
-        vo = "V%d" % (t % 2)
-        vi = v("pb") if t == 1 else v("V%d" % ((t + 1) % 2))
         iv = [v("ivh", 128 * t + 64 * h, 128 * t + 64 * h + 64) for h in range(2)]
         for h in range(2):
             inv_half("ivh", 128 * t, h)
             send([([cores[q]], eng3[q], "ai%d" % (2 * t + h), [iv[h]], [li(h, slot(rank, q))], 0) for q in eng3])
             add("-", "arr", None, [], [li(h, s) for s in range(3)], tok=("ai%d" % (2 * t + h), n3))
+            if t == 0 and h == 0:
+                ts(v("p4"), v("pb"), 0.25, AL.mult)
             if t > 0:
-                for a, b in [(0, 512)] if h == 0 else [(512, 1024), (1024, W)]:
-                    tt(v(vo, a, b), ind(vi, v("du", a // 16, b // 16)), v("R", a, b), AL.mult)
+                for a, b in [(0, 32)] if h == 0 else [(32, 64), (64, 128)] if last else [(32, 128)]:
+                    carry(a, b)
                     if last and a:
-                        dma("G", v(vo, b - 1024, b), v(Mu, b - 1024, b), acc=True)
+                        dma("G", v(vo, 16 * b - 1024, 16 * b), v(Mu, 16 * b - 1024, 16 * b), acc=True)
         if t == 0:
             late_constants()
-        if not last:
-            wipe("tB")
-        fold("Xp", t + 1, 2)
+        def mean(h):
+            for k, x in enumerate([iv[h]] + [li(h, s) for s in range(3)]):
+                mm(v("PC" if h else "PD", 0, 64), v("Iq"), x, k == 0, k == 3)
+
+        fold("Xp", t + 1, 3)
         if t > 0 and not last:
             dma("G", v(vo), v(Mu), acc=True)
         for h in range(2):
             bank = v("PC" if h else "PD", 0, 64)
-            for k, x in enumerate([iv[h]] + [li(h, s) for s in range(3)]):
-                mm(bank, v("Iq"), x, k == 0, k == 3)
+            mean(h)
             ts(v("muu", 64 * h, 64 * h + 64), bank, -0.375, AL.add)
+            for u in range(2) if h and not last else []:
+                for k, x in enumerate([iv[u]] + [li(u, s) for s in range(3)]):
+                    mm(v("PD", 128 + 64 * u, 192 + 64 * u), v("Pq"), x, k == 0, k == 3)
             for k, e in enumerate("DA"):
                 q = 2 * h + k
                 gat(e, v("Wc", 512 * q, 512 * q + 512), v("Wm", 0, W), v("muu", 32 * q, 32 * q + 32))
 
-    far.sort(key=lambda q: topo.die(cores[q]) != topo.die(core))
     order = far + near + [rank]
     cp(v("muf", 0, 128), v("muu"))
-    mu_slope(False)
+    blocks("Wc", v("S3", 32, 56), 3)
+    mu_slope()
+    slopes("PA", lambda: cp(v("Ts", 0, 256), v("PA", 0, 256)))
+    turned(0, 256)
+    turned(1, 384)
+    cp(v("ixu"), v("PS", 0, 128))
+    ts(v("du"), v("PD", 256, 384), -1.0, AL.add)
+    cp(v("gpu"), v("PD", 384, 512))
 
-    def lists(hh):
-        k0 = 32 * min(order[2 * hh:2 * hh + 2])
-        conv("PG", "EC", "Wc", k0, k0 + 64)
-        conv("PA" if hh else "PF", "EB", "Wc", k0, k0 + 64)
-        slopes(k0, k0 + 64, 0)
-        conv("PC" if hh else "PT", "EA", "Wc", k0, k0 + 64)
+    def part(name, q, h=None):
+        return v(name, 512 * q, 512 * q + 512) if h is None else v(name, 512 * q + 256 * h, 512 * q + 256 * h + 256)
 
-    def lists_out(hh):
-        k0 = 32 * min(order[2 * hh:2 * hh + 2])
-        cp(v("du", k0, k0 + 64), v("PA" if hh else "PF", k0, k0 + 64))
-        slopes(k0, k0 + 64, 1)
-        cp(v("gpu", k0, k0 + 64), v("PC" if hh else "PT", k0, k0 + 64))
+    def lst(name, q, h=None):
+        return v(name, 32 * q, 32 * q + 32) if h is None else v(name, 32 * q + 16 * h, 32 * q + 16 * h + 16)
 
-    def part(name, q):
-        return v(name, 512 * q, 512 * q + 512)
-
-    mu_cap()
-    lists(0)
-    lists_out(0)
-    for k, q in enumerate(order):
-        gat("A", part("R", q), v("tab", 64, 96), v("ixu", 32 * q, 32 * q + 32))
-        if k == 0:
-            lists(1)
-        tt(part("V0", q), ind(v("V1"), v("du", 32 * q, 32 * q + 32)), part("R", q), AL.mult)
-        s = slot(rank, q)
-        if k < 2:
-            tt(part("Tg", k), ind(v("p4"), v("gpu", 32 * q, 32 * q + 32)), part("V0", q), AL.add)
-            send([([cores[q]], e_far, "af%d" % s, [part("Tg", k)], [part("lf", s)], 0)])
-        if k == 0:
-            lists_out(1)
-        if k == 1:
-            for x in order[2:]:
-                gat("A", part("D1", x), v("p4"), v("gpu", 32 * x, 32 * x + 32))
-            send([([cores[near[0]]], e_near, "ap", [part("D1", near[0])], [part("D2", 0)], 0)])
-        if k == 2:
-            send([([cores[q]], e_near, "af%d" % s, [part("V0", q)], [part("lf", s)], 0)])
-    gat("A", v("Mg"), v("Mp", 4 * W, 5 * W), v("muu", 32 * rank, 32 * rank + 32), scale=1.0 / 64)
+    for n, (k, h) in enumerate([(0, 0), (0, 1), (1, None)]):
+        q = far[k]
+        gat("A", part("R", q, h), v("tab", 64, 96), lst("ixu", q, h))
+        tt(part("V0", q, h), ind(v("V1"), lst("du", q, h)), part("R", q, h), AL.mult)
+        tt(part("Tg", k, h), ind(v("p4"), lst("gpu", q, h)), part("V0", q, h), AL.add)
+        trs = [([cores[q]], e_far, "af%d" % n, [part("Tg", k, h)], [part("lf", slot(rank, q), h)], 0)]
+        if n == 1:
+            gat("A", part("D1", near[0]), v("p4"), lst("gpu", near[0]))
+            trs.append(([cores[near[0]]], e_near, "ap", [part("D1", near[0])], [part("D2", 0)], 0))
+        send(trs)
+        arrive(part("lf", slot(q, rank), h), "af%d" % n, len(e_far))
+    for q in order[2:]:
+        gat("A", part("R", q), v("tab", 64, 96), lst("ixu", q))
+        tt(part("V0", q), ind(v("V1"), lst("du", q)), part("R", q), AL.mult)
+        if q in near:
+            send([([cores[q]], e_near, "af4", [part("V0", q)], [part("lf", slot(rank, q))], 0)])
+    gat("A", part("D1", rank), v("p4"), lst("gpu", rank))
+    gat("A", v("Mg"), v("Mp", 4 * W, 5 * W), lst("muu", rank), scale=1.0 / 64)
     arrive(part("D2", 0), "ap", len(e_near))
-    for s in range(3):
-        arrive(part("lf", s), "af%d" % s, len(e_near) if (rank + s + 1) % 4 in near else len(e_far))
-    terms = [part("D1", rank), part("D2", 0), v("Mg")]
+    arrive(part("lf", slot(near[0], rank)), "af4", len(e_near))
+    terms = [part("D2", 0), part("D1", rank), v("Mg")]
     for k, x in enumerate(terms):
         mm(v("PB"), v("Ib"), x, k == 0, k == len(terms) - 1)
     tt(v("PB"), v("PB"), part("V0", rank), AL.add)
-    for q in (order[0], order[2]):
+    for q in (far[0], near[0]):
         tt(v("PB"), v("PB"), part("lf", slot(q, rank)), AL.add)
-    s = slot(order[1], rank)
     for h in range(2):
-        a, b = 256 * h, 256 * h + 256
-        tt(v("yo", a, b), v("PB", a, b), v("lf", 512 * s + a, 512 * s + b), AL.add)
-        dma("A" if h else "S", ext(T.y[:, a:b]), v("yo", a, b))
+        tt(part("yo", 0, h), part("PB", 0, h), part("lf", slot(far[1], rank), h), AL.add)
+        dma("A" if h else "S", ext(T.y[:, 256 * h:256 * h + 256]), part("yo", 0, h))
     emit(g, T, ops)

@@ -3,17 +3,38 @@ from concourse.mybir import dt, AluOpType, AxisListType, ActivationFunctionType
 
 W = 2048
 RO = 4
-TW = 2576
-XD = 40
-SE = 3
+REST = 16392.0 - 1.0 / 512
+STEP = 32.0
+LIFT = [15 * 1024.0 + W, 15 * (1024.0 + STEP / 16)]
+TW = 2320
+XD = [48, 48]
+SE = 4
 FS = False
 ZD = 1
-FM = True
-DD = 64
-DE = 32
-MD = 0
-AE = True
-C3 = [0, 56, 96, 128]
+XQ = 1
+WE = ["DADA", "DADA", "DADA"]
+WD = 64
+IWD = 6
+MID = 1
+AH = [0, 0]
+FMO = 0
+ROT = "STAGBDC"
+VA = [0, 64]
+OUT = "R0 R1 V0 V1 T0 S0 R2w T1 P4w S1 R4w V2w V4w S4w T2 S2 T3 S3 R6 P6 V6 M6 E6 A0 A6 A4 Y2"
+MSH = 1
+D0D = 48
+TRIALS = [["", "E0A", "", "m0", "E1D m1", "g2A0:16 m2", "", "m3 +AG +BD p10 g2A48:88 I p11 p00",
+           "p01 g2D40:48 K q00 C s00A L g2A16:40 t30 g2A88:128 s10A s20A p02 s30D s21A t31 s01A s11D s02A -B s22A s12A s31D "
+           "t32 s13A s23A s03A t33 Q s32D G1 s33D G0 G2 G3", "", "", "", ""],
+          ["g1A0:96 M1 M0 g1A96:104", "", "", "", "g1D104:128", "S0 p11", "g2A80:128", "s11A +AG p01 s00A q01 p10 s10A",
+           "g2D0:32 t21 s01A C g2D64:80 I s21A s20A L s23A s03A Q g3D0:32 t31 s13A t33 s22A t32 s12A "
+           "s31D s02A s30A s32D G1 G2 s33D G3 S1 G0 S2", "", "S3", "", ""]]
+XB = [24, 16]
+PLAN = [["x0 e1 x2 d", "n S4 x3", "S5 r56", "x1 e0", "", "k01 k12 r80 m0", "r120", "m1", "k22 r128", "v40", "v120 m2 k33 m3",
+         "v128", "", "", "", "", ""],
+        ["d x1 S4 n h0 x2 r128 x3", "", "", "S5", "", "", "", "", "", "v40 b2", "m0 b3 v64 v104 m1",
+         "a2", "m2 k31", "", "m3", "v128 a3", ""]]
+SW = True
 KK = 8192.0
 F, B, H, I32, U = "float32", "bfloat16", "float16", "int32", "uint16"
 
@@ -23,37 +44,38 @@ def _sb(cols, d):
 
 
 SCRATCH = {
-    "X": _sb(W, B), "Xp": _sb(W, B), "Ms": _sb(W, B), "Mu0": _sb(W, B), "Mu1": _sb(W, B), "Mp": _sb(5 * W, B),
+    "X": _sb(W, B), "Xp": _sb(W, B), "Ms": _sb(3 * W, B), "rsp": _sb(128, H), "Mk": _sb(128, H), "Fr": _sb(128, H), "Fm": _sb(128, H), "B8": _sb(8, H), "Mp": _sb(5 * W, B),
     "lq": _sb(5 * 3 * 512, B), "Wm": _sb(W + 16, B), "Wc": _sb(W, B), "IW": _sb(W, B),
     "D0": _sb(W, B), "D1": _sb(W, B), "D2": _sb(W, B), "D3": _sb(W, B),
-    "tA": _sb(TW, F), "tB": _sb(TW, F), "zer": _sb(1040, F), "val": _sb(256, F), "inv": _sb(W + 16, H), "dec": _sb(2064, B),
+    "tA": _sb(TW, F), "tB": _sb(TW, F), "val": _sb(128, F), "inv": _sb(W, H), "dec": _sb(W, B),
     "rst": _sb(128, H), "cz": _sb(128, H), "Bg": _sb(128, H), "KI": _sb(128, H), "KN": _sb(128, H), "Cs": _sb(136, H),
-    "Sel": _sb(128, H), "Q": _sb(128, H), "Kr": _sb(128, H), "Kf": _sb(128, H), "Z0": _sb(128, H), "cb": _sb(256, H),
-    "Eo": _sb(144, H), "mQ": _sb(256, H), "mF": _sb(256, H), "TA": _sb(144, H), "TB": _sb(144, H),
-    "Rot": _sb(128, H), "io8": _sb(128, F), "iod": _sb(16, F), "Ts": _sb(256, H), "Pq": _sb(128, H), "S3": _sb(56, B), "I3": _sb(128, B), "gn32": _sb(128, I32), "gnh": _sb(128, H), "oh": _sb(128, H),
+    "Sel": _sb(128, H), "Q": _sb(128, H), "Kr": _sb(128, H), "Kf": _sb(128, H), "Z0": _sb(128, H), "cb": _sb(128, H),
+    "mQ": _sb(256, H), "mF": _sb(256, H),
+    "Rot": _sb(128, H), "Ts": _sb(256, H), "Pq": _sb(128, H), "S3": _sb(56, B), "I3": _sb(128, B), "gn32": _sb(128, I32), "gnh": _sb(128, H), "oh": _sb(128, H),
     "pg": _sb(16, F), "ab": _sb(8, F),
     "V0": _sb(W, F), "V1": _sb(W, F), "R": _sb(W, F),
     "pb": _sb(W, B), "p4": _sb(W, B), "Tg": _sb(1024, F), "e32": _sb(512, I32), "eu": _sb(512, U), "eh": _sb(512, H),
     "g32": _sb(128, I32), "gu": _sb(128, U), "rh": _sb(8, F), "tab": _sb(128, F),
-    "pi": _sb(8, I32), "pj": _sb(8, I32), "pf": _sb(16, F), "iom": _sb(144, F), "iog": _sb(128, F), "ib": _sb(16, F),
-    "E": _sb(144, F), "EI": _sb(144, H),
+    "pi": _sb(8, I32), "pj": _sb(8, I32), "pf": _sb(16, F), "iom": _sb(144, B), "iog": _sb(128, B), "ib": _sb(16, F),
+    "E": _sb(144, H), "EI": _sb(144, H),
     "Ih": _sb(128, H), "Iq": _sb(128, H), "Ib": _sb(128, B), "Nb": _sb(128, B), "ob": _sb(384, B),
-    "GM": _sb(128, F), "U1": _sb(128, H), "U2": _sb(128, H),
+    "GM": _sb(128, F), "Rk": _sb(128, B), "U1": _sb(128, H), "U2": _sb(128, H),
     "cap": _sb(128, B), "N5": _sb(128, B), "tie": _sb(4, F), "l0": _sb(128, H), "wr": _sb(8, F),
     "loc": _sb(136, H), "s1": _sb(128, F), "s3": _sb(128, F), "s4": _sb(128, F),
-    "mid": _sb(4, F), "ltA": _sb(16, U), "ltB": _sb(16, U), "l2u": _sb(128, U), "l2h": _sb(128, H), "l3u": _sb(128, U),
+    "mid": _sb(4, F), "ltA": _sb(8, U), "ltB": _sb(8, U), "l2u": _sb(128, U), "l2h": _sb(128, H), "l3u": _sb(128, U),
     "l3h": _sb(128, H), "cu": _sb(128, U), "dg": _sb(512, H), "acc": _sb(16 * RO, F), "mn": _sb(4, F),
     "ivh": _sb(RO * 128, H), "li": _sb(RO * 3 * 128, H), "muu": _sb(128, U), "msu": _sb(128, U), "Rb": _sb(128, B), "rl": _sb(1536, B), "muf": _sb(132, H),
     "du": _sb(128, U), "ixu": _sb(128, U), "gpu": _sb(128, U), "a1": _sb(128, F), "a2": _sb(128, B), "a3": _sb(128, B),
     "lf": _sb(3 * 512, F), "Mg": _sb(512, B), "yo": _sb(512, F),
-    "st": ("dram", [3, 128, 256], B), "ld": ("dram", [3, 128, 256], B),
+    "st": ("dram", [3, 128, 256], B), "ld": ("dram", [3, 128, 256], B), "md": ("dram", [3, 144, W], B),
     "PA": ("psum", [128, 512], F), "PB": ("psum", [128, 512], F), "PC": ("psum", [128, 512], F),
     "PD": ("psum", [128, 512], F), "PG": ("psum", [128, 512], F), "PF": ("psum", [128, 512], F),
     "PS": ("psum", [128, 512], F), "PT": ("psum", [128, 512], F),
 }
 ARR = (["ag", "ap"] + ["aq%d" % t for t in range(5)] + ["ah%d" % t for t in range(5)] + ["ak0", "ak1"] + ["ar%d" % t for t in range(5)] + ["am%d" % t for t in range(5)]
-       + ["ai%d" % t for t in range(2 * RO)] + ["an%d" % t for t in range(3)] + ["af%d" % t for t in range(5)])
-SEMAPHORES = ["cD", "cA", "cP", "cG"] + ARR + ["s%d" % k for k in range(96)]
+       + ["ai%d" % t for t in range(2 * RO)] + ["an%d" % t for t in range(3)] + ["af%d" % t for t in range(6)]
+       + ["aw%d" % t for t in range(9)])
+SEMAPHORES = ["cD", "cA", "cP", "cG"] + ARR + ["s%d" % k for k in range(92)]
 ESZ = {F: 4, B: 2, H: 2, I32: 4, U: 2}
 AL = AluOpType
 AF = ActivationFunctionType
@@ -226,7 +248,10 @@ def rank_program(g, core, T, topo):
             kw["accum_out"] = acc["ap"]
         add("A", "c", lambda e: e.activation(o["ap"], i["ap"], fn, **kw), [i, bias, scale], [o] + ([acc] if acc else []))
 
+    held = set()
+
     def mm(o, l, r, start, stop):
+        assert not (start and o["reg"][0][0] in held)
         add("P", "c", lambda e: e.matmul(o["ap"], l["ap"], r["ap"], start, stop), [l, r], [o])
 
     def dma(q, o, i, acc=False):
@@ -276,6 +301,7 @@ def rank_program(g, core, T, topo):
     hf = len(e_far) // 2
     eng3 = {near[0]: e_near, far[0]: e_far[:hf], far[1]: e_far[hf:]}
     n3 = len(e_near) + len(e_far)
+    mine = [rank] if not MSH else [0, 1, 2, 3] if MSH == 2 else [0, 1] if rank < near[0] else [2, 3]
     prev = (rank - 1) % 4
     e_prev = e_near if prev in near else e_far
     n_next = len(e_near) if (rank + 1) % 4 in near else len(e_far)
@@ -287,9 +313,15 @@ def rank_program(g, core, T, topo):
         c = 1536 * t + 512 * slot(frm, to)
         return v("lq", c, c + 512)
 
-    def quarter(t, q, es, sem):
-        send([([cores[q]], es, sem, [v("Xp", 512 * q, 512 * q + 512)], [lq(t, rank, q)], 0)])
-        arrive(lq(t, q, rank), sem, len(es))
+    later = []
+
+    def post(q, sem, src, dst, lands, hold=False):
+        later.append((q, sem, src, dst, lands))
+        if not hold:
+            send([([cores[q]], e_near if q in near else e_far, sem, [src], [dst], 0) for (q, sem, src, dst, _) in later])
+            for (q, sem, _, _, lands) in later:
+                arrive(lands, sem, len(e_near if q in near else e_far))
+            later.clear()
 
     def mq(u, q):
         return v("Mp", W * u + 512 * q, W * u + 512 * q + 512)
@@ -297,36 +329,34 @@ def rank_program(g, core, T, topo):
     def nothing():
         pass
 
-    def spread(src, dst, lands, sems):
-        for qs in (near + far[:1], far[1:]):
-            send([([cores[q]], e_near if q in near else e_far, sems[(near + far).index(q)], [src(q)], [dst(q)], 0) for q in qs])
+    def spread(src, dst, lands, sems, one=False):
+        for qs in (near + far,) if one else (near + far[:1], far[1:]):
+            send([([cores[q]], eng3[q] if one or q in near else e_far, sems[(near + far).index(q)], [src(q)], [dst(q)], 0) for q in qs])
         for k, q in enumerate(near + far):
-            arrive(lands(q), sems[k], len(e_near) if q in near else len(e_far))
+            arrive(lands(q), sems[k], len(eng3[q]) if one or q in near else len(e_far))
 
-    def fold(src, t, part, f1=nothing, f2=nothing):
-        a, b, c, d = [v(src, 512 * rank, 512 * rank + 512)] + [lq(t, q, rank) for q in near + far]
+    ahead = {}
+
+    def fold(src, t, part, early=None):
+        a, b, c, d = [v(src, 512 * rank, 512 * rank + 512)] + [lq(t, q, rank) for q in (far[:1] + near + far[1:] if t else near + far)]
         r1, r2, r3 = [v("rl", 512 * k, 512 * k + 512) for k in range(3)]
 
         def summed(bank, terms, start, stop):
             for k, (m, x) in enumerate(terms):
                 mm(v(bank), v(m), x, start and k == 0, stop and k == len(terms) - 1)
 
-        if part == 0:
-            summed("PS", [("Ib", a), ("Nb", b)], True, True)
-            act(r1, v("PS"), AF.Relu)
-        elif part == 1:
-            summed("PT", [("Ib", c), ("Nb", d)], True, True)
-            act(r2, v("PT"), AF.Relu)
-        elif part == 2:
-            if t == RO:
-                summed("PF", [("Ib", a), ("Ib", b)], True, False)
+        bank, terms = [("PS", [("Ib", a), ("Nb", b)]), ("PT", [("Ib", b), ("Nb", c), ("Ib", r1)]),
+                       ("PS", [("Ib", c), ("Nb", d), ("Ib", r2)]),
+                       ("PF", [("Rb", d), ("Rb", r3)] if t < RO else [("Ib", a), ("Ib", b), ("Ib", c), ("I3", d), ("Rb", r3)])][part]
+        done = ahead.get((t, part), 0)
+        upto = len(terms) if early is None else min(early, len(terms) - 1)
+        summed(bank, terms[done:upto], done == 0, early is None)
+        ahead[t, part] = max(done, upto)
+        if early is not None:
+            return
+        if part < 3:
+            act((r1, r2, r3)[part], v(bank), AF.Relu)
         else:
-            summed("PG", [("Ib", b), ("Nb", d), ("Ib", r1), ("Nb", r2)], True, True)
-            f1()
-            act(r3, v("PG"), AF.Relu)
-            summed("PF", [("Rb", d), ("Rb", r2), ("Rb", r3)] if t < RO else
-                   [("Ib", c), ("I3", d), ("Rb", r2), ("Rb", r3)], t < RO, True)
-            f2()
             act(mq(t, rank), v("PF"), AF.Identity)
             if t:
                 send([([cores[q]], eng3[q], "am%d" % t, [mq(t, rank)], [mq(t, rank)], 0) for q in eng3])
@@ -342,7 +372,7 @@ def rank_program(g, core, T, topo):
     def turned(k, c):
         mm(v("PD", c, c + 128), v("Ts", 128 * k, 128 * k + 128), v("Ih"), True, True)
 
-    def records(win, bank, f1=nothing, f2=nothing, f3=nothing, f4=nothing, f5=nothing, f6=nothing):
+    def records(win, bank, f1=nothing, f2=nothing, f3=nothing, f4=nothing, f5=nothing, f6=nothing, f7=nothing):
         r8 = (0, 8, 1)
         loc = v("loc", 8, 136)
         mm(v("PC", 0, 128), v("KI"), v("cz"), True, False)
@@ -353,56 +383,79 @@ def rank_program(g, core, T, topo):
         mm(v("PC", 0, 128), v("KN"), loc, False, True)
         mm(v("PG", 0, 128), v("KN"), loc, False, False)
         f1()
-        scan(v("Cs", 1, 129, rows=r8), v("PB", 0, 128, rows=r8), v("zer", 0, 128, rows=r8), 0.0)
+        scan(v("Cs", 1, 129, rows=r8), v("PB", 0, 128, rows=r8), v("rst", rows=r8), 0.0)
         mm(v("PG", 0, 128), v("Cs", 0, 128, rows=r8), v("Sel", rows=r8), False, True)
         tt(v("s3"), v("PC", 0, 128), loc, AL.max)
         f2()
         tt(v("s4"), v("PG", 0, 128), v("s3"), AL.max)
+        f7()
         scan(v("Q", rev=True), v("Bg", rev=True), v("s4", rev=True), 0.0, AL.max, AL.min)
         mm(v("PB", 0, 128), v("Q"), v("Ih"), True, True)
-        mm(v("PA", 0, 256), v("Z0"), v("cb"), True, False)
+        if AH[rnd[0] > 0]:
+            halves = True
+        else:
+            halves = win == "tB"
+        for pb in ("PA", "PG") if halves else ("PA",):
+            mm(v(pb, 0, 128), v("Z0"), v("cb"), True, False)
+        if FMO:
+            scan(v("Fr"), v("rsp"), v("Q"), 0.0, AL.add, AL.min)
+            tt(v("Fm"), v("Fr"), v("Mk"), AL.mult)
         f3()
+        if not FMO:
+            scan(v("Fr"), v("rsp"), v("Q"), 0.0, AL.add, AL.min)
         cp(v("Kr"), v("PB", 0, 128))
-        ts(v("Kf"), v("PB", 0, 128), 2049.0, AL.is_ge)
-        for (mx, kk) in (("mQ", "Kr"), ("mF", "Kf")):
-            for h in range(2):
-                mm(v("PA", h, 255 + h, 2), v(mx, 128 * h, 128 * h + 128), v(kk), False, kk == "Kf" and h == 1)
-        for k in range(8):
-            mm(v("PC", 0, 16), v("Eo", 14 - 2 * k, 142 - 2 * k), v("Kr", k, 121 + k, 8), k == 0, k == 7)
+        ts(v("Kf"), v("PB", 0, 128), thr, AL.is_ge)
+        if not FMO:
+            tt(v("Fm"), v("Fr"), v("Mk"), AL.mult)
+        mm(v("PA", 0, 128), v("mQ", 0, 128), v("Kr"), False, False)
+        mm(v("PA", 0, 128), v("mF", 0, 128), v("Kf"), False, True)
+        mm(v("PC", 0, 8), v("Fm"), v("B8"), True, True)
+        if halves:
+            for mx, kk in (("mQ", "Kr"), ("mF", "Kf")):
+                mm(v("PG", 0, 128), v(mx, 128, 256), v(kk), False, kk == "Kf")
         f4()
-        ts(v("val"), v("PA", 0, 256), 0.0, AL.max)
-        cp(v("l" + win), v("PC", 0, 16))
+        ts(v("val"), v("PA", 0, 128), 0.0, AL.max, bas[rnd[0] % 2], AL.add)
+        cp(v("l" + win), v("PC", 0, 8))
+        if halves and MID:
+            red(v("mid", 1, 2), v("PG", 0, 128), AL.max)
         f5()
         cp(ind(v(win), v("l" + win)), v("val"))
+        if halves and MID:
+            ts(v("mid", 0, 1), v("mid", 1, 2), c4, AL.max, bm4[rnd[0] % 2], AL.add)
         f6()
 
     def running(win, f1=nothing):
         for h in range(2):
-            a, b = (0, 1025) if h == 0 else (1025, W + 1)
-            scan(v("inv", a, b), v("dec", 0, b - a), v(win, a + 1, b + 1), v("mid", 0, 1) if h else 0.0, AL.add, AL.max)
-            if h == 0:
-                cp(v("mid", 0, 1), v("inv", b - 1, b))
+            a, b = 1024 * h, 1024 * h + 1024
+            scan(v("inv", a, b), v("dec", 0, b - a), v(win, a + 1, b + 1), v("mid", 0, 1) if h else bas[rnd[0] % 2], AL.add, AL.max)
+            if h == 0 and not MID:
+                red(v("mid", 1, 2), v("PG", 0, 128), AL.max)
+                ts(v("mid", 0, 1), v("mid", 1, 2), c4, AL.max, bm4[rnd[0] % 2], AL.add)
             counted("PB" if h else "PC", 64 * h, 64 * h + 64)
             if h == 0:
                 f1()
 
     def counted(bank, k0, k1):
-        for o in range(17):
-            em = v("TA", 15, 143) if o == 0 else v("TB", 0, 128) if o == 16 else v("EI", 15 - o, 143 - o)
-            mm(v(bank, k0, k1), em, v("inv", 16 * k0 + o, 16 * k1 + o - 15, 16), o == 0, o == 16)
+        for o in range(16):
+            mm(v(bank, k0, k1), v("EI", 15 - o, 143 - o), v("inv", 16 * k0 + o, 16 * k1 + o - 15, 16), o == 0, o == 15)
 
     def running_whole(win, f1=nothing):
-        scan(v("inv", 0, W + 1), v("dec", 0, W + 1), v(win, 1, W + 2), 0.0, AL.add, AL.max)
+        scan(v("inv", 0, W), v("dec", 0, W), v(win, 1, W + 1), bas[rnd[0] % 2], AL.add, AL.max)
         f1()
         counted("PC", 0, 128)
 
     def inv_half(o, c0, h):
-        cp(v(o, c0 + 64 * h, c0 + 64 * h + 64), v("PB" if h else "PC", 64 * h, 64 * h + 64))
+        ts(v(o, c0 + 64 * h, c0 + 64 * h + 64), v("PB" if h else "PC", 64 * h, 64 * h + 64), LIFT[rnd[0] % 2], AL.add)
 
-    def wipe(win, behind):
-        for h in range(2):
-            dma("S", v(win, 1032 * h, 1032 * h + 1032), v("zer", 0, 1032))
-            ops[-1]["after"] = [behind]
+    def inv_lists():
+        for n in ("l3u", "l3h"):
+            ts(v(n), v("PC", 0, 128), LIFT[rnd[0] % 2], AL.add)
+
+    def wipe(win):
+        iota(v(win, 0, W + 2), [[0, W + 2]], -4096, 0)
+
+    def turned_back(t, c0=0, c1=W):
+        return {"ap": T.md[t - 1, 0:128, c0:c1], "reg": [("md", ALLP, 32 * t, 32 * t + 32)]}
 
     def score(k, lname, l0, Ms, cuts):
         for c in range(len(cuts) - 1):
@@ -441,10 +494,15 @@ def rank_program(g, core, T, topo):
 
     def slopes(bank, f1=nothing, part=None):
         if part != 1:
-            act(v("a1"), v(bank, 256, 384), AF.Abs)
-            f1()
-            act(v("a3"), v("a1"), AF.Relu, bias=4.0, scale=-1.0)
-            act(v("a2"), v("PD", 0, 128), AF.Relu, bias=4.0, scale=-1.0)
+            if part is None:
+                act(v("a1"), v(bank, 256, 384), AF.Abs)
+                act(v("a2"), v("PD", 0, 128), AF.Relu, bias=4.0, scale=-1.0)
+                f1()
+                act(v("a3"), v("a1"), AF.Relu, bias=4.0, scale=-1.0)
+            else:
+                act(v("a1"), v(bank, 256, 384), AF.Abs)
+                act(v("a3"), v("a1"), AF.Relu, bias=4.0, scale=-1.0)
+                act(v("a2"), v("PD", 0, 128), AF.Relu, bias=4.0, scale=-1.0)
         if part == 0:
             return
         mm(v("PS", 0, 128), v("Ib"), v("cap"), True, False)
@@ -453,11 +511,9 @@ def rank_program(g, core, T, topo):
 
     dma("S", v("g32"), ext(T.gam[:]))
     dma("A", v("X"), ext(T.xs[:]))
-    iota(v("pi", 0, 2), [[112, 2]], 0, 1)
+    iota(v("pi", 0, 4), [[16, 2], [112, 2]], 0, 1)
     iota(v("iom"), [[1, 144]], 0, 0)
     iota(v("iog"), [[16, 8], [0, 16]], 0, 0)
-    iota(v("io8"), [[16, 8], [0, 2], [1, 8]], 0, 0)
-    iota(v("iod"), [[1, 8], [1, 2]], 0, 0)
     dma("S", v("e32"), ext(T.ew[:]))
     dma("S", v("rh", 0, 5), ext(T.rho[:]))
     send([([cores[prev]], e_prev, "ag", [v("g32")], [v("gn32")], 0)])
@@ -470,15 +526,16 @@ def rank_program(g, core, T, topo):
         for q, s in zip(near + far, ("ah0", "aq0", "ar0")):
             arrive(lq(0, q, rank), s, len(eng3[q]))
     ms(v("oh"), 1.0)
-    for (c, b, m) in [(0, 1, 15), (1, 2, 112), (3, 2, 127), (5, 1, 7)]:
+    for (c, b, m) in [(0, 1, 15), (1, 2, 112), (3, 3, 127)]:
         ts(v("pj", c, c + b), v("pi", 0, b), m, AL.bitwise_and)
     ms(v("rst"), 0.0)
     cp(v("pf", 0, 6), v("pj", 0, 6))
     ms(v("Bg"), 0.0)
-    pm, gb, gbp, pp, ppm, p8 = [v("pf", k, k + 1) for k in range(6)]
+    pm, gb, gbp, pp, ppm, ppn = [v("pf", k, k + 1) for k in range(6)]
     lo, hi = v("pf", 8, 9), v("pf", 12, 13)
-    gii, i0, c1, c2, eo, p4, p16 = [v("pg", k, k + 1) for k in range(7)]
-    z0, wa, wb, wd = v("wr", 5, 6), v("ab", 0, 1), v("ab", 1, 2), v("ab", 2, 3)
+    thr, c4, nz, p2, p16, nq, n32, wa, wd = [v("pg", k, k + 1) for k in range(9)]
+    bas, bm4 = [[v("pg", k, k + 1), v("pg", k + 1, k + 2)] for k in (10, 12)]
+    z0 = v("wr", 5, 6)
     ts(lo, pm, 8.0, AL.is_ge)
     ts(hi, pm, 8.0, AL.is_lt)
     ms(v("rst", 0, 113, 16), -4096.0)
@@ -486,70 +543,74 @@ def rank_program(g, core, T, topo):
     ts(z0, pm, 0.0, AL.is_equal)
     grp[0] = 1
     for i in range(16):
-        act(v("IW", i, W - 15 + i, 16), v("iom", 0, 128), AF.Identity, bias=v("ib", i, i + 1), scale=hi)
+        if i < IWD:
+            ts(v("IW", i, W - 15 + i, 16), v("iom", 0, 128), hi, AL.mult, v("ib", i, i + 1), AL.add)
+        else:
+            act(v("IW", i, W - 15 + i, 16), v("iom", 0, 128), AF.Identity, bias=v("ib", i, i + 1), scale=hi)
     grp[0] = 0
-    ms(v("zer"), 0.0)
-    wipe("tA", len(ops) - 1)
-    ts(wd, lo, -KK, AL.mult, z0, AL.add)
+    wipe("tA")
+    wipe("tB")
+    ts(nz, pm, 0.0, AL.not_equal)
     ts(p16, pp, 16.0, AL.mult)
-    ts(wd, wd, hi, AL.subtract)
-    act(v("dec", 0, 1032), v("zer", 0, 1032), AF.Identity, bias=wd)
-    dma("S", v("dec", 1032, 2064), v("dec", 0, 1032))
+    ts(wd, nz, -1.0 / 256, AL.mult)
+    ts(bas[0], nz, REST + W, AL.mult, -1.0 * W, AL.add)
+    ts(bas[1], nz, REST + STEP, AL.mult)
     ts(v("Ih"), v("iom", 0, 128), pp, AL.is_equal)
     ts(v("KI"), v("iom", 0, 128), pp, AL.is_equal, KK, AL.mult)
     ts(v("Rot"), v("iom", 0, 128), ppm, AL.is_equal)
     ts(v("KN"), v("iom", 0, 128), pp, AL.is_equal, -KK, AL.mult)
     ts(v("cz"), v("rst"), 0.5, AL.add)
+    cp(v("gu"), v("g32"))
     ms(v("loc", 0, 8), 0.0)
     ms(v("Cs", 0, 8), 0.0)
-    ts(p4, pp, 4.0, AL.mult, 2066.0, AL.add)
-    ts(i0, p8, 0.0, AL.is_equal)
-    ts(gii, gb, p8, AL.add)
+    ts(p2, pp, 2.0, AL.mult, 2050.0, AL.add)
+    ts(thr, z0, 1024.5 - 2049.0, AL.mult, 2049.0, AL.add)
+    ts(nq, nz, 1.0 / 256, AL.mult)
     ts(v("Sel"), v("iog"), p16, AL.is_equal, KK, AL.mult)
-    ts(v("Bg", 7, 128, 8), v("iod"), -2.0, AL.mult, p4, AL.add)
-    cp(v("gu"), v("g32"))
-    cp(v("eu"), v("e32"))
+    ts(v("Bg", 15, 128, 16), v("Bg", 15, 128, 16), p2, AL.add)
     gat("A", v("Wc"), v("IW"), v("gu"))
-    gat("A", v("D1"), v("X"), v("eu", 0, 128))
-    ts(c2, i0, -1.0, AL.add)
-    ts(eo, gb, lo, AL.add)
-    ts(v("s3"), v("io8"), gii, AL.is_equal)
-    ts(v("s4"), v("iog"), gb, AL.is_equal, i0, AL.mult)
-    ts(c1, c2, KK, AL.mult)
-    ts(v("E"), v("iom"), -14.0, AL.add, eo, AL.is_equal)
-    tt(v("s4"), v("s3"), v("s4"), AL.subtract)
-    ts(v("s1"), v("iom", 0, 128), gb, AL.is_equal, c2, AL.mult)
-    ts(v("s3"), v("s3"), c1, AL.mult)
-    ts(v("Eo"), v("E"), i0, AL.mult)
-    ts(v("Z0"), v("iom", 0, 128), pp, AL.is_equal, z0, AL.mult)
-    tt(v("s3"), v("s3"), v("s1"), AL.add)
-    for (mx, base) in (("mQ", "s4"), ("mF", "s3")):
-        for h in range(2):
-            ts(v(mx, 128 * h, 128 * h + 128), v(base), lo if h else hi, AL.mult)
-    for h in range(2):
-        ts(v("cb", 128 * h, 128 * h + 128), v("iom", 0, 128), 8.0, AL.mult, 7.0 + 1024 * h, AL.add)
-    ts(wa, z0, 2.0, AL.mult, hi, AL.subtract)
-    ts(wb, pm, 9.0, AL.is_ge, z0, AL.add)
     ts(v("E"), v("iom"), -15.0, AL.add, gb, AL.is_equal)
-    ts(wb, wb, -1.0, AL.mult, hi, AL.add)
-    ts(v("TA"), v("E"), wa, AL.mult)
-    ts(v("TB"), v("E"), wb, AL.mult)
+    ts(v("Kr"), v("iog"), gb, AL.is_equal, z0, AL.mult)
+    ts(v("Kf"), v("Ih"), 32.0, AL.mult)
+    ts(n32, nz, -1.0, AL.mult)
+    tt(v("Fr"), v("iom", 0, 128), v("iog"), AL.subtract)
+    ts(v("rsp"), v("rst"), -1.0, AL.mult)
+    ts(v("B8"), v("iog", 0, 113, 16), gb, AL.is_equal)
+    tt(v("Q"), v("Ih"), v("Kr"), AL.subtract)
+    tt(v("Kf"), v("Kf"), v("E", 15, 143), AL.add)
+    ts(v("Mk"), v("Fr"), pm, AL.is_equal)
+    ts(v("Z0"), v("Ih"), z0, AL.mult)
+    ts(v("mQ", 0, 128), v("Q"), 1.0 / 256, AL.mult)
+    ts(v("mF", 0, 128), v("Kf"), n32, AL.mult)
+    cp(v("eu", 0, 128), v("e32", 0, 128))
+    gat("A", v("D1", 16 * D0D, W), v("X"), v("eu", D0D, 128))
+    ts(v("cb"), v("iom", 0, 128), 16.0, AL.mult, 15.0, AL.add)
+    ts(wa, z0, 17.0 / 16, AL.mult, -1.0 / 16, AL.add)
+    ts(v("Fm"), v("Kr"), KK, AL.mult)
+    ts(c4, nz, 4.0, AL.mult)
+    ts(v("EI"), v("E"), wa, AL.mult)
+    tt(v("mF", 128, 256), v("mF", 0, 128), v("Fm"), AL.subtract)
+    ts(v("Ib"), v("iom", 0, 128), pp, AL.is_equal)
+    ts(v("Nb"), v("iom", 0, 128), pp, AL.is_equal, -1.0, AL.mult)
+    cp(v("Rb"), v("Rot"))
+    if D0D:
+        gat("D", v("D1", 0, 16 * D0D), v("X"), v("eu", 0, D0D))
     cp(v("gnh"), v("gn32"))
 
     def mid_constants():
-        tt(v("EI", 0, 143), v("TA", 0, 143), v("TB", 1, 144), AL.add)
-        ts(v("Ib"), v("iom", 0, 128), pp, AL.is_equal)
-        ts(v("Nb"), v("iom", 0, 128), pp, AL.is_equal, -1.0, AL.mult)
-        cp(v("Rb"), v("Rot"))
+        ts(v("mQ", 128, 256), v("Ih"), nq, AL.mult)
+        ts(v("pg", 12, 14), v("pg", 10, 12), c4, AL.subtract)
 
-    def sum_constants():
-        ms(v("acc"), 0.0)
-        ts(v("GM"), v("iog"), gb, AL.is_equal)
-        ts(v("tie"), v("iom", 0, 4), 4.0, AL.add, 1.0 / 64, AL.mult)
+    def sum_constants(n):
+        if n:
+            ts(v("GM"), v("iog"), gb, AL.is_equal)
+        else:
+            ms(v("acc"), 0.0)
+            ts(v("tie"), v("iom", 0, 4), 4.0, AL.add, 1.0 / 64, AL.mult)
 
     def mid_constants2():
         ts(v("l0"), v("iom", 0, 128), 16.0, AL.mult, pm, AL.add)
-        cp(v("eh"), v("e32"))
+        cp(v("eh", 0, 128), v("e32", 0, 128))
         ms(v("ob", 0, 128), 1.0)
         ms(v("ob", 128, 384), 0.0)
         ts(v("wr", 0, 4), v("iom", 0, 4), pm, AL.is_equal, 16.0, AL.mult)
@@ -574,6 +635,7 @@ def rank_program(g, core, T, topo):
         ms(v("cap"), 24.0)
 
     def late_constants():
+        ts(v("Rk"), v("iom", 0, 128), ppn, AL.is_equal)
         ts(v("I3"), v("Ib"), 3.0, AL.mult)
         ts(v("N5"), v("Ib"), -5.0, AL.mult)
         ms(v("tab"), 0.0)
@@ -591,8 +653,18 @@ def rank_program(g, core, T, topo):
     for t in range(RO):
         last = t == RO - 1
         rnd[0] = t
-        Ms = ("Ms", 0) if t else ("Mp", 0)
-        Mu = "Mu%d" % (t % 2)
+        Ms = ("Ms", W * (t - 1)) if t else ("Mp", 0)
+        land = [rank] + near + far if not (t and MSH) else mine + [q for q in range(4) if q not in mine]
+        vo = "V%d" % (t % 2)
+        vi = v("pb") if t == 1 else v("V%d" % ((t + 1) % 2))
+        made, carried, landed, begun, ended, less, summed = [0], [0], [], {}, set(), set(), []
+
+        def factors(k1):
+            k0 = made[0]
+            if t > 0 and k1 > k0:
+                gat("A", v("R", 16 * k0, 16 * k1), v("tab", 0 if t == 1 else 32, 32 if t == 1 else 64), v("ixu", k0, k1))
+                made[0] = k1
+
         def xq(q, k0, k1):
             gat(q, v("X", 16 * k0, 16 * k1), v("Xp"), v("muu", k0, k1))
 
@@ -600,146 +672,283 @@ def rank_program(g, core, T, topo):
             for n in names:
                 ts(v(n), v("PD", 256, 384), -1.0, AL.add)
 
+        def msq(q):
+            return v("Ms", Ms[1] + 512 * q, Ms[1] + 512 * q + 512)
+
+        def template(n, e):
+            q = land[n]
+            if MSH == 3:
+                mh, oh = [v("Ms", Ms[1] + 512 * land[k], Ms[1] + 512 * land[k] + 1024) for k in (0, 2)]
+                if n == 0:
+                    gat(e, mh, v("Mp", W * t, W * t + W), v("msu", 0, 64))
+                    post(near[0], "aw%d" % (3 * t - 3), mh, mh, oh)
+                landed[:] = [len(ops) - 1]
+                return
+            gat(e, msq(q), v("Mp", W * t, W * t + W), v("msu", 32 * n, 32 * n + 32))
+            if MSH == 2:
+                pass
+            elif MSH:
+                send([([cores[near[0]]], e_near, "aw%d" % (3 * t - 3 + n), [msq(q)], [msq(q)], 0)])
+                arrive(msq(land[2 + n]), "aw%d" % (3 * t - 3 + n), len(e_near))
+            else:
+                spread(lambda q: msq(rank), lambda q: msq(rank), msq, ["aw%d" % (3 * t - 3 + k) for k in range(3)], SW)
+            landed[:] = [len(ops) - 1]
+
+        def quiet():
+            if t > 1:
+                dma("G", v("V%d" % ((t + 1) % 2)), turned_back(t - 1), acc=True)
+                ops[-1]["after"] = list(landed)
+            if t > 0 and (len(VA) > 1 or not last):
+                dma("S", dr("md", T.md[t - 1, 16:144, :], 2 * t), v("Ms", Ms[1], Ms[1] + W))
+                dma("S", dr("md", T.md[t - 1, 0:16, :], 2 * t + 1), v("Ms", Ms[1], Ms[1] + W, rows=(112, 128, 1)))
+            if t in (1, 2):
+                wipe("tA" if t == 1 else "tB")
+
+        def curve(k, c0, c1):
+            return v(("X", "D1", "D2", "D3")[k], c0, c1)
+
+        def runs(a, b):
+            out = []
+            for n in range(a // 32, (b + 31) // 32):
+                k0, k1 = [32 * land[n] + x for x in (max(a - 32 * n, 0), min(b - 32 * n, 32))]
+                if out and out[-1][1] == k0:
+                    out[-1][1] = k1
+                else:
+                    out.append([k0, k1])
+            return out
+
+        barred = set("AGBDC")
+
+        def begin(k, n, bank=""):
+            while not bank:
+                rot = [b for b in ROT if b not in barred]
+                turn[0] = (turn[0] + 1) % len(rot)
+                assert any("P" + b not in held for b in rot)
+                bank = "" if "P" + rot[turn[0]] in held else rot[turn[0]]
+            begun[k, n] = "P" + bank
+            mm(v(begun[k, n]), v("Ib"), curve(k, 512 * land[n], 512 * land[n] + 512), True, False)
+            held.add(begun[k, n])
+
+        def trials(names):
+            for s in names.split():
+                if s[0] == "g":
+                    k, (a, b) = int(s[1]), [int(x) for x in s[3:].split(":")]
+                    for k0, k1 in runs(a, b):
+                        l0 = 128 * t if k == 1 else 0
+                        gat(s[2], curve(k, 16 * k0, 16 * k1), v("X"), v(("", "eu", "l2u", "l3u")[k], l0 + k0, l0 + k1))
+                elif s[0] == "t":
+                    k, n, m = int(s[1]), int(s[2]), int(s[-1])
+                    less.update((k, x) for x in range(n, m + 1))
+                    for cut in runs(32 * n, 32 * m + 32):
+                        score(k, "l%du" % k, 0, Ms, cut)
+                elif s[0] == "a":
+                    k, n = int(s[1]), int(s[2])
+                    (k0, k1), = runs(32 * n, 32 * n + 64)
+                    d = curve(k, 16 * k0, 16 * k1)
+                    if s[3] == "A":
+                        act(d, d, AF.Abs, acc=acc(n, k))
+                    else:
+                        absred(acc(n, k), d)
+                elif s[0] == "p":
+                    begin(int(s[1]), int(s[2]), s[3:])
+                elif s[0] in "sq":
+                    k, n = int(s[1]), int(s[2])
+                    o = 512 * land[n]
+                    if (k, n) in less:
+                        d = out = curve(k, o, o + 512)
+                    else:
+                        if (k, n) not in begun:
+                            begin(k, n)
+                        d, out = v(begun[k, n]), v("D0", 512 * (len(ended) % 4), 512 * (len(ended) % 4) + 512)
+                        if (k, n) not in ended:
+                            mm(d, v("Nb"), v(Ms[0], Ms[1] + o, Ms[1] + o + 512), False, True)
+                            ended.add((k, n))
+                    if s[0] == "q":
+                        continue
+                    held.discard(begun.get((k, n)))
+                    if s[3] == "A":
+                        act(out, d, AF.Abs, acc=acc(n, k))
+                    else:
+                        absred(acc(n, k), d)
+                elif s[0] == "G":
+                    if not summed:
+                        mm(v("PB", 0, 4), v("GM"), v("tie"), True, False)
+                    summed.append(s)
+                    mm(v("PB", 0, 4), v("GM"), acc(int(s[1]), 0, 4), False, len(summed) == 4)
+                elif s[0] == "M":
+                    if int(s[1]) < len(mine):
+                        template(int(s[1]), s[2:] or "A")
+                elif s[0] == "m":
+                    fold("X", 0, int(s[1]))
+                elif s[0] == "r":
+                    factors(int(s[1:]))
+                elif s[0] == "E":
+                    c = 1024 * int(s[1])
+                    if s[2] == "A":
+                        act(v("dec", c, c + 1024), v("X", c, c + 1024), AF.Identity, bias=wd, scale=0.0)
+                    else:
+                        ts(v("dec", c, c + 1024), v("X", c, c + 1024), 0.0, AL.mult, wd, AL.add)
+                elif s[0] in "ZCL" and s[1:]:
+                    n = int(s[1])
+                    h, bank = land[2 * n] // 2 if t else n, ("PC", "PB")[n]
+                    if s[0] == "Z":
+                        scan(v("inv", 1024 * h, 1024 * h + 1024), v("dec", 0, 1024), v("tA", 1024 * h + 1, 1024 * h + 1025),
+                             v("mid", 0, 1) if h else bas[t % 2], AL.add, AL.max)
+                    elif s[0] == "C":
+                        counted(bank, 64 * h, 64 * h + 64)
+                    else:
+                        for x in ("l3u", "l3h"):
+                            ts(v(x, 64 * h, 64 * h + 64), v(bank, 64 * h, 64 * h + 64), LIFT[t % 2], AL.add)
+                        barred.discard("CB"[n])
+                elif s == "C":
+                    counted("PC", 0, 128)
+                elif s == "L":
+                    inv_lists()
+                    barred.discard("C")
+                elif s[0] == "+":
+                    barred.difference_update(s[1:])
+                elif s[0] == "-":
+                    barred.update(s[1:])
+                elif s == "Q":
+                    quiet()
+                elif s == "I":
+                    dma("S", v("Wc", rows=(1, 128, 8)), v("IW", rows=(1, 128, 8)))
+                elif s == "K":
+                    mid_constants2()
+                    dma("S", v("pb"), ext(T.pay[:]))
+                    ops[-1]["after"] = [len(ops) - 2]
+                elif s == "S0":
+                    cp(v("muf", 0, 128), v("muu"))
+                elif s == "S1":
+                    cp(v("Ts", 128, 256), v("PF", 128, 256))
+                elif s == "S2":
+                    mu_slope()
+                    turned(1, 384)
+                    slopes("PF", part=0)
+                elif s == "S3":
+                    slopes("PF", part=1)
+                elif s == "S4":
+                    cp(v("ixu"), v("PS", 0, 128))
+                elif s == "S5":
+                    cp(v("du"), v("PD", 384, 512))
+
+        plan = TRIALS[t > 0]
         if t > 0:
             blocks("Wc", v("S3", 0, 24), 3, "PF")
-            ts(v("msu"), v("PD", 128, 256), -0.375, AL.add)
-            xq("D", 128 - XD, 128)
-            xq("A", 0, 128 - XD)
-
-            def drawn(q, k0, k1):
-                if k1 > k0:
-                    gat(q, v("D1", 16 * k0, 16 * k1), v("X"), v("eu", 128 * t + k0, 128 * t + k1))
-
-            records("tA", "PF", f1=lambda: cp(v("Ts", 0, 128), v("PF", 0, 128)), f2=lambda: turned(0, 256),
-                    f3=lambda: drawn("D", 128 - DE, 128 - DE // 2), f4=lambda: drawn("D", 128 - DE // 2, 128),
-                    f5=lambda: lists2("l2u"), f6=lambda: lists2("l2h"))
-            drawn("A", 0, DD)
-            for a, b in ((0, 64), (64, 128 - MD)):
-                gat("A", v("Ms", 16 * a, 16 * b), v("Mp", W * t, W * t + W), v("msu", a, b))
-            drawn("A", DD, 128 - DE)
-            if MD:
-                gat("D", v("Ms", W - 16 * MD, W), v("Mp", W * t, W * t + W), v("msu", 128 - MD, 128))
-            dma("S", v(Mu, rows=(16, 128, 1)), v("Ms", rows=(0, 112, 1)))
-            dma("S", v(Mu, rows=(0, 16, 1)), v("Ms", rows=(112, 128, 1)))
-            running_whole("tA", lambda: [stay(c, Ms) for c in range(SE)])
+            ts(v("msu", 0, 32 * len(mine)), v("PD", 128, 128 + 32 * len(mine)), -0.375, AL.add)
+            xd = XD[t > 1]
+            if xd:
+                xq("D", 128 - xd, 128)
+            xq("A", 0, 128 - xd)
+            trials(plan[0])
+            records("tA", "PF", f1=lambda: (cp(v("Ts", 0, 128), v("PF", 0, 128)), trials(plan[1])),
+                    f2=lambda: (turned(0, 256), trials(plan[2])), f7=lambda: trials(plan[3]), f3=lambda: trials(plan[4]),
+                    f4=lambda: trials(plan[5]), f5=lambda: (lists2("l2u"), trials(plan[6])),
+                    f6=lambda: (lists2("l2h"), trials(plan[7])))
         else:
             mm(v("PA", 0, 128), v("Ih"), v("oh"), True, False)
             mm(v("PA", 0, 128), v("gnh"), v("Rot"), False, True)
             mm(v("PD", 256, 384), v("Ih"), v("oh"), True, False)
             mm(v("PD", 256, 384), v("Rot"), v("gnh"), False, True)
-            records("tA", "PA", f1=mid_constants, f2=lambda: fold("X", 0, 0), f3=lambda: (lists2("l2u", "l2h"), fold("X", 0, 1)),
-                    f4=sum_constants)
-            d2 = [lambda k=k: gat("A", v("D2", 512 * k, 512 * k + 512), v("X"), v("l2u", 32 * k, 32 * k + 32))
-                  for k in [rank] + near + far]
-            fold("X", 0, 3, d2[0], d2[1])
-            running_whole("tA", lambda: stay(rank, Ms))
-            for k in range(2, 4):
-                d2[k]()
-            mid_constants2()
-            dma("S", v("pb"), ext(T.pay[:]))
-            ops[-1]["after"] = [len(ops) - 2]
-        dma("S", v("Wc", rows=(1, 128, 8)), v("IW", rows=(1, 128, 8)))
-        if t > 0:
-            score(2, "l2u", 0, Ms, H2[:2])
-            n = len(ops) - 1
-            wipe("tB", n)
-            if not last:
-                wipe("tA", n)
-            if AE:
-                absum(2, H2, [0])
-            for c in range(SE, 4):
-                stay(c, Ms)
-            score(2, "l2u", 0, Ms, H2[1:])
-            cp(v("l3u"), v("PC", 0, 128))
-            cp(v("l3h"), v("PC", 0, 128))
-            for c in range(4):
-                stay(c, Ms, "D1", 1)
-            mm(v("PB", 0, 4), v("GM"), v("tie"), True, False)
-            score(3, "l3u", 0, Ms, C3)
-            cp(v("muf", 0, 128), v("muu"))
-            if not AE:
-                absum(2, H2, [0])
-            absum(3, C3, [0])
-            absum(3, C3, [2, 1], "D")
-            absum(2, H2, [1])
-        else:
-            cp(v("l3u"), v("PC", 0, 128))
-            cp(v("l3h"), v("PC", 0, 128))
-            mm(v("PB", 0, 4), v("GM"), v("tie"), True, False)
-            for c in [rank] + near + far:
-                score(3, "l3u", 0, Ms, Q4[c:c + 2])
-                if c == far[0]:
-                    n = len(ops) - 1
-                    wipe("tB", n)
-                    wipe("tA", n)
-                for (src, k) in ready if c != rank else ready[1:]:
-                    stay(c, Ms, src, k, "D" if k == 2 and c in (near + far)[:ZD] else "A")
-                absum(3, Q4, [c], "D")
-        sums = (3, 0, 2, 1) if t else [rank] + near + far
-        if t > 0:
-            cp(v("Ts", 128, 256), v("PF", 128, 256))
-        for c in sums:
-            mm(v("PB", 0, 4), v("GM"), acc(c, 0, 4), False, c == sums[3])
-        if t > 0:
-            mu_slope()
-            turned(1, 384)
-            slopes("PF", part=0)
+            trials(plan[0])
+            records("tA", "PA", f1=lambda: (lists2("l2u", "l2h"), trials(plan[1])), f2=lambda: trials(plan[2]),
+                    f7=lambda: (mid_constants(), trials(plan[3])), f3=lambda: trials(plan[4]), f4=lambda: trials(plan[5]),
+                    f5=lambda: (sum_constants(0), trials(plan[6])), f6=lambda: (sum_constants(1), trials(plan[7])))
+        if not AH[t > 0]:
+            scan(v("inv", 0, W), v("dec", 0, W), v("tA", 1, W + 1), bas[t % 2], AL.add, AL.max)
+        trials(plan[8])
         red(v("mn", 0, 1), v("PB", 0, 4), AL.min)
+        trials(plan[9])
         for k in range(4):
             ts(v("dg", 128 * k, 128 * k + 128), v("Ih"), v("PB", k, k + 1), AL.mult, v("mn", 0, 1), AL.is_equal)
         for k, l in enumerate([v("l0"), v("eh", 128 * t, 128 * t + 128), v("l2h"), v("l3h")]):
             mm(v("PA", 0, 128), v("dg", 128 * k, 128 * k + 128), l, k == 0, k == 3)
-        if t > 0:
-            slopes("PF", part=1)
+        trials(plan[10])
         cp(v("cu"), v("PA", 0, 128))
-        for h, e in enumerate("DA"):
-            gat(e, v("Wm", 1024 * h, 1024 * h + 1024), v("Wc"), v("cu", 64 * h, 64 * h + 64))
+        trials(plan[11])
+        for e, a, b in (("D", 0, WD), ("A", WD, 128)):
+            gat(e, v("Wm", 16 * a, 16 * b), v("Wc"), v("cu", a, b))
         if not last:
             dma("S", dr("st", T.st[t], t), v("Wm", 0, W, rows=(0, 128, 8)))
         blocks("Wm", v("S3", 24, 32), 1)
-        if t > 0:
-            cp(v("ixu"), v("PS", 0, 128))
-            cp(v("du"), v("PD", 384, 512))
-        for q, sem in zip(far, ("aq%d", "ar%d")):
-            gat("A", v("Xp", 512 * q, 512 * q + 512), v("X"), v("cu", 32 * q, 32 * q + 32))
-            quarter(t + 1, q, e_far, sem % (t + 1))
-        act(v("Wm", W, W + 1), v("Wm", W - 1, W), AF.Identity, bias=lo)
-        vo = "V%d" % (t % 2)
-        vi = v("pb") if t == 1 else v("V%d" % ((t + 1) % 2))
+        trials(plan[12])
 
-        def factors(k0, k1):
+        def carry(k1):
+            k0 = carried[0]
             if t > 0 and k1 > k0:
-                gat("A", v("R", 16 * k0, 16 * k1), v("tab", 0 if t == 1 else 32, 32 if t == 1 else 64), v("ixu", k0, k1))
-
-        def carry(k0, k1):
-            if k1 > k0:
+                factors(k1)
                 tt(v(vo, 16 * k0, 16 * k1), ind(vi, v("du", k0, k1)), v("R", 16 * k0, 16 * k1), AL.mult)
+                carried[0] = k1
+                for a, b in zip(VA, VA[1:]):
+                    if last and k0 < b <= k1:
+                        dma("G", v(vo, 16 * a, 16 * b), turned_back(t, 16 * a, 16 * b), acc=True)
 
-        dma("S", v("Wm", 0, W, rows=(2, 128, 8)), v("Wm", 1, W + 1, rows=(1, 128, 8)))
-        if not last:
-            send([([cores[prev]], e_prev, "an%d" % t, [dr("st", T.st[t], t)], [dr("ld", T.ld[t], t)], 0)])
-            arrive(dr("ld", T.ld[t], t), "an%d" % t, n_next)
-            dma("S", v("Wm", 0, W, rows=(3, 128, 8)), dr("ld", T.ld[t], t))
-        for q in (near[0], rank):
-            gat("A", v("Xp", 512 * q, 512 * q + 512), v("X"), v("cu", 32 * q, 32 * q + 32))
-        quarter(t + 1, near[0], e_near, "ah%d" % (t + 1))
-        if t == 0:
-            records("tB", "PA", f1=mean_constants, f2=lambda: row_constants([(8, 1)]),
-                    f3=lambda: row_constants([(16, 4), (32, 1), (40, 0)]),
-                    f4=lambda: (row_constants([(48, 4)]), slope_constants()))
-        else:
-            records("tB", "PA")
-        factors(0, 64)
-        factors(64, 128)
+        def back(n):
+            mm(v(("PG", "PB")[n % 2]), v("Rk"), msq(n), True, True)
+
+        def added(n):
+            tt(v(vo, 512 * n, 512 * n + 512), v(("PG", "PB")[n % 2]), v(vo, 512 * n, 512 * n + 512), AL.add)
+
+        def elected(q, k0=0, k1=32, e="A", hold=False):
+            if k1 > k0:
+                gat(e, v("Xp", 512 * q + 16 * k0, 512 * q + 16 * k1), v("X"), v("cu", 32 * q + k0, 32 * q + k1))
+            if k1 == 32 and q != rank and e == "A":
+                post(q, ("ah%d", "aq%d", "ar%d")[(near + far).index(q)] % (t + 1), v("Xp", 512 * q, 512 * q + 512),
+                     lq(t + 1, rank, q), lq(t + 1, q, rank), hold)
+
+        def neighbours():
+            act(v("Wm", W, W + 1), v("Wm", W - 1, W), AF.Identity, bias=lo)
+            dma("S", v("Wm", 0, W, rows=(2, 128, 8)), v("Wm", 1, W + 1, rows=(1, 128, 8)))
+            if not last:
+                send([([cores[prev]], e_prev, "an%d" % t, [dr("st", T.st[t], t)], [dr("ld", T.ld[t], t)], 0)])
+                arrive(dr("ld", T.ld[t], t), "an%d" % t, n_next)
+                dma("S", v("Wm", 0, W, rows=(3, 128, 8)), dr("ld", T.ld[t], t))
+
+        def steps(names):
+            for s in names.split():
+                n = int(s[1:] or 0)
+                if s[0] in "xh":
+                    elected((far + near + [rank])[n], XB[last] if n == XQ else 0, hold=s[0] == "h")
+                elif s[0] == "d":
+                    elected(far[XQ], 0, XB[last], "D")
+                elif s[0] == "n":
+                    neighbours()
+                elif s[0] == "r":
+                    factors(n)
+                    if t == 0 and n > made[0]:
+                        act(v("p4", 16 * made[0], 16 * n), v("pb", 16 * made[0], 16 * n), AF.Identity, scale=0.25)
+                        made[0] = n
+                elif s[0] == "e":
+                    if not last:
+                        cp(v(("eu", "eh")[n], 128 * t + 128, 128 * t + 256), v("e32", 128 * t + 128, 128 * t + 256))
+                elif s[0] == "S":
+                    if t > 0:
+                        trials(s)
+                elif s[0] == "v":
+                    carry(n)
+                elif s[0] == "k":
+                    fold("Xp", t + 1, n // 10, n % 10)
+                elif s[0] == "b":
+                    back(n)
+                elif s[0] == "a":
+                    added(n)
+                else:
+                    fold("Xp", t + 1, n)
+
+        plan = PLAN[last]
         if last:
             ts(v("Rb"), v("Ib"), 2.0, AL.mult)
-        fold("Xp", t + 1, 0)
-        fold("Xp", t + 1, 2)
-        if FM:
-            running("tB", lambda: fold("Xp", t + 1, 1))
+        steps(plan[0])
+        if t == 0:
+            records("tB", "PA", f1=mean_constants, f2=lambda: row_constants([(8, 1)]), f7=lambda: row_constants([(16, 4), (32, 1)]),
+                    f3=lambda: row_constants([(40, 0), (48, 4)]), f4=slope_constants)
         else:
-            running("tB")
-            fold("Xp", t + 1, 1)
+            records("tB", "PA", *[lambda k=k: steps(plan[k]) for k in (1, 2, 4, 5)], f7=lambda: steps(plan[3]))
+        if t == 0:
+            steps(" ".join(plan[1:6]))
+        steps(plan[6])
+        running("tB", lambda: steps(plan[7]))
+        steps(plan[8])
 
         def li(h, s):
             c = 384 * t + 192 * h + 64 * s
@@ -750,38 +959,36 @@ def rank_program(g, core, T, topo):
             inv_half("ivh", 128 * t, h)
             send([([cores[q]], eng3[q], "ai%d" % (2 * t + h), [iv[h]], [li(h, slot(rank, q))], 0) for q in eng3])
             add("-", "arr", None, [], [li(h, s) for s in range(3)], tok=("ai%d" % (2 * t + h), n3))
-            if t == 0 and h == 0:
-                ts(v("p4"), v("pb"), 0.25, AL.mult)
-            if t > 0:
-                for a, b in [(0, 32)] if h == 0 else [(32, 64), (64, 128)] if last else [(32, 128)]:
-                    carry(a, b)
-                    if last and a:
-                        dma("G", v(vo, 16 * b - 1024, 16 * b), v(Mu, 16 * b - 1024, 16 * b), acc=True)
+            steps(plan[9 + h])
         if t == 0:
             late_constants()
         def mean(h):
             for k, x in enumerate([iv[h]] + [li(h, s) for s in range(3)]):
                 mm(v("PC" if h else "PD", 0, 64), v("Iq"), x, k == 0, k == 3)
 
-        fold("Xp", t + 1, 3)
-        if t > 0 and not last:
-            dma("G", v(vo), v(Mu), acc=True)
         for h in range(2):
             bank = v("PC" if h else "PD", 0, 64)
             mean(h)
             ts(v("muu", 64 * h, 64 * h + 64), bank, -0.375, AL.add)
-            for u in range(2) if h and not last else []:
-                for k, x in enumerate([iv[u]] + [li(u, s) for s in range(3)]):
-                    mm(v("PD", 128 + 64 * u, 192 + 64 * u), v("Pq"), x, k == 0, k == 3)
-            for k, e in enumerate("DA"):
+            steps(plan[11 + 2 * h])
+            if h and not last:
+                n = min(64, 32 * len(mine))
+                for u, q in enumerate(mine[::2]):
+                    for k in range(4):
+                        c0 = 128 * t + 32 * q if k == 0 else 384 * t + 192 * (q // 2) + 64 * (k - 1) + 32 * (q % 2)
+                        mm(v("PD", 128 + 64 * u, 128 + 64 * u + n), v("Pq"), v("li" if k else "ivh", c0, c0 + n), k == 0, k == 3)
+            for k, e in enumerate(WE[0 if t == 0 else 2 if last else 1][2 * h:2 * h + 2]):
                 q = 2 * h + k
                 gat(e, v("Wc", 512 * q, 512 * q + 512), v("Wm", 0, W), v("muu", 32 * q, 32 * q + 32))
+            steps(plan[12 + 2 * h])
 
     order = far + near + [rank]
     cp(v("muf", 0, 128), v("muu"))
     blocks("Wc", v("S3", 32, 56), 3)
     mu_slope()
+    steps(plan[15])
     slopes("PA", lambda: cp(v("Ts", 0, 256), v("PA", 0, 256)))
+    steps(plan[16])
     turned(0, 256)
     turned(1, 384)
     cp(v("ixu"), v("PS", 0, 128))
@@ -794,33 +1001,54 @@ def rank_program(g, core, T, topo):
     def lst(name, q, h=None):
         return v(name, 32 * q, 32 * q + 32) if h is None else v(name, 32 * q + 16 * h, 32 * q + 16 * h + 16)
 
-    for n, (k, h) in enumerate([(0, 0), (0, 1), (1, None)]):
-        q = far[k]
-        gat("A", part("R", q, h), v("tab", 64, 96), lst("ixu", q, h))
-        tt(part("V0", q, h), ind(v("V1"), lst("du", q, h)), part("R", q, h), AL.mult)
-        tt(part("Tg", k, h), ind(v("p4"), lst("gpu", q, h)), part("V0", q, h), AL.add)
-        trs = [([cores[q]], e_far, "af%d" % n, [part("Tg", k, h)], [part("lf", slot(rank, q), h)], 0)]
-        if n == 1:
-            gat("A", part("D1", near[0]), v("p4"), lst("gpu", near[0]))
-            trs.append(([cores[near[0]]], e_near, "ap", [part("D1", near[0])], [part("D2", 0)], 0))
-        send(trs)
-        arrive(part("lf", slot(q, rank), h), "af%d" % n, len(e_far))
-    for q in order[2:]:
-        gat("A", part("R", q), v("tab", 64, 96), lst("ixu", q))
-        tt(part("V0", q), ind(v("V1"), lst("du", q)), part("R", q), AL.mult)
-        if q in near:
-            send([([cores[q]], e_near, "af4", [part("V0", q)], [part("lf", slot(rank, q))], 0)])
-    gat("A", part("D1", rank), v("p4"), lst("gpu", rank))
-    gat("A", v("Mg"), v("Mp", 4 * W, 5 * W), lst("muu", rank), scale=1.0 / 64)
-    arrive(part("D2", 0), "ap", len(e_near))
-    arrive(part("lf", slot(near[0], rank)), "af4", len(e_near))
-    terms = [part("D2", 0), part("D1", rank), v("Mg")]
-    for k, x in enumerate(terms):
-        mm(v("PB"), v("Ib"), x, k == 0, k == len(terms) - 1)
-    tt(v("PB"), v("PB"), part("V0", rank), AL.add)
-    for q in (far[0], near[0]):
-        tt(v("PB"), v("PB"), part("lf", slot(q, rank)), AL.add)
-    for h in range(2):
-        tt(part("yo", 0, h), part("PB", 0, h), part("lf", slot(far[1], rank), h), AL.add)
-        dma("A" if h else "S", ext(T.y[:, 256 * h:256 * h + 256]), part("yo", 0, h))
+    piece = [(far[0], 0), (far[0], 1), (far[1], 0), (far[1], 1), (near[0], 0), (near[0], 1), (rank, None)]
+    terms = []
+
+    def term(m, x, stop=False):
+        mm(v("PB"), v(m), x, not terms, stop)
+        terms.append(x)
+
+    for s in OUT.split():
+        c, n = s[0], int(s[1])
+        q, h = piece[n]
+        if s[2:]:
+            h = None
+        if c == "R":
+            gat("A", part("R", q, h), v("tab", 64, 96), lst("ixu", q, h))
+        elif c == "V":
+            tt(part("V0", q, h), ind(v("V1"), lst("du", q, h)), part("R", q, h), AL.mult)
+        elif c == "T":
+            tt(part("Tg", n // 2, h), ind(v("p4"), lst("gpu", q, h)), part("V0", q, h), AL.add)
+        elif c == "P":
+            gat("A", part("D1", q, h), v("p4"), lst("gpu", q, h))
+            if q == rank:
+                term("Ib", part("D1", rank))
+            elif q in near:
+                post(q, "ap", part("D1", q), part("D2", 0), part("D2", 0), True)
+        elif c == "U":
+            bank = part(("PS", "PT", "PG", "PA")[n], 0, h and 0)
+            mm(bank, v("Ib"), part("D1", q, h), True, True)
+            tt(part("Tg", n // 2, h), bank, part("V0", q, h), AL.add)
+        elif c in "SH":
+            post(q, "af%d" % n, part("V0", q, h) if q in near else part("Tg", n // 2, h), part("lf", slot(rank, q), h),
+                 part("lf", slot(q, rank), h), c == "H")
+        elif c in "XW":
+            post(near[0], "af%d" % n, part("Tg", 1, h), part("lf", slot(far[0], near[0]), h), part("lf", slot(far[1], rank), h), c == "W")
+        elif c == "J":
+            tt(part("Tg", 0, h), part("Tg", 0, h), part("lf", slot(far[1], rank), h), AL.add)
+        elif c == "M":
+            gat("A", v("Mg"), v("Mp", 4 * W, 5 * W), lst("muu", rank), scale=1.0 / 64)
+            term("Ib", v("Mg"))
+        elif c == "N":
+            term("Ib", part("D2", 0))
+        elif c == "F":
+            term("If", part("V0", rank) if q == rank else part("lf", slot(q, rank)))
+        elif c == "E":
+            term("Ib", part("D2", 0), True)
+        elif c == "A":
+            tt(v("PB"), v("PB"), part("V0", rank) if q == rank else part("lf", slot(q, rank)), AL.add)
+        else:
+            for h in range(2):
+                tt(part("yo", 0, h), part("PB", 0, h), part("lf", slot(q, rank), h), AL.add)
+                dma("A" if h else "S", ext(T.y[:, 256 * h:256 * h + 256]), part("yo", 0, h))
     emit(g, T, ops)

from concourse.bass import DstId, RemoteDMATransfer
from concourse.mybir import dt, AluOpType, AxisListType, ActivationFunctionType

W = 2048
RO = 4
REST = 16392.0 - 1.0 / 512
STEP = 32.0
LIFT = [15 * 1024.0 + W, 15 * (1024.0 + STEP / 16)]
TW = 2320
XD = [48, 48]
SE = 4
FS = False
ZD = 1
XQ = 1
WE = ["DADA", "DADA", "DADA"]
WD = 64
IWD = 6
MID = 1
AH = [0, 0]
FMO = 0
ROT = "STAGBDC"
VA = [0, 64]
OUT = "R0 R1 V0 V1 T0 S0 R2w T1 P4w S1 R4w V2w V4w S4w T2 S2 T3 S3 R6 P6 V6 M6 E6 A0 A6 A4 Y2"
MSH = 1
D0D = 48
TRIALS = [["", "E0A", "", "m0", "E1D m1", "g2A0:16 m2", "", "m3 +AG +BD p10 g2A48:88 I p11 p00",
           "p01 g2D40:48 K q00 C s00A L g2A16:40 t30 g2A88:128 s10A s20A p02 s30D s21A t31 s01A s11D s02A -B s22A s12A s31D "
           "t32 s13A s23A s03A t33 Q s32D G1 s33D G0 G2 G3", "", "", "", ""],
          ["g1A0:96 M1 M0 g1A96:104", "", "", "", "g1D104:128", "S0 p11", "g2A80:128", "s11A +AG p01 s00A q01 p10 s10A",
           "g2D0:32 t21 s01A C g2D64:80 I s21A s20A L s23A s03A Q g3D0:32 t31 s13A t33 s22A t32 s12A "
           "s31D s02A s30A s32D G1 G2 s33D G3 S1 G0 S2", "", "S3", "", ""]]
XB = [24, 16]
PLAN = [["x0 e1 x2 d", "n S4 x3", "S5 r56", "x1 e0", "", "k01 k12 r80 m0", "r120", "m1", "k22 r128", "v40", "v120 m2 k33 m3",
         "v128", "", "", "", "", ""],
        ["d x1 S4 n h0 x2 r128 x3", "", "", "S5", "", "", "", "", "", "v40 b2", "m0 b3 v64 v104 m1",
         "a2", "m2 k31", "", "m3", "v128 a3", ""]]
SW = True
KK = 8192.0
F, B, H, I32, U = "float32", "bfloat16", "float16", "int32", "uint16"


def _sb(cols, d):
    return ("sbuf", [128, cols], d)


SCRATCH = {
    "X": _sb(W, B), "Xp": _sb(W, B), "Ms": _sb(3 * W, B), "rsp": _sb(128, H), "Mk": _sb(128, H), "Fr": _sb(128, H), "Fm": _sb(128, H), "B8": _sb(8, H), "Mp": _sb(5 * W, B),
    "lq": _sb(5 * 3 * 512, B), "Wm": _sb(W + 16, B), "Wc": _sb(W, B), "IW": _sb(W, B),
    "D0": _sb(W, B), "D1": _sb(W, B), "D2": _sb(W, B), "D3": _sb(W, B),
    "tA": _sb(TW, F), "tB": _sb(TW, F), "val": _sb(128, F), "inv": _sb(W, H), "dec": _sb(W, B),
    "rst": _sb(128, H), "cz": _sb(128, H), "Bg": _sb(128, H), "KI": _sb(128, H), "KN": _sb(128, H), "Cs": _sb(136, H),
    "Sel": _sb(128, H), "Q": _sb(128, H), "Kr": _sb(128, H), "Kf": _sb(128, H), "Z0": _sb(128, H), "cb": _sb(128, H),
    "mQ": _sb(256, H), "mF": _sb(256, H),
    "Rot": _sb(128, H), "Ts": _sb(256, H), "Pq": _sb(128, H), "S3": _sb(56, B), "I3": _sb(128, B), "gn32": _sb(128, I32), "gnh": _sb(128, H), "oh": _sb(128, H),
    "pg": _sb(16, F), "ab": _sb(8, F),
    "V0": _sb(W, F), "V1": _sb(W, F), "R": _sb(W, F),
    "pb": _sb(W, B), "p4": _sb(W, B), "Tg": _sb(1024, F), "e32": _sb(512, I32), "eu": _sb(512, U), "eh": _sb(512, H),
    "g32": _sb(128, I32), "gu": _sb(128, U), "rh": _sb(8, F), "tab": _sb(128, F),
    "pi": _sb(8, I32), "pj": _sb(8, I32), "pf": _sb(16, F), "iom": _sb(144, B), "iog": _sb(128, B), "ib": _sb(16, F),
    "E": _sb(144, H), "EI": _sb(144, H),
    "Ih": _sb(128, H), "Iq": _sb(128, H), "Ib": _sb(128, B), "Nb": _sb(128, B), "ob": _sb(384, B),
    "GM": _sb(128, F), "Rk": _sb(128, B), "U1": _sb(128, H), "U2": _sb(128, H),
    "cap": _sb(128, B), "N5": _sb(128, B), "tie": _sb(4, F), "l0": _sb(128, H), "wr": _sb(8, F),
    "loc": _sb(136, H), "s1": _sb(128, F), "s3": _sb(128, F), "s4": _sb(128, F),
    "mid": _sb(4, F), "ltA": _sb(8, U), "ltB": _sb(8, U), "l2u": _sb(128, U), "l2h": _sb(128, H), "l3u": _sb(128, U),
    "l3h": _sb(128, H), "cu": _sb(128, U), "dg": _sb(512, H), "acc": _sb(16 * RO, F), "mn": _sb(4, F),
    "ivh": _sb(RO * 128, H), "li": _sb(RO * 3 * 128, H), "muu": _sb(128, U), "msu": _sb(128, U), "Rb": _sb(128, B), "rl": _sb(1536, B), "muf": _sb(132, H),
    "du": _sb(128, U), "ixu": _sb(128, U), "gpu": _sb(128, U), "a1": _sb(128, F), "a2": _sb(128, B), "a3": _sb(128, B),
    "lf": _sb(3 * 512, F), "Mg": _sb(512, B), "yo": _sb(512, F),
    "st": ("dram", [3, 128, 256], B), "ld": ("dram", [3, 128, 256], B), "md": ("dram", [3, 144, W], B),
    "PA": ("psum", [128, 512], F), "PB": ("psum", [128, 512], F), "PC": ("psum", [128, 512], F),
    "PD": ("psum", [128, 512], F), "PG": ("psum", [128, 512], F), "PF": ("psum", [128, 512], F),
    "PS": ("psum", [128, 512], F), "PT": ("psum", [128, 512], F),
}
ARR = (["ag", "ap"] + ["aq%d" % t for t in range(5)] + ["ah%d" % t for t in range(5)] + ["ak0", "ak1"] + ["ar%d" % t for t in range(5)] + ["am%d" % t for t in range(5)]
       + ["ai%d" % t for t in range(2 * RO)] + ["an%d" % t for t in range(3)] + ["af%d" % t for t in range(6)]
       + ["aw%d" % t for t in range(9)])
SEMAPHORES = ["cD", "cA", "cP", "cG"] + ARR + ["s%d" % k for k in range(92)]
ESZ = {F: 4, B: 2, H: 2, I32: 4, U: 2}
AL = AluOpType
AF = ActivationFunctionType


def bits(es):
    m = 0
    for e in es:
        m |= 1 << e
    return m


def split_engines(T, topo, core):
    mates = topo.cores_of(core)
    far = topo.engines(core, [c for c in T.cores if c not in mates][0])
    near = topo.engines(core, [c for c in mates if c != core][0])
    return [e for e in near if e not in far], far


def dest(topo, d, core):
    rid, pid = topo.addr(d, core)
    return DstId(rid=rid, pnc=pid)


def emit(g, T, ops):
    Q = {"D": g.vector, "A": g.scalar, "P": g.tensor, "G": g, "S": g.sync}
    hist = {}
    know = {q: {} for q in Q}
    for n, o in enumerate(ops):
        deps = set(o.get("after", []))
        for wr, regs in ((False, o["r"]), (True, o["w"])):
            for (b, pm, c0, c1) in regs:
                ps = SCRATCH[b][0] == "psum"
                for (m, w2, pm2, d0, d1) in hist.get(b, []):
                    if o["grp"] and o["grp"] == ops[m]["grp"]:
                        continue
                    u = 1 if o["k"] == "c" and ops[m]["k"] == "c" else 16
                    if ps and ops[m]["q"] != o["q"]:
                        deps.add(m)
                    elif ((wr or w2) and (pm & pm2) and c0 // u <= (d1 - 1) // u and d0 // u <= (c1 - 1) // u
                          and not (ps and o["q"] == "P")):
                        deps.add(m)
        for wr, regs in ((False, o["r"]), (True, o["w"])):
            for (b, pm, c0, c1) in regs:
                hist.setdefault(b, []).append((n, wr, pm, c0, c1))
        o["waits"] = []
        if o["k"] == "arr":
            o["snap"] = {("t", n): n}
            continue
        kn = know[o["q"]]
        for m in sorted(deps, reverse=True):
            p = ops[m]
            key = p["q"] if p["k"] == "c" else ("t", m)
            if kn.get(key, -1) >= m:
                continue
            o["waits"].append(m)
            p["need"] = True
            for k2, v2 in p["snap"].items():
                if kn.get(k2, -1) < v2:
                    kn[k2] = v2
        o["snap"] = dict(kn)
        o["snap"][o["q"] if o["k"] == "c" else ("t", n)] = n
    cnt = {q: 0 for q in Q}
    pool = [0]
    for o in ops:
        if o["k"] == "arr":
            continue
        e = Q[o["q"]]
        for m in o["waits"]:
            e.wait_ge(T.sem[ops[m]["tok"][0]], ops[m]["tok"][1])
        if o["k"] == "c":
            ins = o["f"](e)
            if o.get("need"):
                cnt[o["q"]] += 1
                o["tok"] = ("c" + o["q"], cnt[o["q"]])
                ins.then_inc(T.sem[o["tok"][0]], 1)
        else:
            s = "s%d" % pool[0]
            pool[0] += 1
            if o["k"] == "dma":
                o["tok"] = (s, 16)
                o["f"](e).then_inc(T.sem[s], 16)
            else:
                o["tok"] = (s, o["n"])
                o["f"](e, T.sem[s])
    for o in ops:
        if o["k"] != "c" and not o.get("need"):
            g.wait_ge(T.sem[o["tok"][0]], o["tok"][1])


def rank_program(g, core, T, topo):
    rank = T.rank_of(core)
    if rank is None:
        return
    cores = list(T.cores)
    ops = []
    grp = [0]
    rnd = [0]
    turn = [0]
    ALLP = (1 << 128) - 1

    def v(name, c0=None, c1=None, st=1, rows=None, rev=False):
        shp, d = SCRATCH[name][1], SCRATCH[name][2]
        c0 = 0 if c0 is None else c0
        c1 = shp[1] if c1 is None else c1
        pm = ALLP
        if rows is None:
            rs = slice(0, 128)
        else:
            rs = slice(rows[0], rows[1], rows[2])
            pm = bits(range(rows[0], rows[1], rows[2]))
        ap = T[name][rs, c0:c1:st] if st != 1 else T[name][rs, c0:c1]
        if rev:
            ap = T[name][rs, ::-1]
        z = ESZ[d]
        return {"ap": ap, "reg": [(name, pm, c0 * z, c1 * z)]}

    def dr(name, ap, k):
        return {"ap": ap, "reg": [(name, ALLP, 16 * k, 16 * k + 16)]}

    def ext(ap):
        return {"ap": ap, "reg": []}

    def ind(win, off):
        return {"ap": win["ap"].indirect(off["ap"]), "reg": win["reg"] + off["reg"], "off": off["reg"], "win": win["reg"]}

    def add(q, k, f, r, w, **kw):
        rr, ww = [], []
        for x in r:
            if isinstance(x, dict):
                rr += x["reg"]
        for x in w:
            ww += x.get("win", x["reg"])
            rr += x.get("off", [])
        o = {"q": q, "k": k, "f": f, "r": rr, "w": ww, "grp": grp[0]}
        o.update(kw)
        ops.append(o)

    def a_(x):
        return x["ap"] if isinstance(x, dict) else x

    def cp(o, i):
        add("D", "c", lambda e: e.tensor_copy(o["ap"], i["ap"]), [i], [o])

    def tt(o, a, b, op):
        add("D", "c", lambda e: e.tensor_tensor(o["ap"], a["ap"], b["ap"], op), [a, b], [o])

    def ts(o, a, s1, op0, s2=None, op1=None):
        if op1 is None:
            add("D", "c", lambda e: e.tensor_scalar(o["ap"], a["ap"], a_(s1), None, op0), [a, s1], [o])
        else:
            add("D", "c", lambda e: e.tensor_scalar(o["ap"], a["ap"], a_(s1), a_(s2), op0, op1), [a, s1, s2], [o])

    def ms(o, c):
        add("D", "c", lambda e: e.memset(o["ap"], c), [], [o])

    def red(o, i, op):
        add("D", "c", lambda e: e.tensor_reduce(o["ap"], i["ap"], AxisListType.X, op), [i], [o])

    def scan(o, a, b, init, op0=AL.max, op1=AL.max):
        add("D", "c", lambda e: e.tensor_tensor_scan(o["ap"], a["ap"], b["ap"], a_(init), op0, op1), [a, b, init], [o])

    def act(o, i, fn, bias=None, scale=None, acc=None):
        kw = {}
        if bias is not None:
            kw["bias"] = a_(bias)
        if scale is not None:
            kw["scale"] = a_(scale)
        if acc is not None:
            kw["accum_out"] = acc["ap"]
        add("A", "c", lambda e: e.activation(o["ap"], i["ap"], fn, **kw), [i, bias, scale], [o] + ([acc] if acc else []))

    held = set()

    def mm(o, l, r, start, stop):
        assert not (start and o["reg"][0][0] in held)
        add("P", "c", lambda e: e.matmul(o["ap"], l["ap"], r["ap"], start, stop), [l, r], [o])

    def dma(q, o, i, acc=False):
        if acc:
            add(q, "dma", lambda e: e.dma_start(o["ap"], i["ap"], accum_op=AL.add), [i], [o])
        else:
            add(q, "dma", lambda e: e.dma_start(o["ap"], i["ap"]), [i], [o])

    def iota(o, pat, base, cm):
        small = SCRATCH[o["reg"][0][0]][2] != I32
        add("G", "c", lambda e: e.iota(o["ap"], pat, base, cm, allow_small_or_imprecise_dtypes=small) if small
            else e.iota(o["ap"], pat, base, cm), [], [o])

    def send(trs):
        def f(e, s):
            e.remote_dma_fused([RemoteDMATransfer(dst_ids=[dest(topo, c, core) for c in cs], dma_engine_mask=bits(es),
                                                  remote_sem=T.sem[sem], srcs=[x["ap"] for x in srcs],
                                                  dsts=[x["ap"] for x in dsts], alu_op=alu)
                                for (cs, es, sem, srcs, dsts, alu) in trs], local_sem=s)
        add("G", "rem", f, [x for tr in trs for x in tr[3]], [], n=sum(len(tr[1]) for tr in trs))

    def arrive(o, sem, n):
        add("-", "arr", None, [], [o], tok=(sem, n))

    def gat(q, o, win, off, scale=None):
        if q == "D" and scale is not None:
            ts(o, ind(win, off), scale, AL.mult)
        elif q == "D":
            cp(o, ind(win, off))
        else:
            act(o, ind(win, off), AF.Identity, scale=scale)

    def gat4(oname, win, lname, qd=(0, 1), qa=(2, 3)):
        for a, b in zip(qd, qa):
            gat("D", v(oname, 512 * a, 512 * a + 512), win, v(lname, 32 * a, 32 * a + 32))
            gat("A", v(oname, 512 * b, 512 * b + 512), win, v(lname, 32 * b, 32 * b + 32))

    def conv(o, em, src, k0=0, k1=128):
        for i in range(16):
            mm(v(o, k0, k1), v(em, 15 - i, 143 - i), v(src, 16 * k0 + i, 16 * (k1 - 1) + i + 1, 16), i == 0, i == 15)

    chipmates = topo.cores_of(core)
    near = [q for q in range(4) if q != rank and cores[q] in chipmates]
    far = [q for q in range(4) if cores[q] not in chipmates]
    far.sort(key=lambda q: topo.die(cores[q]) != topo.die(core))
    e_near, e_far = split_engines(T, topo, core)
    hf = len(e_far) // 2
    eng3 = {near[0]: e_near, far[0]: e_far[:hf], far[1]: e_far[hf:]}
    n3 = len(e_near) + len(e_far)
    mine = [rank] if not MSH else [0, 1, 2, 3] if MSH == 2 else [0, 1] if rank < near[0] else [2, 3]
    prev = (rank - 1) % 4
    e_prev = e_near if prev in near else e_far
    n_next = len(e_near) if (rank + 1) % 4 in near else len(e_far)

    def slot(frm, to):
        return (frm - to) % 4 - 1

    def lq(t, frm, to):
        c = 1536 * t + 512 * slot(frm, to)
        return v("lq", c, c + 512)

    later = []

    def post(q, sem, src, dst, lands, hold=False):
        later.append((q, sem, src, dst, lands))
        if not hold:
            send([([cores[q]], e_near if q in near else e_far, sem, [src], [dst], 0) for (q, sem, src, dst, _) in later])
            for (q, sem, _, _, lands) in later:
                arrive(lands, sem, len(e_near if q in near else e_far))
            later.clear()

    def mq(u, q):
        return v("Mp", W * u + 512 * q, W * u + 512 * q + 512)

    def nothing():
        pass

    def spread(src, dst, lands, sems, one=False):
        for qs in (near + far,) if one else (near + far[:1], far[1:]):
            send([([cores[q]], eng3[q] if one or q in near else e_far, sems[(near + far).index(q)], [src(q)], [dst(q)], 0) for q in qs])
        for k, q in enumerate(near + far):
            arrive(lands(q), sems[k], len(eng3[q]) if one or q in near else len(e_far))

    ahead = {}

    def fold(src, t, part, early=None):
        a, b, c, d = [v(src, 512 * rank, 512 * rank + 512)] + [lq(t, q, rank) for q in (far[:1] + near + far[1:] if t else near + far)]
        r1, r2, r3 = [v("rl", 512 * k, 512 * k + 512) for k in range(3)]

        def summed(bank, terms, start, stop):
            for k, (m, x) in enumerate(terms):
                mm(v(bank), v(m), x, start and k == 0, stop and k == len(terms) - 1)

        bank, terms = [("PS", [("Ib", a), ("Nb", b)]), ("PT", [("Ib", b), ("Nb", c), ("Ib", r1)]),
                       ("PS", [("Ib", c), ("Nb", d), ("Ib", r2)]),
                       ("PF", [("Rb", d), ("Rb", r3)] if t < RO else [("Ib", a), ("Ib", b), ("Ib", c), ("I3", d), ("Rb", r3)])][part]
        done = ahead.get((t, part), 0)
        upto = len(terms) if early is None else min(early, len(terms) - 1)
        summed(bank, terms[done:upto], done == 0, early is None)
        ahead[t, part] = max(done, upto)
        if early is not None:
            return
        if part < 3:
            act((r1, r2, r3)[part], v(bank), AF.Relu)
        else:
            act(mq(t, rank), v("PF"), AF.Identity)
            if t:
                send([([cores[q]], eng3[q], "am%d" % t, [mq(t, rank)], [mq(t, rank)], 0) for q in eng3])
                add("-", "arr", None, [], [mq(t, q) for q in eng3], tok=("am%d" % t, n3))
            else:
                spread(lambda q: mq(t, rank), lambda q: mq(t, rank), lambda q: mq(t, q), ("ak0", "am0", "ak1"))

    def blocks(src, sel, n, bank="PA"):
        mm(v(bank, 0, 128 * n), v("Ib"), v("ob", 0, 128 * n), True, False)
        for o in range(16):
            mm(v(bank, o, 128 * n - 15 + o, 16), v(src, o, W - 15 + o, 16), sel, False, o == 15)

    def turned(k, c):
        mm(v("PD", c, c + 128), v("Ts", 128 * k, 128 * k + 128), v("Ih"), True, True)

    def records(win, bank, f1=nothing, f2=nothing, f3=nothing, f4=nothing, f5=nothing, f6=nothing, f7=nothing):
        r8 = (0, 8, 1)
        loc = v("loc", 8, 136)
        mm(v("PC", 0, 128), v("KI"), v("cz"), True, False)
        mm(v("PG", 0, 128), v("KI"), v("oh"), True, False)
        scan(loc, v("rst"), v(bank, 0, 128), 0.0, AL.add, AL.max)
        mm(v("PB", 0, 128, rows=r8), v("loc", 23, 136, 16), v("Ih"), True, True)
        mm(v("PC", 0, 128), v("KI"), v("loc", 7, 135), False, False)
        mm(v("PC", 0, 128), v("KN"), loc, False, True)
        mm(v("PG", 0, 128), v("KN"), loc, False, False)
        f1()
        scan(v("Cs", 1, 129, rows=r8), v("PB", 0, 128, rows=r8), v("rst", rows=r8), 0.0)
        mm(v("PG", 0, 128), v("Cs", 0, 128, rows=r8), v("Sel", rows=r8), False, True)
        tt(v("s3"), v("PC", 0, 128), loc, AL.max)
        f2()
        tt(v("s4"), v("PG", 0, 128), v("s3"), AL.max)
        f7()
        scan(v("Q", rev=True), v("Bg", rev=True), v("s4", rev=True), 0.0, AL.max, AL.min)
        mm(v("PB", 0, 128), v("Q"), v("Ih"), True, True)
        if AH[rnd[0] > 0]:
            halves = True
        else:
            halves = win == "tB"
        for pb in ("PA", "PG") if halves else ("PA",):
            mm(v(pb, 0, 128), v("Z0"), v("cb"), True, False)
        if FMO:
            scan(v("Fr"), v("rsp"), v("Q"), 0.0, AL.add, AL.min)
            tt(v("Fm"), v("Fr"), v("Mk"), AL.mult)
        f3()
        if not FMO:
            scan(v("Fr"), v("rsp"), v("Q"), 0.0, AL.add, AL.min)
        cp(v("Kr"), v("PB", 0, 128))
        ts(v("Kf"), v("PB", 0, 128), thr, AL.is_ge)
        if not FMO:
            tt(v("Fm"), v("Fr"), v("Mk"), AL.mult)
        mm(v("PA", 0, 128), v("mQ", 0, 128), v("Kr"), False, False)
        mm(v("PA", 0, 128), v("mF", 0, 128), v("Kf"), False, True)
        mm(v("PC", 0, 8), v("Fm"), v("B8"), True, True)
        if halves:
            for mx, kk in (("mQ", "Kr"), ("mF", "Kf")):
                mm(v("PG", 0, 128), v(mx, 128, 256), v(kk), False, kk == "Kf")
        f4()
        ts(v("val"), v("PA", 0, 128), 0.0, AL.max, bas[rnd[0] % 2], AL.add)
        cp(v("l" + win), v("PC", 0, 8))
        if halves and MID:
            red(v("mid", 1, 2), v("PG", 0, 128), AL.max)
        f5()
        cp(ind(v(win), v("l" + win)), v("val"))
        if halves and MID:
            ts(v("mid", 0, 1), v("mid", 1, 2), c4, AL.max, bm4[rnd[0] % 2], AL.add)
        f6()

    def running(win, f1=nothing):
        for h in range(2):
            a, b = 1024 * h, 1024 * h + 1024
            scan(v("inv", a, b), v("dec", 0, b - a), v(win, a + 1, b + 1), v("mid", 0, 1) if h else bas[rnd[0] % 2], AL.add, AL.max)
            if h == 0 and not MID:
                red(v("mid", 1, 2), v("PG", 0, 128), AL.max)
                ts(v("mid", 0, 1), v("mid", 1, 2), c4, AL.max, bm4[rnd[0] % 2], AL.add)
            counted("PB" if h else "PC", 64 * h, 64 * h + 64)
            if h == 0:
                f1()

    def counted(bank, k0, k1):
        for o in range(16):
            mm(v(bank, k0, k1), v("EI", 15 - o, 143 - o), v("inv", 16 * k0 + o, 16 * k1 + o - 15, 16), o == 0, o == 15)

    def running_whole(win, f1=nothing):
        scan(v("inv", 0, W), v("dec", 0, W), v(win, 1, W + 1), bas[rnd[0] % 2], AL.add, AL.max)
        f1()
        counted("PC", 0, 128)

    def inv_half(o, c0, h):
        ts(v(o, c0 + 64 * h, c0 + 64 * h + 64), v("PB" if h else "PC", 64 * h, 64 * h + 64), LIFT[rnd[0] % 2], AL.add)

    def inv_lists():
        for n in ("l3u", "l3h"):
            ts(v(n), v("PC", 0, 128), LIFT[rnd[0] % 2], AL.add)

    def wipe(win):
        iota(v(win, 0, W + 2), [[0, W + 2]], -4096, 0)

    def turned_back(t, c0=0, c1=W):
        return {"ap": T.md[t - 1, 0:128, c0:c1], "reg": [("md", ALLP, 32 * t, 32 * t + 32)]}

    def score(k, lname, l0, Ms, cuts):
        for c in range(len(cuts) - 1):
            a, b = cuts[c], cuts[c + 1]
            tt(v("D%d" % k, 16 * a, 16 * b), ind(v("X"), v(lname, l0 + a, l0 + b)), v(Ms[0], Ms[1] + 16 * a, Ms[1] + 16 * b), AL.subtract)

    def acc(c, k, n=1):
        return v("acc", 16 * rnd[0] + 4 * c + k, 16 * rnd[0] + 4 * c + k + n)

    def absum(k, cuts, which, q="A"):
        for c in which:
            d = v("D%d" % k, 16 * cuts[c], 16 * cuts[c + 1])
            o = acc(c, k)
            if q == "A":
                act(d, d, AF.Abs, acc=o)
            else:
                absred(o, d)

    def absred(o, d):
        add("D", "c", lambda e: e.tensor_reduce(o["ap"], d["ap"], AxisListType.X, AL.add, apply_absolute_value=True), [d], [o])

    def stay(c, Ms, src="X", k=0, q="A"):
        o = 512 * c
        turn[0] = (turn[0] + 1) % 4
        bank, a = v(("PS", "PT", "PA", "PG")[turn[0]]), acc(c, k)
        mm(bank, v("Ib"), v(src, o, o + 512), True, False)
        mm(bank, v("Nb"), v(Ms[0], Ms[1] + o, Ms[1] + o + 512), False, True)
        if q == "A":
            act(v("D0", 512 * turn[0], 512 * turn[0] + 512), bank, AF.Abs, acc=a)
        else:
            absred(a, bank)

    def mu_slope():
        mm(v("PD", 0, 128), v("U1"), v("muf", 0, 128), True, False)
        mm(v("PD", 0, 128), v("U2"), v("muf", 1, 129), False, True)

    def slopes(bank, f1=nothing, part=None):
        if part != 1:
            if part is None:
                act(v("a1"), v(bank, 256, 384), AF.Abs)
                act(v("a2"), v("PD", 0, 128), AF.Relu, bias=4.0, scale=-1.0)
                f1()
                act(v("a3"), v("a1"), AF.Relu, bias=4.0, scale=-1.0)
            else:
                act(v("a1"), v(bank, 256, 384), AF.Abs)
                act(v("a3"), v("a1"), AF.Relu, bias=4.0, scale=-1.0)
                act(v("a2"), v("PD", 0, 128), AF.Relu, bias=4.0, scale=-1.0)
        if part == 0:
            return
        mm(v("PS", 0, 128), v("Ib"), v("cap"), True, False)
        mm(v("PS", 0, 128), v("a3"), v("N5"), False, False)
        mm(v("PS", 0, 128), v("Nb"), v("a2"), False, True)

    dma("S", v("g32"), ext(T.gam[:]))
    dma("A", v("X"), ext(T.xs[:]))
    iota(v("pi", 0, 4), [[16, 2], [112, 2]], 0, 1)
    iota(v("iom"), [[1, 144]], 0, 0)
    iota(v("iog"), [[16, 8], [0, 16]], 0, 0)
    dma("S", v("e32"), ext(T.ew[:]))
    dma("S", v("rh", 0, 5), ext(T.rho[:]))
    send([([cores[prev]], e_prev, "ag", [v("g32")], [v("gn32")], 0)])
    arrive(v("gn32"), "ag", n_next)
    if FS:
        spread(lambda q: v("X", 512 * q, 512 * q + 512), lambda q: lq(0, rank, q), lambda q: lq(0, q, rank), ("ah0", "aq0", "ar0"))
    else:
        send([([cores[q]], eng3[q], s, [v("X", 512 * q, 512 * q + 512)], [lq(0, rank, q)], 0)
              for q, s in zip(near + far, ("ah0", "aq0", "ar0"))])
        for q, s in zip(near + far, ("ah0", "aq0", "ar0")):
            arrive(lq(0, q, rank), s, len(eng3[q]))
    ms(v("oh"), 1.0)
    for (c, b, m) in [(0, 1, 15), (1, 2, 112), (3, 3, 127)]:
        ts(v("pj", c, c + b), v("pi", 0, b), m, AL.bitwise_and)
    ms(v("rst"), 0.0)
    cp(v("pf", 0, 6), v("pj", 0, 6))
    ms(v("Bg"), 0.0)
    pm, gb, gbp, pp, ppm, ppn = [v("pf", k, k + 1) for k in range(6)]
    lo, hi = v("pf", 8, 9), v("pf", 12, 13)
    thr, c4, nz, p2, p16, nq, n32, wa, wd = [v("pg", k, k + 1) for k in range(9)]
    bas, bm4 = [[v("pg", k, k + 1), v("pg", k + 1, k + 2)] for k in (10, 12)]
    z0 = v("wr", 5, 6)
    ts(lo, pm, 8.0, AL.is_ge)
    ts(hi, pm, 8.0, AL.is_lt)
    ms(v("rst", 0, 113, 16), -4096.0)
    ts(v("ib"), v("iom", 0, 16), lo, AL.mult)
    ts(z0, pm, 0.0, AL.is_equal)
    grp[0] = 1
    for i in range(16):
        if i < IWD:
            ts(v("IW", i, W - 15 + i, 16), v("iom", 0, 128), hi, AL.mult, v("ib", i, i + 1), AL.add)
        else:
            act(v("IW", i, W - 15 + i, 16), v("iom", 0, 128), AF.Identity, bias=v("ib", i, i + 1), scale=hi)
    grp[0] = 0
    wipe("tA")
    wipe("tB")
    ts(nz, pm, 0.0, AL.not_equal)
    ts(p16, pp, 16.0, AL.mult)
    ts(wd, nz, -1.0 / 256, AL.mult)
    ts(bas[0], nz, REST + W, AL.mult, -1.0 * W, AL.add)
    ts(bas[1], nz, REST + STEP, AL.mult)
    ts(v("Ih"), v("iom", 0, 128), pp, AL.is_equal)
    ts(v("KI"), v("iom", 0, 128), pp, AL.is_equal, KK, AL.mult)
    ts(v("Rot"), v("iom", 0, 128), ppm, AL.is_equal)
    ts(v("KN"), v("iom", 0, 128), pp, AL.is_equal, -KK, AL.mult)
    ts(v("cz"), v("rst"), 0.5, AL.add)
    cp(v("gu"), v("g32"))
    ms(v("loc", 0, 8), 0.0)
    ms(v("Cs", 0, 8), 0.0)
    ts(p2, pp, 2.0, AL.mult, 2050.0, AL.add)
    ts(thr, z0, 1024.5 - 2049.0, AL.mult, 2049.0, AL.add)
    ts(nq, nz, 1.0 / 256, AL.mult)
    ts(v("Sel"), v("iog"), p16, AL.is_equal, KK, AL.mult)
    ts(v("Bg", 15, 128, 16), v("Bg", 15, 128, 16), p2, AL.add)
    gat("A", v("Wc"), v("IW"), v("gu"))
    ts(v("E"), v("iom"), -15.0, AL.add, gb, AL.is_equal)
    ts(v("Kr"), v("iog"), gb, AL.is_equal, z0, AL.mult)
    ts(v("Kf"), v("Ih"), 32.0, AL.mult)
    ts(n32, nz, -1.0, AL.mult)
    tt(v("Fr"), v("iom", 0, 128), v("iog"), AL.subtract)
    ts(v("rsp"), v("rst"), -1.0, AL.mult)
    ts(v("B8"), v("iog", 0, 113, 16), gb, AL.is_equal)
    tt(v("Q"), v("Ih"), v("Kr"), AL.subtract)
    tt(v("Kf"), v("Kf"), v("E", 15, 143), AL.add)
    ts(v("Mk"), v("Fr"), pm, AL.is_equal)
    ts(v("Z0"), v("Ih"), z0, AL.mult)
    ts(v("mQ", 0, 128), v("Q"), 1.0 / 256, AL.mult)
    ts(v("mF", 0, 128), v("Kf"), n32, AL.mult)
    cp(v("eu", 0, 128), v("e32", 0, 128))
    gat("A", v("D1", 16 * D0D, W), v("X"), v("eu", D0D, 128))
    ts(v("cb"), v("iom", 0, 128), 16.0, AL.mult, 15.0, AL.add)
    ts(wa, z0, 17.0 / 16, AL.mult, -1.0 / 16, AL.add)
    ts(v("Fm"), v("Kr"), KK, AL.mult)
    ts(c4, nz, 4.0, AL.mult)
    ts(v("EI"), v("E"), wa, AL.mult)
    tt(v("mF", 128, 256), v("mF", 0, 128), v("Fm"), AL.subtract)
    ts(v("Ib"), v("iom", 0, 128), pp, AL.is_equal)
    ts(v("Nb"), v("iom", 0, 128), pp, AL.is_equal, -1.0, AL.mult)
    cp(v("Rb"), v("Rot"))
    if D0D:
        gat("D", v("D1", 0, 16 * D0D), v("X"), v("eu", 0, D0D))
    cp(v("gnh"), v("gn32"))

    def mid_constants():
        ts(v("mQ", 128, 256), v("Ih"), nq, AL.mult)
        ts(v("pg", 12, 14), v("pg", 10, 12), c4, AL.subtract)

    def sum_constants(n):
        if n:
            ts(v("GM"), v("iog"), gb, AL.is_equal)
        else:
            ms(v("acc"), 0.0)
            ts(v("tie"), v("iom", 0, 4), 4.0, AL.add, 1.0 / 64, AL.mult)

    def mid_constants2():
        ts(v("l0"), v("iom", 0, 128), 16.0, AL.mult, pm, AL.add)
        cp(v("eh", 0, 128), v("e32", 0, 128))
        ms(v("ob", 0, 128), 1.0)
        ms(v("ob", 128, 384), 0.0)
        ts(v("wr", 0, 4), v("iom", 0, 4), pm, AL.is_equal, 16.0, AL.mult)
        ts(v("ab", 4, 8), v("iom", 8, 12), pm, AL.is_equal)
        ts(v("wr", 6, 7), pm, 0.0, AL.not_equal)
        tt(v("wr", 0, 4), v("wr", 0, 4), v("ab", 4, 8), AL.add)
        tt(v("wr", 4, 5), v("wr", 2, 3), v("wr", 1, 2), AL.subtract)
        ts(v("S3", 24, 32), v("E", 15, 128, 16), v("wr", 0, 1), AL.mult)

    def row_constants(cols):
        for (c, k) in cols:
            ts(v("S3", c, c + 8), v("E", 15, 128, 16), v("wr", k, k + 1), AL.mult)

    def mean_constants():
        ts(v("Iq"), v("Ih"), 0.25, AL.mult)
        ts(v("Pq"), v("Rot"), 0.25, AL.mult)
        ts(v("S3", 0, 8), v("iog", 0, 113, 16), gbp, AL.is_equal, v("wr", 3, 4), AL.mult)

    def slope_constants():
        ts(v("U2"), v("E", 0, 128), v("wr", 5, 6), AL.mult)
        ts(v("a1"), v("iom", 1, 129), pp, AL.is_equal, v("wr", 6, 7), AL.mult)
        ms(v("cap"), 24.0)

    def late_constants():
        ts(v("Rk"), v("iom", 0, 128), ppn, AL.is_equal)
        ts(v("I3"), v("Ib"), 3.0, AL.mult)
        ts(v("N5"), v("Ib"), -5.0, AL.mult)
        ms(v("tab"), 0.0)
        ms(v("muf", 128, 132), 4096.0)
        tt(v("U1"), v("a1"), v("Ih"), AL.subtract)
        ts(v("cap", 127, 128), pm, 15.0, AL.not_equal, 3.0, AL.mult)
        ts(v("cap", 127, 128), v("cap", 127, 128), 21.0, AL.add)
        for s in range(5):
            ts(v("tab", 32 + 5 * s, 37 + 5 * s), v("rh", 0, 5), v("rh", s, s + 1), AL.mult)
        ts(v("tab", 0, 25), v("tab", 32, 57), 32.0, AL.mult)
        ts(v("tab", 64, 89), v("tab", 32, 57), 1.0 / 128, AL.mult)

    H2, Q4 = [0, 64, 128], [0, 32, 64, 96, 128]
    ready = (("X", 0), ("D1", 1), ("D2", 2))
    for t in range(RO):
        last = t == RO - 1
        rnd[0] = t
        Ms = ("Ms", W * (t - 1)) if t else ("Mp", 0)
        land = [rank] + near + far if not (t and MSH) else mine + [q for q in range(4) if q not in mine]
        vo = "V%d" % (t % 2)
        vi = v("pb") if t == 1 else v("V%d" % ((t + 1) % 2))
        made, carried, landed, begun, ended, less, summed = [0], [0], [], {}, set(), set(), []

        def factors(k1):
            k0 = made[0]
            if t > 0 and k1 > k0:
                gat("A", v("R", 16 * k0, 16 * k1), v("tab", 0 if t == 1 else 32, 32 if t == 1 else 64), v("ixu", k0, k1))
                made[0] = k1

        def xq(q, k0, k1):
            gat(q, v("X", 16 * k0, 16 * k1), v("Xp"), v("muu", k0, k1))

        def lists2(*names):
            for n in names:
                ts(v(n), v("PD", 256, 384), -1.0, AL.add)

        def msq(q):
            return v("Ms", Ms[1] + 512 * q, Ms[1] + 512 * q + 512)

        def template(n, e):
            q = land[n]
            if MSH == 3:
                mh, oh = [v("Ms", Ms[1] + 512 * land[k], Ms[1] + 512 * land[k] + 1024) for k in (0, 2)]
                if n == 0:
                    gat(e, mh, v("Mp", W * t, W * t + W), v("msu", 0, 64))
                    post(near[0], "aw%d" % (3 * t - 3), mh, mh, oh)
                landed[:] = [len(ops) - 1]
                return
            gat(e, msq(q), v("Mp", W * t, W * t + W), v("msu", 32 * n, 32 * n + 32))
            if MSH == 2:
                pass
            elif MSH:
                send([([cores[near[0]]], e_near, "aw%d" % (3 * t - 3 + n), [msq(q)], [msq(q)], 0)])
                arrive(msq(land[2 + n]), "aw%d" % (3 * t - 3 + n), len(e_near))
            else:
                spread(lambda q: msq(rank), lambda q: msq(rank), msq, ["aw%d" % (3 * t - 3 + k) for k in range(3)], SW)
            landed[:] = [len(ops) - 1]

        def quiet():
            if t > 1:
                dma("G", v("V%d" % ((t + 1) % 2)), turned_back(t - 1), acc=True)
                ops[-1]["after"] = list(landed)
            if t > 0 and (len(VA) > 1 or not last):
                dma("S", dr("md", T.md[t - 1, 16:144, :], 2 * t), v("Ms", Ms[1], Ms[1] + W))
                dma("S", dr("md", T.md[t - 1, 0:16, :], 2 * t + 1), v("Ms", Ms[1], Ms[1] + W, rows=(112, 128, 1)))
            if t in (1, 2):
                wipe("tA" if t == 1 else "tB")

        def curve(k, c0, c1):
            return v(("X", "D1", "D2", "D3")[k], c0, c1)

        def runs(a, b):
            out = []
            for n in range(a // 32, (b + 31) // 32):
                k0, k1 = [32 * land[n] + x for x in (max(a - 32 * n, 0), min(b - 32 * n, 32))]
                if out and out[-1][1] == k0:
                    out[-1][1] = k1
                else:
                    out.append([k0, k1])
            return out

        barred = set("AGBDC")

        def begin(k, n, bank=""):
            while not bank:
                rot = [b for b in ROT if b not in barred]
                turn[0] = (turn[0] + 1) % len(rot)
                assert any("P" + b not in held for b in rot)
                bank = "" if "P" + rot[turn[0]] in held else rot[turn[0]]
            begun[k, n] = "P" + bank
            mm(v(begun[k, n]), v("Ib"), curve(k, 512 * land[n], 512 * land[n] + 512), True, False)
            held.add(begun[k, n])

        def trials(names):
            for s in names.split():
                if s[0] == "g":
                    k, (a, b) = int(s[1]), [int(x) for x in s[3:].split(":")]
                    for k0, k1 in runs(a, b):
                        l0 = 128 * t if k == 1 else 0
                        gat(s[2], curve(k, 16 * k0, 16 * k1), v("X"), v(("", "eu", "l2u", "l3u")[k], l0 + k0, l0 + k1))
                elif s[0] == "t":
                    k, n, m = int(s[1]), int(s[2]), int(s[-1])
                    less.update((k, x) for x in range(n, m + 1))
                    for cut in runs(32 * n, 32 * m + 32):
                        score(k, "l%du" % k, 0, Ms, cut)
                elif s[0] == "a":
                    k, n = int(s[1]), int(s[2])
                    (k0, k1), = runs(32 * n, 32 * n + 64)
                    d = curve(k, 16 * k0, 16 * k1)
                    if s[3] == "A":
                        act(d, d, AF.Abs, acc=acc(n, k))
                    else:
                        absred(acc(n, k), d)
                elif s[0] == "p":
                    begin(int(s[1]), int(s[2]), s[3:])
                elif s[0] in "sq":
                    k, n = int(s[1]), int(s[2])
                    o = 512 * land[n]
                    if (k, n) in less:
                        d = out = curve(k, o, o + 512)
                    else:
                        if (k, n) not in begun:
                            begin(k, n)
                        d, out = v(begun[k, n]), v("D0", 512 * (len(ended) % 4), 512 * (len(ended) % 4) + 512)
                        if (k, n) not in ended:
                            mm(d, v("Nb"), v(Ms[0], Ms[1] + o, Ms[1] + o + 512), False, True)
                            ended.add((k, n))
                    if s[0] == "q":
                        continue
                    held.discard(begun.get((k, n)))
                    if s[3] == "A":
                        act(out, d, AF.Abs, acc=acc(n, k))
                    else:
                        absred(acc(n, k), d)
                elif s[0] == "G":
                    if not summed:
                        mm(v("PB", 0, 4), v("GM"), v("tie"), True, False)
                    summed.append(s)
                    mm(v("PB", 0, 4), v("GM"), acc(int(s[1]), 0, 4), False, len(summed) == 4)
                elif s[0] == "M":
                    if int(s[1]) < len(mine):
                        template(int(s[1]), s[2:] or "A")
                elif s[0] == "m":
                    fold("X", 0, int(s[1]))
                elif s[0] == "r":
                    factors(int(s[1:]))
                elif s[0] == "E":
                    c = 1024 * int(s[1])
                    if s[2] == "A":
                        act(v("dec", c, c + 1024), v("X", c, c + 1024), AF.Identity, bias=wd, scale=0.0)
                    else:
                        ts(v("dec", c, c + 1024), v("X", c, c + 1024), 0.0, AL.mult, wd, AL.add)
                elif s[0] in "ZCL" and s[1:]:
                    n = int(s[1])
                    h, bank = land[2 * n] // 2 if t else n, ("PC", "PB")[n]
                    if s[0] == "Z":
                        scan(v("inv", 1024 * h, 1024 * h + 1024), v("dec", 0, 1024), v("tA", 1024 * h + 1, 1024 * h + 1025),
                             v("mid", 0, 1) if h else bas[t % 2], AL.add, AL.max)
                    elif s[0] == "C":
                        counted(bank, 64 * h, 64 * h + 64)
                    else:
                        for x in ("l3u", "l3h"):
                            ts(v(x, 64 * h, 64 * h + 64), v(bank, 64 * h, 64 * h + 64), LIFT[t % 2], AL.add)
                        barred.discard("CB"[n])
                elif s == "C":
                    counted("PC", 0, 128)
                elif s == "L":
                    inv_lists()
                    barred.discard("C")
                elif s[0] == "+":
                    barred.difference_update(s[1:])
                elif s[0] == "-":
                    barred.update(s[1:])
                elif s == "Q":
                    quiet()
                elif s == "I":
                    dma("S", v("Wc", rows=(1, 128, 8)), v("IW", rows=(1, 128, 8)))
                elif s == "K":
                    mid_constants2()
                    dma("S", v("pb"), ext(T.pay[:]))
                    ops[-1]["after"] = [len(ops) - 2]
                elif s == "S0":
                    cp(v("muf", 0, 128), v("muu"))
                elif s == "S1":
                    cp(v("Ts", 128, 256), v("PF", 128, 256))
                elif s == "S2":
                    mu_slope()
                    turned(1, 384)
                    slopes("PF", part=0)
                elif s == "S3":
                    slopes("PF", part=1)
                elif s == "S4":
                    cp(v("ixu"), v("PS", 0, 128))
                elif s == "S5":
                    cp(v("du"), v("PD", 384, 512))

        plan = TRIALS[t > 0]
        if t > 0:
            blocks("Wc", v("S3", 0, 24), 3, "PF")
            ts(v("msu", 0, 32 * len(mine)), v("PD", 128, 128 + 32 * len(mine)), -0.375, AL.add)
            xd = XD[t > 1]
            if xd:
                xq("D", 128 - xd, 128)
            xq("A", 0, 128 - xd)
            trials(plan[0])
            records("tA", "PF", f1=lambda: (cp(v("Ts", 0, 128), v("PF", 0, 128)), trials(plan[1])),
                    f2=lambda: (turned(0, 256), trials(plan[2])), f7=lambda: trials(plan[3]), f3=lambda: trials(plan[4]),
                    f4=lambda: trials(plan[5]), f5=lambda: (lists2("l2u"), trials(plan[6])),
                    f6=lambda: (lists2("l2h"), trials(plan[7])))
        else:
            mm(v("PA", 0, 128), v("Ih"), v("oh"), True, False)
            mm(v("PA", 0, 128), v("gnh"), v("Rot"), False, True)
            mm(v("PD", 256, 384), v("Ih"), v("oh"), True, False)
            mm(v("PD", 256, 384), v("Rot"), v("gnh"), False, True)
            trials(plan[0])
            records("tA", "PA", f1=lambda: (lists2("l2u", "l2h"), trials(plan[1])), f2=lambda: trials(plan[2]),
                    f7=lambda: (mid_constants(), trials(plan[3])), f3=lambda: trials(plan[4]), f4=lambda: trials(plan[5]),
                    f5=lambda: (sum_constants(0), trials(plan[6])), f6=lambda: (sum_constants(1), trials(plan[7])))
        if not AH[t > 0]:
            scan(v("inv", 0, W), v("dec", 0, W), v("tA", 1, W + 1), bas[t % 2], AL.add, AL.max)
        trials(plan[8])
        red(v("mn", 0, 1), v("PB", 0, 4), AL.min)
        trials(plan[9])
        for k in range(4):
            ts(v("dg", 128 * k, 128 * k + 128), v("Ih"), v("PB", k, k + 1), AL.mult, v("mn", 0, 1), AL.is_equal)
        for k, l in enumerate([v("l0"), v("eh", 128 * t, 128 * t + 128), v("l2h"), v("l3h")]):
            mm(v("PA", 0, 128), v("dg", 128 * k, 128 * k + 128), l, k == 0, k == 3)
        trials(plan[10])
        cp(v("cu"), v("PA", 0, 128))
        trials(plan[11])
        for e, a, b in (("D", 0, WD), ("A", WD, 128)):
            gat(e, v("Wm", 16 * a, 16 * b), v("Wc"), v("cu", a, b))
        if not last:
            dma("S", dr("st", T.st[t], t), v("Wm", 0, W, rows=(0, 128, 8)))
        blocks("Wm", v("S3", 24, 32), 1)
        trials(plan[12])

        def carry(k1):
            k0 = carried[0]
            if t > 0 and k1 > k0:
                factors(k1)
                tt(v(vo, 16 * k0, 16 * k1), ind(vi, v("du", k0, k1)), v("R", 16 * k0, 16 * k1), AL.mult)
                carried[0] = k1
                for a, b in zip(VA, VA[1:]):
                    if last and k0 < b <= k1:
                        dma("G", v(vo, 16 * a, 16 * b), turned_back(t, 16 * a, 16 * b), acc=True)

        def back(n):
            mm(v(("PG", "PB")[n % 2]), v("Rk"), msq(n), True, True)

        def added(n):
            tt(v(vo, 512 * n, 512 * n + 512), v(("PG", "PB")[n % 2]), v(vo, 512 * n, 512 * n + 512), AL.add)

        def elected(q, k0=0, k1=32, e="A", hold=False):
            if k1 > k0:
                gat(e, v("Xp", 512 * q + 16 * k0, 512 * q + 16 * k1), v("X"), v("cu", 32 * q + k0, 32 * q + k1))
            if k1 == 32 and q != rank and e == "A":
                post(q, ("ah%d", "aq%d", "ar%d")[(near + far).index(q)] % (t + 1), v("Xp", 512 * q, 512 * q + 512),
                     lq(t + 1, rank, q), lq(t + 1, q, rank), hold)

        def neighbours():
            act(v("Wm", W, W + 1), v("Wm", W - 1, W), AF.Identity, bias=lo)
            dma("S", v("Wm", 0, W, rows=(2, 128, 8)), v("Wm", 1, W + 1, rows=(1, 128, 8)))
            if not last:
                send([([cores[prev]], e_prev, "an%d" % t, [dr("st", T.st[t], t)], [dr("ld", T.ld[t], t)], 0)])
                arrive(dr("ld", T.ld[t], t), "an%d" % t, n_next)
                dma("S", v("Wm", 0, W, rows=(3, 128, 8)), dr("ld", T.ld[t], t))

        def steps(names):
            for s in names.split():
                n = int(s[1:] or 0)
                if s[0] in "xh":
                    elected((far + near + [rank])[n], XB[last] if n == XQ else 0, hold=s[0] == "h")
                elif s[0] == "d":
                    elected(far[XQ], 0, XB[last], "D")
                elif s[0] == "n":
                    neighbours()
                elif s[0] == "r":
                    factors(n)
                    if t == 0 and n > made[0]:
                        act(v("p4", 16 * made[0], 16 * n), v("pb", 16 * made[0], 16 * n), AF.Identity, scale=0.25)
                        made[0] = n
                elif s[0] == "e":
                    if not last:
                        cp(v(("eu", "eh")[n], 128 * t + 128, 128 * t + 256), v("e32", 128 * t + 128, 128 * t + 256))
                elif s[0] == "S":
                    if t > 0:
                        trials(s)
                elif s[0] == "v":
                    carry(n)
                elif s[0] == "k":
                    fold("Xp", t + 1, n // 10, n % 10)
                elif s[0] == "b":
                    back(n)
                elif s[0] == "a":
                    added(n)
                else:
                    fold("Xp", t + 1, n)

        plan = PLAN[last]
        if last:
            ts(v("Rb"), v("Ib"), 2.0, AL.mult)
        steps(plan[0])
        if t == 0:
            records("tB", "PA", f1=mean_constants, f2=lambda: row_constants([(8, 1)]), f7=lambda: row_constants([(16, 4), (32, 1)]),
                    f3=lambda: row_constants([(40, 0), (48, 4)]), f4=slope_constants)
        else:
            records("tB", "PA", *[lambda k=k: steps(plan[k]) for k in (1, 2, 4, 5)], f7=lambda: steps(plan[3]))
        if t == 0:
            steps(" ".join(plan[1:6]))
        steps(plan[6])
        running("tB", lambda: steps(plan[7]))
        steps(plan[8])

        def li(h, s):
            c = 384 * t + 192 * h + 64 * s
            return v("li", c, c + 64)

        iv = [v("ivh", 128 * t + 64 * h, 128 * t + 64 * h + 64) for h in range(2)]
        for h in range(2):
            inv_half("ivh", 128 * t, h)
            send([([cores[q]], eng3[q], "ai%d" % (2 * t + h), [iv[h]], [li(h, slot(rank, q))], 0) for q in eng3])
            add("-", "arr", None, [], [li(h, s) for s in range(3)], tok=("ai%d" % (2 * t + h), n3))
            steps(plan[9 + h])
        if t == 0:
            late_constants()
        def mean(h):
            for k, x in enumerate([iv[h]] + [li(h, s) for s in range(3)]):
                mm(v("PC" if h else "PD", 0, 64), v("Iq"), x, k == 0, k == 3)

        for h in range(2):
            bank = v("PC" if h else "PD", 0, 64)
            mean(h)
            ts(v("muu", 64 * h, 64 * h + 64), bank, -0.375, AL.add)
            steps(plan[11 + 2 * h])
            if h and not last:
                n = min(64, 32 * len(mine))
                for u, q in enumerate(mine[::2]):
                    for k in range(4):
                        c0 = 128 * t + 32 * q if k == 0 else 384 * t + 192 * (q // 2) + 64 * (k - 1) + 32 * (q % 2)
                        mm(v("PD", 128 + 64 * u, 128 + 64 * u + n), v("Pq"), v("li" if k else "ivh", c0, c0 + n), k == 0, k == 3)
            for k, e in enumerate(WE[0 if t == 0 else 2 if last else 1][2 * h:2 * h + 2]):
                q = 2 * h + k
                gat(e, v("Wc", 512 * q, 512 * q + 512), v("Wm", 0, W), v("muu", 32 * q, 32 * q + 32))
            steps(plan[12 + 2 * h])

    order = far + near + [rank]
    cp(v("muf", 0, 128), v("muu"))
    blocks("Wc", v("S3", 32, 56), 3)
    mu_slope()
    steps(plan[15])
    slopes("PA", lambda: cp(v("Ts", 0, 256), v("PA", 0, 256)))
    steps(plan[16])
    turned(0, 256)
    turned(1, 384)
    cp(v("ixu"), v("PS", 0, 128))
    ts(v("du"), v("PD", 256, 384), -1.0, AL.add)
    cp(v("gpu"), v("PD", 384, 512))

    def part(name, q, h=None):
        return v(name, 512 * q, 512 * q + 512) if h is None else v(name, 512 * q + 256 * h, 512 * q + 256 * h + 256)

    def lst(name, q, h=None):
        return v(name, 32 * q, 32 * q + 32) if h is None else v(name, 32 * q + 16 * h, 32 * q + 16 * h + 16)

    piece = [(far[0], 0), (far[0], 1), (far[1], 0), (far[1], 1), (near[0], 0), (near[0], 1), (rank, None)]
    terms = []

    def term(m, x, stop=False):
        mm(v("PB"), v(m), x, not terms, stop)
        terms.append(x)

    for s in OUT.split():
        c, n = s[0], int(s[1])
        q, h = piece[n]
        if s[2:]:
            h = None
        if c == "R":
            gat("A", part("R", q, h), v("tab", 64, 96), lst("ixu", q, h))
        elif c == "V":
            tt(part("V0", q, h), ind(v("V1"), lst("du", q, h)), part("R", q, h), AL.mult)
        elif c == "T":
            tt(part("Tg", n // 2, h), ind(v("p4"), lst("gpu", q, h)), part("V0", q, h), AL.add)
        elif c == "P":
            gat("A", part("D1", q, h), v("p4"), lst("gpu", q, h))
            if q == rank:
                term("Ib", part("D1", rank))
            elif q in near:
                post(q, "ap", part("D1", q), part("D2", 0), part("D2", 0), True)
        elif c == "U":
            bank = part(("PS", "PT", "PG", "PA")[n], 0, h and 0)
            mm(bank, v("Ib"), part("D1", q, h), True, True)
            tt(part("Tg", n // 2, h), bank, part("V0", q, h), AL.add)
        elif c in "SH":
            post(q, "af%d" % n, part("V0", q, h) if q in near else part("Tg", n // 2, h), part("lf", slot(rank, q), h),
                 part("lf", slot(q, rank), h), c == "H")
        elif c in "XW":
            post(near[0], "af%d" % n, part("Tg", 1, h), part("lf", slot(far[0], near[0]), h), part("lf", slot(far[1], rank), h), c == "W")
        elif c == "J":
            tt(part("Tg", 0, h), part("Tg", 0, h), part("lf", slot(far[1], rank), h), AL.add)
        elif c == "M":
            gat("A", v("Mg"), v("Mp", 4 * W, 5 * W), lst("muu", rank), scale=1.0 / 64)
            term("Ib", v("Mg"))
        elif c == "N":
            term("Ib", part("D2", 0))
        elif c == "F":
            term("If", part("V0", rank) if q == rank else part("lf", slot(q, rank)))
        elif c == "E":
            term("Ib", part("D2", 0), True)
        elif c == "A":
            tt(v("PB"), v("PB"), part("V0", rank) if q == rank else part("lf", slot(q, rank)), AL.add)
        else:
            for h in range(2):
                tt(part("yo", 0, h), part("PB", 0, h), part("lf", slot(q, rank), h), AL.add)
                dma("A" if h else "S", ext(T.y[:, 256 * h:256 * h + 256]), part("yo", 0, h))
    emit(g, T, ops)
